import numpy as np, ml_dtypes
CORES = [3,11,19,27,35,43,51,59]
N = 8
BF = ml_dtypes.bfloat16
def gentries(a):
    return np.ascontiguousarray(a.reshape(8, 16, -1).transpose(0, 2, 1)).reshape(8, -1)
def gtable(e):
    e = np.asarray(e); return np.ascontiguousarray(e.reshape(8, -1, 16).transpose(0, 2, 1)).reshape(128, -1).astype(np.int32)
L, S, T, H, C, X, LG = 2304, 384, 3, 3, 96, 112, 12
W = 2 ** LG; EMPTY = 16 * W - 1; OLD = 8
def parts(rng):
    z = rng.random((N, 8, 3, L)); p = 1.3 * rng.random((N, 8, 3, T * S)) - 0.15; mix = 220 * (2 * rng.random((N, 8, 16, 3)) - 1)
    w = np.clip(np.rint(128 + np.matmul(mix, z - 0.5)) + rng.integers(-6, 7, (N, 8, 16, L)), 0, 255).astype(np.int64)
    x = np.clip(np.rint(128 + np.matmul(mix, p - 0.5)) + rng.integers(-6, 7, (N, 8, 16, T * S)), 0, 255).astype(np.int64)
    ed = np.zeros((N, 8, 16, L), np.int64)
    for j in range(3):
        o = np.argsort(13 * np.floor(13 * z[:, :, j]) + np.floor(13 * z[:, :, (j + 1) % 3]) + z[:, :, (j + 2) % 3], axis=-1); at = np.argsort(o, axis=-1)
        for i in range(4): ed[:, :, 4 * j + i] = np.take_along_axis(o, (at + (1 - 2 * (i % 2)) * rng.integers(1, 7, (N, 8, L))) % L, -1)
    ids = ed[:, :, rng.permutation(12)]
    ed[:, :, :12] = np.where(rng.random(ids.shape) < 0.15, EMPTY, W * rng.integers(0, OLD + 1, ids.shape) + ids)
    ed[:, :, 12:] = (np.arange(L) + rng.integers(1, L, (N, 8, 4, L))) % L
    c = rng.integers(0, L, (N, 8, T * S, 8)); far = np.zeros(c.shape)
    for j in range(3): far = far + np.abs(np.take_along_axis(z[:, :, j], c.reshape(N, 8, -1), -1).reshape(c.shape) - p[:, :, j, :, None])
    best = np.take_along_axis(c, np.argmin(far, axis=-1)[..., None], -1)[..., 0]
    ent = np.where(rng.random(best.shape) < 0.5, best, c[..., 0])
    return w, ed, x, ent, rng.integers(100, 700, (N, 8))
def take(a, i): return np.take_along_axis(a, i[:, :, None, :], 3)
def pack(w, ed, x, ent, th):
    return {"w": np.ascontiguousarray(w.reshape(N, 128, L)).astype(np.float32).astype(BF), "nb": np.ascontiguousarray(ed.reshape(N, 128, L)).astype(np.int32),
            "x": np.ascontiguousarray(x.reshape(N, 128, T * S)).astype(np.float32).astype(BF), "ent": np.stack([gtable(a) for a in ent]),
            "th": np.repeat(th.reshape(N, 8, 1), 16, axis=2).reshape(N, 128, 1).astype(np.int32)}
def setup_inputs(rng):
    w, ed, x, ent, th = parts(rng); i = np.where(rng.random(ent.shape) < 0.15, rng.integers(0, T * S, ent.shape), np.arange(T * S))
    return pack(w, ed, take(x, i), np.take_along_axis(ent, i, -1), th)
def setup_inputs_crowd(rng):
    w, ed, x, ent, th = parts(rng); ent[..., 0] = 0; ent[..., 1] = L - 1
    pool = rng.choice(np.array([2, 5, 12, 40, 100, S, T * S]), (N, 8, 1)); pool[0, :, 0] = (1, 2, 3, 12, 40, 100, S, T * S)
    i = np.floor(rng.random(ent.shape) * pool).astype(np.int64)
    return pack(w, ed, take(x, i), np.take_along_axis(ent, i, -1), np.maximum(th - 80, 20))
def setup_inputs_room(rng):
    w, ed, x, ent, th = parts(rng); th[:] = 1; odd = np.add.reduce(w, axis=2) & 1; w[:, :, 0] = w[:, :, 0] ^ odd
    f = (0, C - 1, C, C + 1, C + X - 1, C + X, C + X + 1, S)
    for q in range(N):
        for g in range(8):
            o = rng.permutation(L); a, b = o[:S], o[S:2 * S]; n = f[g] if q == 0 else f[int(rng.integers(0, 8))]
            if n == 0 or n == S: w[q, g][:, a[-1]] = w[q, g][:, a[0]]; b[-1] = b[0]
            w[q, g][:, b] = w[q, g][:, a]; ed[q, g, 0, a] = W * rng.integers(0, OLD + 1, S) + b
            v = w[q, g][:, a]; v[3] = np.where(rng.permutation(S) < n, v[3] ^ 1, v[3])
            x[q, g, :, :S] = v; ent[q, g, :S] = a
    return pack(w, ed, x, ent, th)
def setup_inputs_ties(rng):
    w, ed, x, ent, th = parts(rng); point = rng.integers(0, 256, (N, 8, 16, 12)); point[:, :, 0] = rng.integers(0, 100, (N, 8, 12))
    w = take(point, rng.integers(0, 12, (N, 8, L))); th = rng.integers(3, 60, (N, 8))
    x = take(w, ent); x[:, :, 0] = x[:, :, 0] + th[..., None] + rng.integers(-1, 2, ent.shape)
    ent = np.where(rng.random(ent.shape) < 0.3, rng.integers(0, L, ent.shape), ent)
    h = ed[:, :, :6]; ed[:, :, 6:12] = np.where(h == EMPTY, EMPTY, W * rng.integers(0, OLD + 1, h.shape) + (h & (W - 1)))
    h = ed[:, 1::2, :12]; ed[:, 1::2, :12] = np.where(h == EMPTY, EMPTY, 4 * W + (h & (W - 1)))
    return pack(w, ed, x, ent, th)
def setup_inputs_aged(rng):
    w, ed, x, ent, th = parts(rng); x = np.tile(x[..., :S], (1, 1, 1, T)); ent = np.tile(ent[..., :S], (1, 1, T))
    th = np.where(rng.random((N, 8)) < 0.5, 4096, th)
    for q in range(N):
        for g in range(8):
            e = ed[q, g, :12]; ids = np.where(e == EMPTY, ed[q, g, 12:13], e & (W - 1)); age = rng.integers(0, OLD + 1, e.shape); i = (g + q) % 8
            if i < 3: e = np.where(e == EMPTY, EMPTY, (OLD - i) * W + ids)
            elif i == 3: e = np.full(e.shape, EMPTY)
            elif i == 4: e = age * W + ed[q, g, 12:13]
            elif i == 5: e = np.where(np.arange(12)[:, None] % 2 == 0, OLD, 0) * W + ids
            elif i == 6: e = 3 * (q % 2) * W + ids
            else: e = age * W + ids
            ed[q, g, :12] = e
    c = [int(i) for i in 1 + rng.permutation(L - 1)[:5]]; cut = [0] + c[2:]
    u = w[:, 1]; u[:, :, c + [0]] = 100; u[:, 1, c[1]] = 101
    for j in range(4): u[:, 0, cut[j]] = 140; u[:, 2 + j, cut[j]] = 160
    e = ed[:, 1]; e[:, :12, c[0]] = EMPTY; e[:, 0, c[0]] = c[1]
    for j in range(4): e[:, 12 + j, c[0]] = cut[j]
    x[:, 1] = 100; x[:, 1, 0, :S] = 180; x[:, 1, 0, S:] = 140
    for t in range(1, T): x[:, 1, 1 + t, t * S:(t + 1) * S] = 122
    ent[:, 1] = c[0]; th[:, 1] = 40
    return pack(w, ed, x, ent, th)
def setup_inputs_spread(rng):
    w, ed, x, ent, th = parts(rng)
    w = np.minimum(np.exp2(8.1 * rng.random((N, 8, 1, L))) * rng.random((N, 8, 16, L)), 255).astype(np.int64)
    x = np.minimum(np.exp2(8.1 * rng.random((N, 8, 1, T * S))) * rng.random((N, 8, 16, T * S)), 255).astype(np.int64)
    th = np.exp2(12 * rng.random((N, 8))).astype(np.int64); th[0, 0] = 0; th[1, 1] = 4096
    h = ed[:, ::2, :12]; ed[:, ::2, :12] = np.where(h == EMPTY, EMPTY, (h >> LG) * W + (np.arange(L) + rng.integers(1, L, h.shape)) % L)
    ent = np.where(rng.random(ent.shape) < 0.1, rng.choice(np.array([0, L - 1]), ent.shape), ent)
    for q in range(N):
        for g in (2, 3, 6, 7):
            w[q, g] = rng.integers(0, 4, (16, L)); x[q, g] = rng.integers(252, 256, (16, T * S))
            gone = rng.random((12, L)) < rng.choice(np.array([0.3, 0.6, 0.9, 1.0]), (1, L)); ed[q, g, :12] = np.where(gone, EMPTY, ed[q, g, :12])
            a, b = [int(c) for c in rng.permutation(L)[:2]]; i = (q + g) % 5; ent[q, g, 0] = a
            if i < 3:
                w[q, g, :, a] = 3; th[q, g] = np.add.reduce(x[q, g, :, 0]) - 48 + i - 1
            else:
                w[q, g, :, a] = 0; w[q, g, :, b] = 0; x[q, g, :, 0] = 255
                ed[q, g, :12, a] = EMPTY; ed[q, g, 12:, a] = b; th[q, g] = 4080 + i - 3
            if g >= 6: w[q, g] = 255 - w[q, g]; x[q, g] = 255 - x[q, g]
    return pack(w, ed, x, ent, th)
def check_inputs(d):
    bad = []
    for k in ("w", "x"):
        a = np.asarray(d[k]).astype(np.float32)
        if not np.all((a >= 0) & (a <= 255) & (a == np.floor(a))): bad.append("whole numbers of " + k)
    e = np.asarray(d["nb"]).astype(np.int64).reshape(N, 8, 16, L); own = np.arange(L); h = e[:, :, :12]; s = e[:, :, 12:]; c = h & (W - 1)
    if not np.all((h == EMPTY) | ((h >= 0) & (h < (OLD + 1) * W) & (c < L) & (c != own))): bad.append("edges of nb")
    if not np.all((s >= 0) & (s < L) & (s != own)): bad.append("shortcuts of nb")
    if np.min(d["ent"]) < 0 or np.max(d["ent"]) > L - 1: bad.append("range of ent")
    t = np.asarray(d["th"]).astype(np.int64).reshape(N, 8, 16)
    if np.min(t) < 0 or np.max(t) > 4096: bad.append("range of th")
    if not np.all(t == t[:, :, :1]): bad.append("th alike in a group")
    return bad
def near(wu, ed, xb, cur):
    a = np.arange(N * 8)[:, None]; c = ed[a, cur] & (W - 1)
    d = np.add.reduce(np.abs(xb[:, :, None, :] - wu[a[:, :, None], c]), axis=3)
    d = np.where(c == W - 1, 2 ** 20, d); i = np.argmin(d, axis=2)[:, :, None]
    return np.take_along_axis(c, i, 2)[:, :, 0], np.take_along_axis(d, i, 2)[:, :, 0]
def slot(e, c):
    return np.argmax(np.where((e[:, :12] & (W - 1)) == c[:, None], 16, e[:, :12] >> LG), axis=1)
def reference(w, nb, x, ent, th):
    M = N * 8; a = np.arange(M)[:, None]
    wu = np.zeros((M, W, 16), np.int32); wu[:, :L] = w.astype(np.float32).reshape(M, 16, L).transpose(0, 2, 1)
    ed = np.full((M, W, 16), EMPTY, np.int64); ed[:, :L] = nb.reshape(M, 16, L).transpose(0, 2, 1)
    xs = np.array(x.astype(np.float32).reshape(M, 16, T * S).transpose(0, 2, 1), dtype=np.int32, order="C")
    en = np.stack([gentries(b) for b in ent]).reshape(M, T * S).astype(np.int64)
    tv = th.astype(np.int64).reshape(M, 16)[:, :1]
    for t in range(T):
        xb = xs[:, t * S:(t + 1) * S]; eb = en[:, t * S:(t + 1) * S]; u = eb
        du = np.add.reduce(np.abs(xb - wu[a, u]), axis=2)
        for h in range(H):
            c, d = near(wu, ed, xb, u); go = d < du
            u = np.where(go, c, u); du = np.where(go, d, du)
        v, dv = near(wu, ed, xb, u)
        s = np.broadcast_to(np.arange(S), (M, S)); first = np.full((M, W), S)
        np.minimum.at(first, (a, u), s); np.minimum.at(first, (a, v), s)
        counts = (first[a, u] >= s) & (first[a, v] >= s)
        far = du >= tv; want = (counts & far).astype(np.int64); k = np.add.accumulate(want, axis=1) - want
        split = (want == 1) & (k < C); rest = far & ~split
        m, j = np.nonzero(counts); i = np.arange(len(m)); uu = u[m, j]; vv = v[m, j]; sp = split[m, j]; nn = L + C * t + k[m, j]
        xx = xb[m, j]; w0 = wu[m, uu]; w1 = wu[m, vv]; e0 = ed[m, uu]; e1 = ed[m, vv]; i0 = slot(e0, vv); i1 = slot(e1, uu)
        e0[:, :12] = np.where(e0[:, :12] + W >= (OLD + 1) * W, EMPTY, e0[:, :12] + W)
        e0[i, i0] = np.where(sp, nn, vv); e1[i, i1] = np.where(sp, nn, uu)
        e2 = np.full(e0.shape, EMPTY); e2[:, 0] = uu; e2[:, 1] = vv; e2[:, 12:] = e0[:, 12:]
        ed[m, uu] = e0; ed[m, vv] = e1; ed[m[sp], nn[sp]] = e2[sp]
        wu[m, uu] = w0 + ((xx - w0) >> 2); wu[m, vv] = w1 + ((xx - w1) >> 3); wu[m[sp], nn[sp]] = ((w0 + xx) >> 1)[sp]
        if t + 1 < T:
            place = np.argsort(~rest, axis=1, kind="stable")[:, :X]; num = np.add.reduce(rest.astype(np.int64), axis=1)
            kk = np.arange(X)[None, :]; q = (np.arange(N)[:, None] - 1 - kk % (N - 1)) % N
            mm = (q[:, None, :] * 8 + np.arange(8)[None, :, None]).reshape(M, X); pl = place[mm, kk]; got = num[mm] > kk
            lo, hi = (t + 2) * S - X, (t + 2) * S
            xs[:, lo:hi] = np.where(got[:, :, None], xb[mm, pl], xs[:, lo:hi]); en[:, lo:hi] = np.where(got, eb[mm, pl], en[:, lo:hi])
    P = L + T * C
    yw = np.ascontiguousarray(wu[:, :P].transpose(0, 2, 1)).reshape(N, 128, P).astype(np.float32).astype(BF)
    yn = np.ascontiguousarray(ed[:, :P].transpose(0, 2, 1)).reshape(N, 128, P).astype(np.float32)
    return {"yw": yw, "yn": yn}

@@ -1,0 +1,673 @@
+import math
+from concourse.bass import DstId, RemoteDMATransfer
+from concourse.mybir import AluOpType as A, ActivationFunctionType as F
+
+L, S, NT, CN, XN, N = 2304, 384, 3, 96, 112, 8
+PU = L + NT * CN
+GW = 2608
+TW = GW + 2 * S
+HB = 162
+LN2 = math.log(2.0)
+RND = 12582912.0
+bf, f32, i32, u16, f16 = "bfloat16", "float32", "int32", "uint16", "float16"
+SCRATCH = {}
+for _d, _s in (
+        (bf, "W:3376 OH:2608 ONE:2608 X:1200 BH:384 G:6144 M:6144 G0:384 M0:384 BH0:384 BB:7776 OT:768 AW:768 TS:672 RR:1024 SMB:64 "
+             "WB:800 AGB:768 WT:768 MT:768 SG:768 RB:384 WI:768 WS:96 XS:96 IB:128 NI:256 RC:80 TRI:128 ON:128 ZR:128 ZM:256 SI:640 "
+             "SJ:512 I162:162"),
+        (f32, "NF:3376 IOT:2608 THB:128 TH8:8 SC:768 ID0:384 THK:24 HF:48 SMA:320 PK:24 LF:96 LSA:192 CP:864 EB:800 UV:800 MS:768 "
+              "DA:768 TR:384 Q:768 NW:768 TA:128 NU:384 XE:800 SND:448 LND:448 OWN:448 CI:256 CM:128 CD:128 PC:32 RA:16 R32:8 SMM:128 "
+              "SGM:128 IF:128 NF32:128 D0:256 MK:128 MK24:192 THR:64 DUM:48 DS:24 CT:64"),
+        (i32, "NB:3376 EN:72 THI:8 I32:384 KM:48 CUR:48 FH:96 FU:96 HT:96 LI:48 MX:224 MY:224 PI:8 CTI:16"),
+        (u16, "LE:72 O16:384 LH:48 LUV:48 LT:48 LD:48 LTG:48 LP:24 LSN:16 LSP:16 XL:32 PL:16"),
+        (f16, "A16:384 EX:384 EXP:192 C16:208 E16:112 I16:128 LG:1024 DG:2048")):
+    for _x in _s.split():
+        SCRATCH[_x.split(":")[0]] = ("sbuf", [128, int(_x.split(":")[1])], _d)
+for _k in range(8):
+    SCRATCH["P%d" % _k] = ("psum", [128, 512], f32)
+SEMAPHORES = ["sv", "sa", "sp", "st", "arr0", "arr1", "loc0", "loc1"] + ["d%d" % _k for _k in range(20)]
+
+GAM, SIG, CY, PECY = 1.56, 3.8, 1.0, 0.55
+NE = 2
+STAG = [0.0, -4000.0, -8000.0]
+BINIT, LOOK, ROUNDS, TRIES = 5000.0, 60.0, 5, 24
+CACHE = {}
+ID = F.Identity
+
+
+def build(T, topo, rank, core):
+    ops = []
+    bias = [0.0]
+    last_w, readers, bank = {}, {}, {}
+    P = [T["P%d" % k] for k in range(8)]
+
+    def op(eng, fn, r, w, cost, pb=(), kind="c", after=()):
+        n = len(ops)
+        deps = {}
+        for x in r:
+            if x in last_w:
+                deps[last_w[x]] = True
+        for x in w:
+            if x in last_w:
+                deps.setdefault(last_w[x], False)
+            for y in readers.get(x, ()):
+                deps.setdefault(y, False)
+        for b in pb:
+            st = bank.setdefault(b, [None, [], []])
+            if st[0] != eng:
+                st[0], st[2], st[1] = eng, st[1], []
+            for y in st[2]:
+                deps.setdefault(y, False)
+            if eng == "t" and st[1]:
+                deps.setdefault(st[1][-1], False)
+            st[1].append(n)
+        for y in after:
+            deps.setdefault(y, False)
+        for x in r:
+            readers.setdefault(x, []).append(n)
+        for x in w:
+            last_w[x] = n
+            readers[x] = []
+        deps.pop(n, None)
+        ops.append({"w": w, "b": bias[0], "e": eng, "f": fn, "d": deps, "c": cost, "k": kind})
+        return n
+
+    def vc(n, c=1.0):
+        return 20 + max(64, n * c) * CY
+
+    def ts(o, i, s1, s2, o0, o1, r, w, n, c=1.0, pb=(), ga=False):
+        cost = 60 + n * GAM * CY if ga else vc(n, c)
+        if o1 is None:
+            return op("v", lambda q: q.tensor_scalar(o, i, s1, None, o0), r, w, cost, pb)
+        return op("v", lambda q: q.tensor_scalar(o, i, s1, s2, o0, o1), r, w, cost, pb)
+
+    def tt(o, a, b, o0, r, w, n, pb=(), ga=False):
+        cost = 60 + n * GAM * CY if ga else vc(n, 1.0 if pb else 2.0)
+        return op("v", lambda q: q.tensor_tensor(o, a, b, o0), r, w, cost, pb)
+
+    def cp(o, i, r, w, n, c=1.0, pb=(), ga=False, sc=False):
+        cost = 60 + n * (SIG if sc else GAM) * CY if (ga or sc) else vc(n, c)
+        return op("v", lambda q: q.tensor_copy(o, i), r, w, cost, pb)
+
+    def ms(o, v, w, n, c=1.0):
+        return op("v", lambda q: q.memset(o, v), [], w, vc(n, c))
+
+    def act(o, i, fn, r, w, n, bias=0.0, scale=1.0, pb=(), ga=False):
+        cost = 80 + n * (GAM if ga else 1.0) * CY
+        return op("a", lambda q: q.activation(o, i, fn, bias=bias, scale=scale), r, w, cost, pb)
+
+    def mm(o, l, rr, st, sp, r, w, m, n, pb, x=1):
+        return op("t", lambda q: q.matmul(o, l, rr, st, sp), r, w, 8 + x * max(min(64, m), n) * PECY, [pb])
+
+    def iota(o, pat, base, cm, w, n, fl=True):
+        if fl:
+            return op("g", lambda q: q.iota(o, pat, base, cm, allow_small_or_imprecise_dtypes=True), [], w, 130 + 2 * n * CY)
+        return op("g", lambda q: q.iota(o, pat, base, cm), [], w, 130 + 2 * n * CY)
+
+    def dma(eng, o, i, r, w, nbytes):
+        return op(eng, lambda q: q.dma_start(o, i), r, w, 2000 + nbytes / 190.0, kind="d")
+
+    dma("s", T.EN[:], T.ent[:], [], ["EN"], 36864)
+    dma("s", T.NB[:, 0:L], T.nb[:], [], ["NBa"], 128 * L * 4)
+    dma("a", T.W[:, 0:L], T.w[:], [], ["Wa"], 128 * L * 6)
+    dma("a", T.X[:, 0:S], T.x[:, 0:S], [], ["X00", "X01", "X02"], 128 * L * 2)
+    dma("s", T.THI[:, 0:1], T.th[:], [], ["THI"], 128 * L * 3)
+    for t in (1, 2):
+        dma("s", T.X[:, 400 * t:400 * t + S], T.x[:, S * t:S * t + S], ["Wa"], ["X%d0" % t, "X%d1" % t, "X%d2" % t], 128 * S * 2)
+    ms(T.NB[:, L:TW], 65535, ["NBb"], TW - L)
+    ms(T.W[:, L:PU], 0.0, ["Wb"], 288, .5)
+    ms(T.W[:, PU:TW], 8192.0, ["Wc"], TW - PU, .5)
+    ms(T.NF[:, GW:TW], 0.0, ["NF4"], 768)
+    for t in range(NT):
+        ms(T.X[:, 400 * t + S:400 * t + 400], 0.0, ["Xd%d" % t], 16)
+    NBR, WR = ["NBa", "NBb"], ["Wa", "Wb", "Wc"]
+    cp(T.LE[:], T.EN[:], ["EN"], ["LE%d%d" % (t, c) for t in range(NT) for c in range(3)], 72)
+
+    PC, CP_ = T.PC, ["CI", "PC"]
+    iota(T.CI[:], [[1, 256]], 0, 0, ["CI"], 256)
+    iota(T.PI[:, 0:1], [[0, 1]], 0, 1, ["PI0"], 1, False)
+    iota(T.CM[:], [[0, 8], [1, 16]], 0, 0, ["CM"], 128)
+    iota(T.CD[:], [[1, 8], [0, 16]], 0, 0, ["CD"], 128)
+    iota(T.IOT[:], [[1, GW]], 0, 0, ["IOT"], GW)
+    ms(T.ONE[0:32, :], 1.0, ["ONE"], GW, .5)
+    op("g", lambda q: q.affine_select(T.OH[0:16, :], T.ONE[0:16, :], [[0, GW // 16], [-1, 16]], A.is_equal, 0.0, 0, 1),
+       ["ONE"], ["OH0"], 170 + 2 * GW * CY)
+    for k in range(1, 8):
+        dma("s", T.OH[16 * k:16 * k + 16, :], T.OH[0:16, :], ["OH0"], ["OH%d" % k], 90000)
+    OHR = ["OH%d" % k for k in range(8)]
+    ts(T.PI[:, 1:2], T.PI[:, 0:1], 15, None, A.bitwise_and, None, ["PI0"], ["PI1"], 1)
+    ts(T.PI[:, 2:3], T.PI[:, 0:1], 4, None, A.arith_shift_right, None, ["PI0"], ["PI2"], 1)
+    ts(T.PI[:, 3:4], T.PI[:, 0:1], 4, 1, A.arith_shift_right, A.bitwise_and, ["PI0"], ["PI3"], 1)
+    ts(T.PI[:, 4:5], T.PI[:, 0:1], 3, 1, A.arith_shift_right, A.bitwise_and, ["PI0"], ["PI4"], 1)
+    cp(PC[:, 0:5], T.PI[:, 0:5], ["PI0", "PI1", "PI2", "PI3", "PI4"], ["PC"], 5)
+    cP, cA, cG, cO, cH = [PC[:, k:k + 1] for k in range(5)]
+    ts(T.SMM[:], T.CM[:], cA, None, A.is_equal, None, ["CM", "PC"], ["SMM"], 128)
+    ts(T.SGM[:], T.CD[:], cG, None, A.is_equal, None, ["CD", "PC"], ["SGM"], 128)
+    for o, v, nm in ((T.IB[:], 1.0, "IB"), (T.I16[:], 1.0, "I16"), (T.NI[:, 0:128], -1.0, "NI0"), (T.NI[:, 128:256], -1.0 / 64, "NI1"),
+                     (T.SI[:, 0:128], .75, "SI0"), (T.SI[:, 128:256], .25, "SI1"), (T.SI[:, 256:384], .875, "SI2"),
+                     (T.SI[:, 384:512], .125, "SI3"), (T.SI[:, 512:640], -65536.0, "SI4"), (T.IF[:], 1.0, "IF"), (T.NF32[:], -1.0, "NF32"),
+                     (T.SJ[:, 0:128], 4096.0, "SJ0"), (T.SJ[:, 128:256], 65536.0, "SJ1"), (T.SJ[:, 256:384], -.375, "SJ2"),
+                     (T.SJ[:, 384:512], -.4375, "SJ3")):
+        ts(o, T.CI[:, 0:128], cP, v, A.is_equal, A.mult, CP_, [nm], 128)
+    for o, v in ((0, 4096.0), (8, 4096.0), (16, -8192.0), (24, -8192.0), (32, 1.0), (64, -4096.0), (72, -4096.0)):
+        ts(T.RC[:, o:o + 8], T.CI[:, 0:8], cG, v, A.is_equal, A.mult, CP_, ["RC%d" % o], 8)
+    ts(T.R32[:], T.CI[:, 0:8], cG, 256.0, A.is_equal, A.mult, CP_, ["R32"], 8)
+    ms(T.RA[:, 8:16], 0.0, ["RA1"], 8)
+    ts(T.RA[:, 0:8], T.CI[:, 0:128:16], cP, None, A.is_equal, None, CP_, ["RA0"], 8)
+    ts(T.RC[:, 48:56], T.CI[:, 0:128:16], cP, -1.0, A.is_equal, A.mult, CP_, ["RC48"], 8)
+    ts(T.RC[:, 56:64], T.CI[:, 0:128:16], cP, -1.0 / 64, A.is_equal, A.mult, CP_, ["RC56"], 8)
+    ms(T.D0[:], -128.0, ["D0"], 256)
+    ms(T.D0[:, 0:256:16], 1.0e9, ["D0"], 16)
+    for k in range(8):
+        ts(T.LG[:, 128 * k:128 * k + 128], T.CI[:, 0:128], -16.0 * k, cA, A.add, A.is_equal, CP_, ["LG%d" % k], 128)
+    for k in range(16):
+        ts(T.DG[:, 128 * k:128 * k + 128], T.I16[:], T.SMM[:, k:k + 1], None, A.mult, None, ["I16", "SMM"], ["DG%d" % k], 128, .5)
+    iota(T.MK24[:], [[0, 24], [1, 8]], 0, 0, ["MK24"], 192)
+    ts(T.MK[:, 0:64], T.MK24[:, 0:64], cG, None, A.is_equal, None, ["MK24", "PC"], ["MK0"], 64)
+    ts(T.MK[:, 64:128], T.MK24[:, 0:64], cG, -64.0, A.is_equal, A.mult, ["MK24", "PC"], ["MK1"], 64)
+    ts(T.MK24[:], T.MK24[:], cG, None, A.is_equal, None, ["MK24", "PC"], ["MK24"], 192)
+    ts(T.CT[:, 0:12], T.CI[:, 0:24:2], cH, None, A.add, None, CP_, ["CT0"], 12)
+    cp(T.XL[:, 0:12], T.CT[:, 0:12], ["CT0"], ["XLa"], 12)
+    ts(T.XL[:, 12:20], T.CT[:, 0:8], 2.0, None, A.mult, None, ["CT0"], ["XLb"], 8)
+    ts(T.XL[:, 20:28], T.CT[:, 0:8], 2.0, 1.0, A.mult, A.add, ["CT0"], ["XLc"], 8)
+    ts(T.TRI[:], T.CI[:, 0:128], cP, None, A.is_gt, None, CP_, ["TRI"], 128)
+    ms(T.ON[:], 1.0, ["ON"], 128)
+    ms(T.ZR[:], 0.0, ["ZR"], 128)
+    cp(T.I162[:], T.CI[:, 0:HB], ["CI"], ["I162"], HB)
+    ts(PC[:, 5:6], cA, 12.0, 4096.0, A.is_lt, A.mult, ["PC"], ["PC5"], 1)
+    ts(PC[:, 14:15], PC[:, 5:6], -1.0, 65535.0, A.mult, A.add, ["PC5"], ["PC14"], 1)
+    ts(PC[:, 6:7], cA, 12.0, None, A.is_ge, None, ["PC"], ["PC6"], 1)
+    ts(PC[:, 17:18], cA, 2.0, 65535.0 / 4096, A.is_ge, A.mult, ["PC"], ["PC17"], 1)
+    tt(PC[:, 7:8], PC[:, 17:18], PC[:, 5:6], A.mult, ["PC17", "PC5"], ["PC7"], 1)
+    ts(PC[:, 8:9], cA, 0.0, None, A.is_equal, None, ["PC"], ["PC8"], 1)
+    ts(PC[:, 9:10], cA, 1.0, None, A.is_equal, None, ["PC"], ["PC9"], 1)
+    ts(PC[:, 18:19], cA, -LN2, LN2 * (11 - 108 - 1548), A.mult, A.add, ["PC"], ["PC18"], 1)
+    ts(PC[:, 10:11], PC[:, 6:7], -400.0, PC[:, 18:19], A.mult, A.add, ["PC6", "PC18"], ["PC10"], 1)
+    ts(PC[:, 19:20], cA, -LN2, LN2 * 107, A.mult, A.add, ["PC"], ["PC19"], 1)
+    ts(PC[:, 20:21], PC[:, 6:7], -400.0, PC[:, 19:20], A.mult, A.add, ["PC6", "PC19"], ["PC20"], 1)
+    lr = math.log(1.9)
+    for c in range(3):
+        ts(PC[:, 21 + c:22 + c], cP, -lr, 118 * LN2 - lr * 128 * (c % 2), A.mult, A.add, ["PC"], ["PC%d" % (21 + c)], 1)
+    act(PC[:, 24:28], PC[:, 20:24], F.Exp, ["PC20", "PC21", "PC22", "PC23"], ["PCe"], 1300)
+    cZ, cW = PC[:, 24:25], [PC[:, 25 + c:26 + c] for c in range(3)]
+    ts(PC[:, 12:13], cO, float(HB), None, A.mult, None, ["PC"], ["PC12"], 1)
+    ts(T.CM[:], T.IB[:], 2.0, None, A.mult, None, ["IB", "CM"], ["CM"], 128)
+    tt(T.ZM[:, 0:128], T.CM[:], T.SGM[:], A.subtract, ["CM", "SGM"], ["ZM0"], 128)
+    ts(T.ZM[:, 128:256], T.ZM[:, 0:128], cZ, None, A.mult, None, ["ZM0", "PCe"], ["ZM1"], 128)
+    ms(T.THR[:, 48:64], 0.0, ["THRx"], 16)
+    for c in range(3):
+        ts(T.THR[:, c:48:3], T.ON[:, 0:16], cW[c], 2.5, A.mult, A.mult, ["ON", "PCe"], ["THR%d" % c], 16)
+        ts(T.DS[:, c:24:3], T.ON[:, 0:8], cP, 480.0 + 128 * c, A.mult, A.add, ["ON", "PC"], ["DS%d" % c], 8)
+    ts(T.CT[:, 16:64], T.CI[:, 0:48], 16.0, float(GW), A.mult, A.add, ["CI"], ["CT1"], 48)
+    ts(T.DUM[:], T.CT[:, 16:64], cA, None, A.add, None, ["CT1", "PC"], ["DUM"], 48)
+    ts(T.CT[:, 0:7], T.CI[:, 0:112:16], cA, None, A.add, None, ["CI", "PC", "CT0"], ["CT0"], 7)
+    ts(T.CTI[:, 0:7], T.CT[:, 0:7], 1.0 / 7, -3.0 / 7, A.mult, A.add, ["CT0"], ["CTI"], 7)
+    ts(T.CT[:, 8:15], T.CTI[:, 0:7], -223.0 / 32, None, A.mult, None, ["CTI", "CT0"], ["CT2"], 7)
+    tt(T.CT[:, 8:15], T.CT[:, 8:15], T.CT[:, 0:7], A.add, ["CT2", "CT0"], ["CT2"], 7)
+    ts(T.PL[:, 0:7], T.CT[:, 8:15], 32.0, None, A.mult, None, ["CT2"], ["PLa"], 7)
+    ts(T.PL[:, 7:14], T.CT[:, 8:15], 32.0, 16.0, A.mult, A.add, ["CT2"], ["PLb"], 7)
+    ms(T.CP[:, 208:864], 0.0, ["CPb"], 656)
+    ms(T.TS[:, 324:336], 0.0, ["TSd"], 8)
+    for b, nm, v in ((T.EB, "EB", 65535.0), (T.UV, "UV", 65535.0), (T.WB, "WB", 0.0), (T.XE, "XE", 0.0)):
+        ms(b[:, S:400], v, [nm + "d"], 16)
+        if nm in ("UV", "XE"):
+            ms(b[:, 400 + S:800], v, [nm + "e"], 16)
+    cp(PC[:, 28:29], T.THI[:, 0:1], ["THI"], ["PC28"], 1)
+    ts(T.THB[:], T.ON[:], PC[:, 28:29], -3.0, A.mult, A.add, ["ON", "PC28"], ["THB"], 128)
+    mm(P[4][:, 0:8], T.THB[:], T.R32[:], True, True, ["THB", "R32"], ["dl4"], 128, 8, 4, 4)
+    cp(T.TH8[:], P[4][:, 0:8], ["dl4"], ["TH8"], 8, pb=[4])
+    for t in (1, 2):
+        o = 224 * (t - 1)
+        act(T.OWN[:, o:o + XN], T.X[:, 400 * t + 272:400 * t + S], ID, ["X%d2" % t], ["OWx%d" % t], XN)
+        act(T.TA[:], T.IOT[:].indirect(T.LE[:, 24 * t + 16:24 * t + 24]), ID, ["IOT", "LE%d2" % t], ["TA0"], 128, ga=True)
+        act(T.OWN[:, o + XN:o + 224], T.TA[:, 16:128], ID, ["TA0"], ["OWe%d" % t], XN)
+
+    send = [None, None]
+    for t in range(NT):
+        last = t == NT - 1
+        n0 = L + CN * t
+        xo = 400 * t
+        if t > 0:
+            o = 224 * (t - 1)
+            op("x", None, [], ["LND%d" % t], 6000, kind="x%d" % (t - 1), after=[send[t - 1]])
+            tt(T.MX[:], T.LND[:, o:o + 224].indirect(T.PL[:, 0:14]), T.OWN[:, o:o + 224], A.max,
+               ["LND%d" % t, "PLa", "PLb", "OWx%d" % t, "OWe%d" % t], ["MX"], 224, ga=True)
+            ts(T.MY[:], T.MX[:], 4095, None, A.bitwise_and, None, ["MX"], ["MY"], 224)
+            cp(T.X[:, xo + 272:xo + S], T.MY[:, 0:XN], ["MY"], ["X%d2" % t], XN)
+            ts(T.E16[:], T.MY[:, XN:224], -1312.0, None, A.add, None, ["MY"], ["E16"], XN)
+            for a in range(16):
+                mm(P[3][:, 288:295], T.DG[:, 128 * a:128 * a + 128], T.E16[:, a:XN:16], a == 0, a == 15, ["DG%d" % a, "E16"], ["k2e"], 128, 7, 3)
+            ts(T.LE[:, 24 * t + 17:24 * t + 24], P[3][:, 288:295], 1312.0, None, A.add, None, ["k2e"], ["LE%d2" % t], 7, pb=[3])
+        if last:
+            for k in range(4):
+                cp(T.NF[:, 652 * k:652 * k + 652], T.NB[:, 652 * k:652 * k + 652], NBR, ["NF%d" % k], 652)
+        xb = [0, 0, 7]
+        xp = [P[0][:, 0:128], P[0][:, 128:256], P[7][:, 0:128]]
+        for c in range(3):
+            C = str(c)
+            cs = slice(128 * c, 128 * c + 128)
+            K, kb = P[1 + c], 1 + c
+            xc, xn = T.X[:, xo + 128 * c:xo + 128 * c + 128], "X%d%d" % (t, c)
+            le, ln = T.LE[:, 24 * t + 8 * c:24 * t + 8 * c + 8], "LE%d%d" % (t, c)
+            bias[0] = BINIT
+            if c == 0:
+                mm(P[0][:, 0:256], T.IB[:], T.X[:, xo:xo + 256], True, True, ["IB", xn, "X%d1" % t], ["xp0", "xp1"], 128, 256, 0)
+            if c == 2:
+                mm(xp[c], T.IB[:], xc, True, True, ["IB", xn], ["xp2"], 128, 128, xb[c])
+            act(T.ID0[:, cs], T.IOT[:].indirect(le), ID, ["IOT", ln], ["ID0" + C], 128, bias=-1312.0, ga=True)
+            act(T.BH0[:, cs], T.ID0[:, cs], ID, ["ID0" + C], ["BH0" + C], 128, bias=8256.0 + 1312.0)
+            act(T.G0[:, cs], T.W[:, 0:GW].indirect(le), ID, WR + [ln], ["G0" + C], 128, ga=True)
+            tt(T.M0[:, cs], T.G0[:, cs], xp[c], A.min, ["G0" + C, "xp" + C], ["M0" + C], 128, pb=[xb[c]])
+            mm(K[:, 280:288], xc, T.RC[:, 0:8], True, True, [xn, "RC0"], ["ks" + C], 128, 8, kb)
+            mm(K[:, 264:280], T.BH0[:, cs], T.RC[:, 48:64], True, False, ["BH0" + C, "RC48", "RC56"], ["ki" + C], 128, 16, kb)
+            mm(K[:, 264:280], T.ID0[:, cs], T.RA[:], False, False, ["ID0" + C, "RA0", "RA1"], ["ki" + C], 128, 16, kb, 4)
+            mm(K[:, 264:280], T.G0[:, cs], T.RC[:, 0:16], False, False, ["G0" + C, "RC0", "RC8"], ["ki" + C], 128, 16, kb)
+            mm(K[:, 264:280], T.M0[:, cs], T.RC[:, 16:32], False, True, ["M0" + C, "RC16", "RC24"], ["ki" + C], 128, 16, kb)
+            k16 = slice(16 * c, 16 * c + 16)
+            cp(T.KM[:, k16], K[:, 264:280], ["ki" + C], ["KM" + C], 16, pb=[kb])
+            tt(T.THK[:, 8 * c:8 * c + 8], T.TH8[:], K[:, 280:288], A.subtract, ["TH8", "ks" + C], ["THK" + C], 8, pb=[kb])
+            ts(T.CUR[:, k16], T.KM[:, k16], -3969, None, A.bitwise_and, None, ["KM" + C], ["CUR" + C], 16)
+            bias[0] = 0.0
+            if not last:
+                act(T.XE[:, cs], xc, ID, [xn], ["XEx" + C], 128, bias=4096.0)
+                act(T.XE[:, 400 + 128 * c:528 + 128 * c], T.ID0[:, cs], ID, ["ID0" + C], ["XEe" + C], 128, bias=4096.0 + 1312.0)
+        for h in range(4):
+            for c in range(3):
+                bias[0] = STAG[c]
+                cs = slice(128 * c, 128 * c + 128)
+                k16 = slice(16 * c, 16 * c + 16)
+                K, kb = P[1 + c], 1 + c
+                C = str(c)
+                xc, xn = T.X[:, xo + 128 * c:xo + 128 * c + 128], "X%d%d" % (t, c)
+                if h == 0:
+                    li, ln = T.LE[:, 24 * t + 8 * c:24 * t + 8 * c + 8], "LE%d%d" % (t, c)
+                elif h < 3:
+                    li, ln = T.LH[:, 24 * (h - 1) + 8 * c:24 * (h - 1) + 8 * c + 8], "LH%d%d" % (h, c)
+                else:
+                    li, ln = T.LUV[:, 8 * c:8 * c + 8], "LU0" + C
+                if h < 2:
+                    lo, lon = T.LH[:, 24 * h + 8 * c:24 * h + 8 * c + 8], "LH%d%d" % (h + 1, c)
+                else:
+                    lo, lon = T.LUV[:, 24 * (h - 2) + 8 * c:24 * (h - 2) + 8 * c + 8], "LU%d%d" % (h - 2, c)
+                ts(T.I32[:, cs], T.NB[:, 0:GW].indirect(li), 4095, None, A.bitwise_and, None, NBR + [ln], ["I32" + C], 128, ga=True)
+                ts(T.O16[:, cs], T.I32[:, cs], float(PU), None, A.min, None, ["I32" + C], ["O16" + C], 128)
+                go = 2048 * c
+                act(T.G[:, go:go + 2048], T.W[:, 0:GW].indirect(T.O16[:, cs]), ID, WR + ["O16" + C], ["G" + C], 2048, ga=True)
+                ts(T.BH[:, cs], T.O16[:, cs], 8256.0, None, A.add, None, ["O16" + C], ["BH" + C], 128, .5)
+                ts(T.A16[:, cs], T.O16[:, cs], -1312.0, None, A.add, None, ["O16" + C], ["A16" + C], 128, .5)
+                mm(K[:, 0:256], T.BH[:, cs], T.NI[:], True, False, ["BH" + C, "NI0", "NI1"], ["k" + C], 128, 256, kb)
+                mm(K[:, 0:128], T.A16[:, cs], T.I16[:], False, False, ["A16" + C, "I16"], ["k" + C], 128, 128, kb)
+                nv, db = 16 - NE, 4 + (3 * h + c) % 2
+                for i in range(nv, 16):
+                    o = P[db][:, 128 * (i - nv):128 * (i - nv) + 128]
+                    mm(o, T.IB[:], T.G[:, go + i:go + 2048:16], True, False, ["IB", "G" + C], ["dl%d" % db], 128, 128, db)
+                    mm(o, T.NI[:, 0:128], xc, False, True, ["NI0", xn], ["dl%d" % db], 128, 128, db)
+                    mm(K[:, i:256:16], xc, T.RC[:, 64:80], False, False, [xn, "RC64", "RC72"], ["k" + C], 128, 16, kb)
+                act(T.M[:, go + 128 * nv:go + 2048], P[db][:, 0:128 * NE], F.Abs, ["dl%d" % db], ["M%d_%d" % (c, i) for i in range(nv, 16)], 128 * NE, pb=[db])
+                for i in range(nv):
+                    tt(T.M[:, go + 128 * i:go + 128 * i + 128], T.G[:, go + i:go + 2048:16], xp[c], A.min,
+                       ["G" + C, "xp" + C], ["M%d_%d" % (c, i)], 128, pb=[xb[c]])
+                for i in range(nv):
+                    mm(K[:, i:256:16], T.G[:, go + i:go + 2048:16], T.RC[:, 0:16], False, False, ["G" + C, "RC0", "RC8"], ["k" + C], 128, 16, kb)
+                for i in range(16):
+                    mm(K[:, i:256:16], T.M[:, go + 128 * i:go + 128 * i + 128], T.RC[:, 16:32] if i < nv else T.RC[:, 0:16], False, i == 15,
+                       ["M%d_%d" % (c, i), "RC0", "RC8", "RC16", "RC24"], ["k" + C], 128, 16, kb)
+                sc = T.SC[:, 256 * c:256 * c + 256]
+                op("v", lambda q, sc=sc, K=K: q.tensor_tensor_scan(sc, T.D0[:], K[:, 0:256], 0.0, A.add, A.min),
+                   ["D0", "k" + C], ["SC" + C], vc(256), [kb])
+                ends = T.SC[:, 256 * c + 15:256 * c + 256:16]
+                if h < 3:
+                    tt(T.KM[:, k16], ends, T.CUR[:, k16], A.min, ["SC" + C, "CUR" + C], ["KM" + C], 16)
+                else:
+                    cp(T.KM[:, k16], ends, ["SC" + C], ["KM" + C], 16)
+                FB, fn, uv = (T.FH, "FH" + C, h) if h < 2 else (T.FU, "FU" + C, h - 2)
+                if t == 0 and uv == 0:
+                    ms(FB[:, 32 * c + 1:32 * c + 32:2], 0, [fn + "1"], 16)
+                ts(FB[:, 32 * c + uv:32 * c + 32:2], T.KM[:, k16], 127, None, A.bitwise_and, None, ["KM" + C], [fn + str(uv)], 16)
+                if h < 3:
+                    ts(T.CUR[:, k16], T.KM[:, k16], -3969, None, A.bitwise_and, None, ["KM" + C], ["CUR" + C], 16)
+                tt(T.EX[:, cs], FB[:, 32 * c:32 * c + 32].indirect(T.XL[:, 12 + 8 * uv:20 + 8 * uv]), T.MK[:], A.mult,
+                   [fn + "0", fn + "1", "XLb", "XLc", "MK0", "MK1"], ["EX" + C], 128, ga=True)
+                for j in range(16):
+                    mm(K[:, 256:264], T.LG[:, 128 * (j % 8):128 * (j % 8) + 128], T.EX[:, 128 * c + 8 * j:128 * c + 8 * j + 8], j == 0, j == 15,
+                       ["LG%d" % (j % 8), "EX" + C], ["kl" + C], 128, 8, kb)
+                ts(lo, K[:, 256:264], 8096.0, None, A.add, None, ["kl" + C], [lon], 8, pb=[kb])
+        bias[0] = 0.0
+        for tb, pbk in ((0, 6), (1, 7)):
+            mm(P[pbk][:, 128:452], T.ZR[:], T.SI[:, 0:324], True, False, ["ZR", "SI0", "SI1", "SI2"], ["tb%d" % tb], 128, 324, pbk)
+        for c in range(3):
+            C = str(c)
+            K, kb = P[1 + c], 1 + c
+            cs = slice(128 * c, 128 * c + 128)
+            xc, xn = T.X[:, xo + 128 * c:xo + 128 * c + 128], "X%d%d" % (t, c)
+            lu = [T.LUV[:, 24 * u + 8 * c:24 * u + 8 * c + 8] for u in range(2)]
+            ln = ["LU0" + C, "LU1" + C]
+            US = ["0" + C, "1" + C]
+            bs = [slice(S * u + 128 * c, S * u + 128 * c + 128) for u in range(2)]
+            es = [slice(400 * u + 128 * c, 400 * u + 128 * c + 128) for u in range(2)]
+            tb, pbk = c // 2, 6 + c // 2
+            tt(T.SMA[:, c:24:3], T.CUR[:, 16 * c:16 * c + 8], T.THK[:, 8 * c:8 * c + 8], A.is_ge, ["CUR" + C, "THK" + C], ["far" + C], 8)
+            for u in range(2):
+                U = US[u]
+                ha, hc = slice(16 * c + u, 16 * c + 16, 2), slice(48 + 16 * c + u, 64 + 16 * c, 2)
+                ts(T.HT[:, ha], T.FU[:, 32 * c + u:32 * c + 16:2], 4, None, A.arith_shift_right, None, ["FU%d%d" % (c, u)], ["HTa" + U], 8)
+                ts(T.HT[:, hc], T.FU[:, 32 * c + 16 + u:32 * c + 32:2], -4.0, 506.0, A.mult, A.add, ["FU%d%d" % (c, u)], ["HTb" + U], 8)
+                tt(T.HF[:, ha], T.HT[:, ha], T.HT[:, hc], A.add, ["HTa" + U, "HTb" + U], ["HF" + U], 8)
+                act(T.OT[:, bs[u]], T.OH[:].indirect(lu[u]), ID, OHR + [ln[u]], ["OT" + U], 128, ga=True)
+                mm(P[4 + u][:, cs], T.OT[:, bs[u]], T.IB[:], True, True, ["OT" + U, "IB"], ["dl%d" % (4 + u)], 128, 128, 4 + u)
+                act(T.AW[:, bs[u]], P[4 + u][:, cs], ID, ["dl%d" % (4 + u), "PCe"], ["AW" + U], 128, scale=cW[c], pb=[4 + u])
+                for gg in range(8):
+                    j = 16 * c + 2 * gg + u
+                    ts(T.BB[:, HB * j:HB * j + HB], T.I162[:], T.HF[:, j:j + 1], None, A.is_equal, None, ["I162", "HF" + U], ["BB%d" % j], HB, .5)
+                    a = 32 * (gg // 2)
+                    o = 128 + HB * (gg % 2)
+                    ao = S * u + 128 * c + a
+                    mm(P[pbk][a:a + 32, o:o + HB], T.AW[:, ao:ao + 32], T.BB[:, HB * j:HB * j + HB], False, False,
+                       ["AW" + U, "BB%d" % j], ["tb%d" % tb], 32, HB, pbk)
+            if c > 0:
+                mm(P[pbk][:, 128:452], T.ZR[:], T.SI[:, 0:324], False, True, ["ZR", "SI0", "SI1", "SI2"], ["tb%d" % tb], 128, 324, pbk)
+                act(T.TS[:, 336 * tb:336 * tb + 324], P[pbk][:, 128:452], ID, ["tb%d" % tb], ["TS%d" % tb], 324, pb=[pbk])
+            Z = [K[:, 0:128], K[:, 128:256]]
+            Y = [K[:, 256:384], K[:, 384:512]]
+            kz, ky = ["k" + C], ["kl" + C, "ki" + C, "ks" + C] + (["k2e"] if c == 2 else [])
+            for u in range(2):
+                U = US[u]
+                cp(T.EB[:, es[u]], T.NB[:, 0:GW].indirect(lu[u]), NBR + [ln[u]], ["EB" + U], 128, ga=True)
+                act(T.UV[:, es[u]], T.IOT[:].indirect(lu[u]), ID, ["IOT", ln[u]], ["UV" + U], 128, ga=True)
+                act(T.WB[:, es[u]], T.W[:, 0:GW].indirect(lu[u]), ID, WR + [ln[u]], ["WB" + U], 128, ga=True)
+                act(T.AGB[:, bs[u]], T.EB[:, es[u]], ID, ["EB" + U], ["AG" + U], 128, bias=128.7, scale=1.0 / 4096)
+                act(T.WT[:, bs[u]], T.AGB[:, bs[u]], F.Exp, ["AG" + U, "PC10"], ["WT" + U], 128, bias=PC[:, 10:11], scale=12 * LN2)
+            act(T.RB[:, cs], T.EB[:, es[0]], F.Relu, ["EB0" + C], ["RB" + C], 128, bias=-32767.0 * 65536, scale=65536.0)
+            for u in range(2):
+                U = US[u]
+                mm(Y[u], T.IF[:], T.UV[:, es[1 - u]], True, False, ["IF", "UV" + US[1 - u]], ky, 128, 128, kb, 4)
+                mm(Y[u], T.NF32[:], T.EB[:, es[u]], False, False, ["NF32", "EB" + U], ky, 128, 128, kb, 4)
+                mm(Y[u], T.SJ[:, 0:128], T.AGB[:, bs[u]], False, True, ["SJ0", "AG" + U], ky, 128, 128, kb)
+            mm(Z[0], T.IF[:], T.EB[:, es[0]], True, False, ["IF", "EB0" + C], kz, 128, 128, kb, 4)
+            mm(Z[0], T.IB[:], T.RB[:, cs], False, True, ["IB", "RB" + C], kz, 128, 128, kb)
+            for u in range(2):
+                act(T.DA[:, bs[u]], Y[u], F.Abs, ky, ["DA" + US[u]], 128, bias=-129.0 * 4096, pb=[kb])
+            act(T.TR[:, cs], Z[0], F.Relu, kz + ["PC14"], ["TR" + C], 128, bias=PC[:, 14:15], scale=-1.0, pb=[kb])
+            for u in range(2):
+                act(T.MT[:, bs[u]], T.DA[:, bs[u]], F.Relu, ["DA" + US[u]], ["MT" + US[u]], 128, bias=1.0, scale=-1.0)
+            for u in range(2):
+                U = US[u]
+                mm(Z[u], T.ZM[:, 0:128], T.WT[:, bs[u]], True, False, ["ZM0", "WT" + U], kz, 128, 128, kb)
+                mm(Z[u], T.ZM[:, 128:256], T.MT[:, bs[u]], False, True, ["ZM1", "MT" + U], kz, 128, 128, kb)
+                mm(Y[u], T.SJ[:, 256 + 128 * u:384 + 128 * u], T.ON[:], True, False, ["SJ2", "SJ3", "ON"], ky, 128, 128, kb)
+                mm(Y[u], T.SI[:, 256 * u:256 * u + 128], T.WB[:, es[u]], False, False, ["SI0", "SI2", "WB" + U], ky, 128, 128, kb)
+                mm(Y[u], T.SI[:, 256 * u + 128:256 * u + 256], xc, False, True, ["SI1", "SI3", xn], ky, 128, 128, kb)
+            for u in range(2):
+                U = US[u]
+                act(T.SG[:, bs[u]], Z[u], F.Sign, kz, ["SG" + U], 128, pb=[kb])
+                act(T.DA[:, bs[u]], Y[u], ID, ky, ["DA" + U], 128, bias=RND, pb=[kb])
+            for u in range(2):
+                U = US[u]
+                act(T.WI[:, bs[u]], T.DA[:, bs[u]], ID, ["DA" + U], ["WI" + U], 128, bias=-RND)
+                mm(Z[u], T.SI[:, 512:640], T.SG[:, bs[u]], True, False, ["SI4", "SG" + U], kz, 128, 128, kb)
+                if u == 0:
+                    mm(Z[0], T.NI[:, 0:128], T.ON[:], False, False, ["NI0", "ON"], kz, 128, 128, kb)
+                    mm(Z[0], T.NF32[:], T.TR[:, cs], False, True, ["NF32", "TR" + C], kz, 128, 128, kb, 4)
+                else:
+                    mm(Z[1], T.SI[:, 512:640], T.ON[:], False, False, ["SI4", "ON"], kz, 128, 128, kb)
+                    mm(Z[1], T.IF[:], T.EB[:, es[1]], False, True, ["IF", "EB1" + C], kz, 128, 128, kb, 4)
+            for u in range(2):
+                act(T.MS[:, bs[u]], Z[u], ID, kz, ["MS" + US[u]], 128, pb=[kb])
+        LUR = ["LU%d%d" % (u, c) for u in range(2) for c in range(3)]
+        al = lambda s: [s + "%d%d" % (u, c) for u in range(2) for c in range(3)]
+        cp(T.LF[:, 0:48], T.LUV[:], LUR, ["LF"], 48)
+        ts(T.LF[:, 48:72], T.LUV[:, 24:48], -float(n0), None, A.add, None, LUR, ["LFa"], 24)
+        ts(T.LF[:, 72:96], T.LUV[:, 0:24], -float(n0), None, A.add, None, LUR, ["LFb"], 24)
+        RP = P[0]
+        for c0, c1 in ((0, 2), (2, 3)):
+            for u in range(2):
+                a, b, nm = 24 * u + 8 * c0, 24 * u + 8 * c1, "%d%d" % (u, c0)
+                cp(T.LI[:, a:b], T.LUV[:, a:b], ["LU%d%d" % (u, c) for c in range(c0, c1)], ["LI" + nm], 16)
+                ts(T.LI[:, a:b], T.LI[:, a:b], 4, None, A.arith_shift_right, None, ["LI" + nm], ["LI" + nm], 16)
+                ts(T.LT[:, a:b], T.LI[:, a:b], PC[:, 12:13], None, A.add, None, ["LI" + nm, "PC12"], ["LT" + nm], 16)
+                d = slice(S * u + 128 * c0, S * u + 128 * c1)
+                ot = ["OT%d%d" % (u, c) for c in range(c0, c1)]
+                tt(T.RR[:, d], T.TS[:, 0:336].indirect(T.LT[:, a:b]), T.OT[:, d], A.mult, ["TS0", "TSd", "LT" + nm] + ot, ["RR" + nm], 128 * (c1 - c0), ga=True)
+                if c0 == 2:
+                    tt(T.RR[:, 768 + 128 * u:896 + 128 * u], T.TS[:, 336:660].indirect(T.LT[:, a:b]), T.OT[:, d], A.mult, ["TS1", "LT" + nm] + ot, ["RS%d" % u], 128, ga=True)
+        for u in range(2):
+            for c in range(3):
+                o = RP[:, 256 + 24 * u + c:256 + 24 * u + 24:3] if c < 2 else RP[:, 304 + 8 * u:312 + 8 * u]
+                mm(o, T.RR[:, S * u + 128 * c:S * u + 128 * c + 128], T.RC[:, 32:40], True, True, ["RR%d%d" % (u, c // 2 * 2), "RC32"], ["rp%d%d" % (u, c)], 128, 8, 0)
+        for u in range(2):
+            mm(RP[:, 258 + 24 * u:280 + 24 * u:3], T.RR[:, 768 + 128 * u:896 + 128 * u], T.RC[:, 32:40], True, True, ["RS%d" % u, "RC32"], ["rq%d" % u], 128, 8, 0)
+        m = T.SMA
+        FAR = ["far0", "far1", "far2"]
+        far, ok, cnt, cn, aa, c1, ns, b2, m1 = m[:, 0:24], m[:, 32:96], m[:, 96:120], m[:, 128:152], m[:, 160:184], m[:, 192:216], m[:, 224:248], m[:, 256:280], m[:, 288:312]
+        want, rest = T.SMB[:, 0:24], T.SMB[:, 32:56]
+        tt(ok, RP[:, 256:320], T.THR[:], A.is_le, al("rp") + ["rq0", "rq1", "THR0", "THR1", "THR2", "THRx"], ["ok"], 64, pb=[0])
+        tt(m[:, 34:80:3], m[:, 34:80:3], m[:, 80:96], A.mult, ["ok"], ["ok"], 16)
+        tt(cnt, m[:, 32:56], m[:, 56:80], A.mult, ["ok"], ["cnt"], 24)
+        tt(want, cnt, far, A.mult, ["cnt"] + FAR, ["want"], 24)
+
+        def prefix(o, src, nm, on):
+            mm(RP[:, o:o + 24], T.TRI[:], T.SMB[:, src:src + 24], True, False, ["TRI", nm], [on], 128, 24, 0)
+            for x, y in ((0, 1), (0, 2), (1, 2)):
+                mm(RP[:, o + y:o + 24:3], T.ON[:], T.SMB[:, src + x:src + 24:3], False, x == 1, ["ON", nm], [on], 128, 8, 0)
+        prefix(320, 0, "want", "kp")
+        ts(aa, want, -2048.0, 2048.0, A.mult, A.add, ["want"], ["aa"], 24)
+        ts(cn, cnt, 1024.0, None, A.mult, None, ["cnt"], ["cn"], 24)
+        tt(c1, aa, RP[:, 320:344], A.add, ["aa", "kp"], ["c1"], 24, pb=[0])
+        if not last:
+            ts(ns, c1, 96.0, None, A.is_ge, None, ["c1"], ["ns"], 24)
+            tt(rest, ns, far, A.mult, ["ns"] + FAR, ["rest"], 24)
+            prefix(352, 32, "rest", "kq")
+        ts(aa, c1, 96.0, 2048.0, A.is_ge, A.mult, ["c1"], ["aa"], 24)
+        tt(c1, c1, aa, A.add, ["c1", "aa"], ["c1"], 24)
+        tt(m1, c1, T.DS[:], A.min, ["c1", "DS0", "DS1", "DS2"], ["m1"], 24)
+        if not last:
+            ts(b2, rest, -2048.0, 2144.0, A.mult, A.add, ["rest"], ["b2"], 24)
+            tt(b2, b2, RP[:, 352:376], A.add, ["b2", "kq"], ["b2"], 24, pb=[0])
+            tt(m1, m1, b2, A.min, ["m1", "b2"], ["m1"], 24)
+        tt(T.PK[:], m1, cn, A.add, ["m1", "cn"], ["PK"], 24)
+        tt(T.EXP[:], T.PK[:].indirect(T.XL[:, 0:12]), T.MK24[:], A.mult, ["PK", "XLa", "MK24"], ["EXP"], 192, ga=True)
+        for r_ in range(2):
+            for gg in range(8):
+                mm(RP[:, 384 + 24 * r_:408 + 24 * r_], T.LG[:, 128 * gg:128 * gg + 128], T.EXP[:, 24 * gg:24 * gg + 24], gg == 0, gg == 7,
+                   ["LG%d" % gg, "EXP"], ["pp%d" % r_], 128, 24, 0)
+        l = T.LSA
+        P2, lm, pos, l1, l2 = RP[:, 384:432], l[:, 0:48], l[:, 48:96], l[:, 96:144], l[:, 144:192]
+        PP = ["pp0", "pp1"]
+        ts(lm, P2, 1024.0, -1024.0, A.is_ge, A.mult, PP, ["lm"], 48, pb=[0])
+        ts(l1, P2, 1024.0, 4096.0, A.is_lt, A.mult, PP, ["l1"], 48, pb=[0])
+        tt(pos, lm, P2, A.add, PP + ["lm"], ["pos"], 48, pb=[0])
+        cp(T.LP[:], l[:, 48:72], ["pos"], ["LP"], 24)
+        ms(T.CP[:, 0:208], float(S), ["CPa"], 208)
+        cp(T.CP[:].indirect(T.LP[:]), T.IOT[:, 0:S], ["IOT", "LP"], ["CPa", "CPb"], S, sc=True)
+        cp(T.C16[:], T.CP[:, 0:208], ["CPa"], ["C16"], 208)
+        if not last:
+            for a in range(16):
+                mm(P[6][:, 0:7], T.DG[:, 128 * a:128 * a + 128], T.C16[:, CN + 7 * a:CN + 7 * a + 7], a == 0, a == 15, ["DG%d" % a, "C16"], ["ps"], 128, 7, 6)
+            ts(T.LSN[:, 0:14:2], P[6][:, 0:7], 0.0, None, A.add, None, ["ps"], ["LSa"], 7, pb=[6])
+            ts(T.LSN[:, 1:14:2], P[6][:, 0:7], 400.0, None, A.add, None, ["ps"], ["LSb"], 7, pb=[6])
+            so = 224 * t
+            act(T.SND[:, so:so + 224], T.XE[:].indirect(T.LSN[:, 0:14]), ID,
+                ["LSa", "LSb", "XEd", "XEe"] + ["XEx%d" % c for c in range(3)] + ["XEe%d" % c for c in range(3)], ["SND%d" % t], 224, ga=True)
+
+            def fire(q, t=t, so=so):
+                tr = []
+                for k in range(N - 1):
+                    dst = T.cores[(rank + 1 + k) % N]
+                    rid, pid = topo.addr(dst)[0:2]
+                    en = topo.engines(core, dst)
+                    tr.append(RemoteDMATransfer(dst_ids=[DstId(rid=rid, pnc=pid)], dma_engine_mask=1 << en[k % len(en)],
+                                                remote_sem=T.sem["arr%d" % t], src=T.SND[:, so + 32 * k:so + 32 * k + 32],
+                                                dst=T.LND[:, so + 32 * k:so + 32 * k + 32]))
+                return q.remote_dma_fused(tr, local_sem=T.sem["loc%d" % t])
+            send[t] = op("g", fire, ["SND%d" % t], [], 1000, kind="r")
+        for a in range(16):
+            mm(P[7][:, 460:466], T.DG[:, 128 * a:128 * a + 128], T.C16[:, a:CN:16], a == 0, a == 15, ["DG%d" % a, "C16"], ["pt"], 128, 6, 7)
+        ts(T.LSP[:, 0:6], P[7][:, 460:466], 0.0, None, A.add, None, ["pt"], ["LPa"], 6, pb=[7])
+        ts(T.LSP[:, 6:12], P[7][:, 460:466], 400.0, None, A.add, None, ["pt"], ["LPb"], 6, pb=[7])
+        tt(l1, l1, T.LF[:, 0:48], A.add, ["l1", "LF"], ["l1"], 48)
+        tt(l1, l1, T.DUM[:], A.min, ["l1", "DUM"], ["l1"], 48)
+        cp(T.LD[:], l1, ["l1"], ["LD"], 48)
+        ts(l2, pos, 96.0, -8192.0, A.is_ge, A.mult, ["pos"], ["l2"], 48)
+        tt(l2, l2, pos, A.add, ["l2", "pos"], ["l2"], 48)
+        tt(l2, l2, T.LF[:, 48:96], A.max, ["l2", "LFa", "LFb"], ["l2"], 48)
+        ts(T.LTG[:], l2, float(n0), None, A.add, None, ["l2"], ["LTG"], 48)
+        TB, TBN = (T.NF, ["NF%d" % k for k in range(5)] + ["NFn"]) if last else (T.NB, NBR)
+        EBR = ["EB0%d" % c for c in range(3)] + ["EBd"]
+        UVR = al("UV") + ["UVd", "UVe"]
+        nu = T.NU
+        act(nu[:, 0:96], T.EB[:, 0:400].indirect(T.LSP[:, 0:6]), ID, EBR + ["LPa", "PC6", "PC7"], ["nu0"], 96, bias=PC[:, 7:8], scale=PC[:, 6:7], ga=True)
+        act(nu[:, 96:192], T.UV[:].indirect(T.LSP[:, 0:6]), ID, UVR + ["LPa", "PC8"], ["nu1"], 96, scale=PC[:, 8:9], ga=True)
+        act(nu[:, 192:288], T.UV[:].indirect(T.LSP[:, 6:12]), ID, UVR + ["LPb", "PC9"], ["nu2"], 96, scale=PC[:, 9:10], ga=True)
+        for k in range(3):
+            mm(P[6][:, 16:112], T.IF[:], nu[:, 96 * k:96 * k + 96], k == 0, k == 2, ["IF", "nu%d" % k], ["pn"], 128, 96, 6, 4)
+        act(T.XS[:], T.X[:, xo:xo + 400].indirect(T.LSP[:, 0:6]), ID, ["X%d%d" % (t, c) for c in range(3)] + ["Xd%d" % t, "LPa"], ["XS"], 96, ga=True)
+        act(T.WS[:], T.WB[:, 0:400].indirect(T.LSP[:, 0:6]), ID, ["WB0%d" % c for c in range(3)] + ["WBd", "LPa"], ["WS"], 96, ga=True)
+        for k, (a, b, nm) in enumerate(((T.SJ[:, 256:384], T.ON[:, 0:96], ["SJ2", "ON"]), (T.IB[:], T.XS[:], ["IB", "XS"]), (T.IB[:], T.WS[:], ["IB", "WS"]))):
+            mm(P[7][:, 128:224], a, b, k == 0, k == 2, nm, ["tb1"], 128, 96, 7)
+        act(nu[:, 288:384], P[7][:, 128:224], ID, ["tb1"], ["nu3"], 96, bias=RND, scale=.5, pb=[7])
+        for u in range(2):
+            b = slice(S * u, S * u + S)
+            qn = ["dl%d" % (4 + u)]
+            act(T.Q[:, b], T.IOT[:].indirect(T.LTG[:, 24 * u:24 * u + 24]), ID, ["IOT", "LTG"], ["Q%d" % u], S, bias=-65536.0, ga=True)
+            mm(P[4 + u][:, 0:S], T.SJ[:, 128:256], T.SG[:, b], True, False, ["SJ1"] + ["SG%d%d" % (u, c) for c in range(3)], qn, 128, S, 4 + u)
+            mm(P[4 + u][:, 0:S], T.IF[:], T.Q[:, b], False, True, ["IF", "Q%d" % u], qn, 128, S, 4 + u, 4)
+            tt(T.NW[:, b], T.MS[:, b], P[4 + u][:, 0:S], A.max, qn + ["MS%d%d" % (u, c) for c in range(3)], ["NW%d" % u], S, pb=[4 + u])
+            cp(TB[:].indirect(T.LD[:, 24 * u:24 * u + 24]), T.NW[:, b], ["NW%d" % u, "LD"], TBN, S, sc=True)
+        for u in range(2):
+            cp(T.W[:].indirect(T.LD[:, 24 * u:24 * u + 24]), T.WI[:, S * u:S * u + S], ["LD"] + ["WI%d%d" % (u, c) for c in range(3)], WR + ["Wn"], S, sc=True)
+        if last:
+            dma("a", T.yw[:, 0:n0], T.W[:, 0:n0], WR, ["yw"], 128 * PU * 6)
+            dma("s", T.yn[:, 0:n0], T.NF[:, 0:n0], TBN[0:5], ["yn"], 128 * PU * 4)
+            act(T.NF[:, n0:PU], P[6][:, 16:112], ID, ["pn"], ["NFn"], 96, pb=[6])
+            act(T.W[:, n0:PU], nu[:, 288:384], ID, ["nu3"], ["Wn"], 96, bias=-RND)
+            dma("s", T.yn[:, n0:PU], T.NF[:, n0:PU], ["NFn"], ["yn2"], 50000)
+            dma("s", T.yw[:, n0:PU], T.W[:, n0:PU], ["Wn"], ["yw2"], 25000)
+        else:
+            cp(T.NB[:, n0:n0 + CN], P[6][:, 16:112], ["pn"], NBR, 96, pb=[6])
+            act(T.W[:, n0:n0 + CN], nu[:, 288:384], ID, ["nu3"], WR, 96, bias=-RND)
+    return ops
+
+
+def plan(ops):
+    n = len(ops)
+    pred = [[] for _ in range(n)]
+    succ = [[] for _ in range(n)]
+    for i, o in enumerate(ops):
+        for d in o["d"]:
+            w = (70 if o["d"][d] or o["e"] != "t" else 0) if ops[d]["e"] == o["e"] and ops[d]["k"] == "c" else 120
+            pred[i].append((d, w))
+            succ[d].append((i, w))
+    eng = [o["e"] for o in ops]
+    cost = [o["c"] for o in ops]
+    busy = [o["c"] if o["k"] == "c" else 60.0 for o in ops]
+
+    def run(prio, before, behind):
+        left = [len(x) for x in before]
+        rdy, fin = [0.0] * n, [0.0] * n
+        free = {e: 0.0 for e in "vatgsx"}
+        ready = {e: [] for e in "vatgsx"}
+        for i in range(n):
+            if not left[i]:
+                ready[eng[i]].append(i)
+        order = []
+        while len(order) < n:
+            best = None
+            for e, lst in ready.items():
+                if lst:
+                    t0 = max(free[e], min([rdy[i] for i in lst]))
+                    if best is None or t0 < best[0]:
+                        best = (t0, e)
+            t0, e = best
+            i = max([j for j in ready[e] if rdy[j] <= t0 + LOOK], key=lambda j: prio[j])
+            t0 = max(t0, rdy[i])
+            ready[e].remove(i)
+            order.append(i)
+            fin[i] = t0 + cost[i]
+            free[e] = t0 + busy[i]
+            for j, w in behind[i]:
+                if fin[i] + w > rdy[j]:
+                    rdy[j] = fin[i] + w
+                left[j] -= 1
+                if not left[j]:
+                    ready[eng[j]].append(j)
+        return order, fin
+    base = [0.0] * n
+    for i in range(n - 1, -1, -1):
+        base[i] = cost[i] + max([base[j] + w for j, w in succ[i]] + [0.0])
+    best = None
+    for k in range(TRIES):
+        prio = [base[i] + ops[i]["b"] * (k % 4 + 1) / 2.0 + (i * 2654435761 * (k // 4) % 1000) * 0.3 for i in range(n)]
+        for _ in range(ROUNDS):
+            order, fin = run(prio, pred, succ)
+            if best is None or max(fin) < best[0]:
+                best = (max(fin), order)
+            prio = run(fin, succ, pred)[1]
+    return best[1]
+
+
+def rank_program(g, core, T, topo):
+    rank = T.rank_of(core)
+    if rank is None:
+        return
+    ops = build(T, topo, rank, core)
+    if "order" not in CACHE:
+        CACHE["order"] = plan(ops)
+    order = CACHE["order"]
+    q = {"v": g.vector, "a": g.scalar, "t": g.tensor, "g": g, "s": g.sync}
+    esem = {"v": "sv", "a": "sa", "t": "st", "g": "sp"}
+    at = {i: k for k, i in enumerate(order)}
+
+    def needs(i, d):
+        a, b = ops[d], ops[i]
+        if a["k"] == "r" or b["k"][0] == "x":
+            return False
+        if a["e"] == b["e"] == "t":
+            return b["d"][d]
+        return True
+    waits = []
+    marked = set()
+    for i in range(len(ops)):
+        w = {}
+        for d in ops[i]["d"]:
+            if needs(i, d):
+                key = ops[d]["e"] if ops[d]["k"] == "c" else d
+                if key not in w or at[d] > at[w[key]]:
+                    w[key] = d
+        waits.append(list(w.values()))
+    seen = {}
+    for i in order:
+        keep = []
+        for d in waits[i]:
+            key = (ops[i]["e"], ops[d]["e"] if ops[d]["k"] == "c" else d)
+            if seen.get(key, -1) < at[d]:
+                seen[key] = at[d]
+                keep.append(d)
+                marked.add(d)
+        waits[i] = keep
+    count = {e: 0 for e in esem}
+    token = {}
+    nd = 0
+    for i in order:
+        o = ops[i]
+        if o["k"][0] == "x":
+            token[i] = ("arr" + o["k"][1], N - 1)
+            continue
+        for d in waits[i]:
+            q[o["e"]].wait_ge(T.sem[token[d][0]], token[d][1])
+        ins = o["f"](q[o["e"]])
+        if o["k"] == "d":
+            token[i] = ("d%d" % nd, 16)
+            ins.then_inc(T.sem["d%d" % nd], 16)
+            nd += 1
+        elif o["k"] == "c" and i in marked:
+            count[o["e"]] += 1
+            token[i] = (esem[o["e"]], count[o["e"]])
+            ins.then_inc(T.sem[esem[o["e"]]], 1)
+    for e in esem:
+        if count[e]:
+            g.wait_ge(T.sem[esem[e]], count[e])
+    for k in range(nd):
+        g.wait_ge(T.sem["d%d" % k], 16)
+    for t in range(NT - 1):
+        g.wait_ge(T.sem["loc%d" % t], N - 1)
+        g.wait_ge(T.sem["arr%d" % t], N - 1)

@@ -7,30 +7,40 @@ PU = L + NT * CN
 GW = 2608
 TW = GW + 2 * S
 HB = 162
+MID = 1344.0
 LN2 = math.log(2.0)
 RND = 12582912.0
+XLO, XHI = 64, 384
+XW = 16 * (XHI - XLO)
 bf, f32, i32, u16, f16 = "bfloat16", "float32", "int32", "uint16", "float16"
 SCRATCH = {}
 for _d, _s in (
-        (bf, "W:3376 OH:2608 ONE:2608 X:1200 BH:384 G:6144 M:6144 G0:384 M0:384 BH0:384 BB:7776 OT:768 AW:768 TS:672 RR:1024 SMB:64 "
-             "WB:800 AGB:768 WT:768 MT:768 SG:768 RB:384 WI:768 WS:96 XS:96 IB:128 NI:256 RC:80 TRI:128 ON:128 ZR:128 ZM:256 SI:640 "
-             "SJ:512 I162:162"),
-        (f32, "NF:3376 IOT:2608 THB:128 TH8:8 SC:768 ID0:384 THK:24 HF:48 SMA:320 PK:24 LF:96 LSA:192 CP:864 EB:800 UV:800 MS:768 "
-              "DA:768 TR:384 Q:768 NW:768 TA:128 NU:384 XE:800 SND:448 LND:448 OWN:448 CI:256 CM:128 CD:128 PC:32 RA:16 R32:8 SMM:128 "
-              "SGM:128 IF:128 NF32:128 D0:256 MK:128 MK24:192 THR:64 DUM:48 DS:24 CT:64"),
-        (i32, "NB:3376 EN:72 THI:8 I32:384 KM:48 CUR:48 FH:96 FU:96 HT:96 LI:48 MX:224 MY:224 PI:8 CTI:16"),
-        (u16, "LE:72 O16:384 LH:48 LUV:48 LT:48 LD:48 LTG:48 LP:24 LSN:16 LSP:16 XL:32 PL:16"),
-        (f16, "A16:384 EX:384 EXP:192 C16:208 E16:112 I16:128 LG:1024 DG:2048")):
+        (bf, "W:3376 OH:2608 X:1200 XR:15360 BH:384 G:6144 M:6144 G0:384 M0:384 BH0:384 BB:7776 OT:768 AW:768 TS:672 TG:324 RR:768 RX:1088 "
+             "WB:800 AGB:768 WT:768 MT:768 SG:768 RB:384 WS:96 XS:96 WN:96 IB:128 NI:400 RC:48 ON:384 ZR:128 ZM:256 SI:640 "
+             "SJ:640 I162:162 GS:2048 SGB:128 CC:128"),
+        (f32, "NF:3376 IOT:2608 THB:128 THK:24 XE:384 HF:48 FAR:72 LSA:240 CP:864 EB:768 MS:768 NEW:400 NFN:96 "
+              "NW:768 TA:128 NU:96 SND:224 LND:224 OWN:224 CI:256 CM:128 CD:128 PC:32 R32:24 SMM:128 "
+              "SGM:128 IS:136 IF:128 D0:544 MK24:320 THR:48 DUM:48 DS:72 CT:64 TRI:128 K17:408"),
+        (i32, "NB:3376 EN:72 THI:8 I32:384 SC:816 CUR:48 FH:72 HT:96 LI:48 MX:112 MY:224 PI:16 WI:768"),
+        (u16, "LE:72 O16:384 LH:48 LUV:48 LT:48 LD:48 LP:24 LSP:8 XL:32 PL:16"),
+        (f16, "A16:384 EX:384 EXP:192 C16:96 E16:112 I16:520 LG:240 SH:304 ID0:384 RA:16 D16:256 IO6:384 SEL:2048 SG6:128 TB:384 LF:72 TGT:48 CL:192 IS6:384 UV:768")):
     for _x in _s.split():
         SCRATCH[_x.split(":")[0]] = ("sbuf", [128, int(_x.split(":")[1])], _d)
 for _k in range(8):
     SCRATCH["P%d" % _k] = ("psum", [128, 512], f32)
 SEMAPHORES = ["sv", "sa", "sp", "st", "arr0", "arr1", "loc0", "loc1"] + ["d%d" % _k for _k in range(20)]
 
-GAM, SIG, CY, PECY = 1.56, 3.8, 1.0, 0.55
-NE = 2
-STAG = [0.0, -4000.0, -8000.0]
-BINIT, LOOK, ROUNDS, TRIES = 5000.0, 60.0, 5, 24
+GAM, SIG, CY, PECY, VF, AF, TF = 1.56, 3.8, 0.83, 0.44, 5.0, 30.0, 5.0
+NA = [[0, 0, 0]] * 4
+NE = [[0, 0, 0]] * 4
+AP_, BP_ = 32, 64
+ND, EBS = 2, True
+LATE = ["OT12", "TS1", "TS1"]
+AWV = (2,)
+SI32, MSS = True, (False, True)
+STAG = [0.0, 0.0, 0.0]
+BINIT, LOOK, ROUNDS, TRIES, SHAKES = 5000.0, 60.0, 3, 8, 150
+WSAME, WOTHER = 200.0, 200.0
 CACHE = {}
 ID = F.Identity
 
@@ -45,8 +55,7 @@ def build(T, topo, rank, core):
         n = len(ops)
         deps = {}
         for x in r:
-            if x in last_w:
-                deps[last_w[x]] = True
+            deps[last_w[x]] = True
         for x in w:
             if x in last_w:
                 deps.setdefault(last_w[x], False)
@@ -73,68 +82,77 @@ def build(T, topo, rank, core):
         return n
 
     def vc(n, c=1.0):
-        return 20 + max(64, n * c) * CY
+        return VF + max(64, n * c) * CY
 
     def ts(o, i, s1, s2, o0, o1, r, w, n, c=1.0, pb=(), ga=False):
-        cost = 60 + n * GAM * CY if ga else vc(n, c)
+        cost = 50 + n * GAM * CY if ga else vc(n, c)
         if o1 is None:
             return op("v", lambda q: q.tensor_scalar(o, i, s1, None, o0), r, w, cost, pb)
         return op("v", lambda q: q.tensor_scalar(o, i, s1, s2, o0, o1), r, w, cost, pb)
 
     def tt(o, a, b, o0, r, w, n, pb=(), ga=False):
-        cost = 60 + n * GAM * CY if ga else vc(n, 1.0 if pb else 2.0)
+        cost = 50 + n * GAM * CY if ga else vc(n, 1.0 if pb else 2.0)
         return op("v", lambda q: q.tensor_tensor(o, a, b, o0), r, w, cost, pb)
 
     def cp(o, i, r, w, n, c=1.0, pb=(), ga=False, sc=False):
-        cost = 60 + n * (SIG if sc else GAM) * CY if (ga or sc) else vc(n, c)
+        cost = 50 + n * (SIG if sc else GAM) * CY if (ga or sc) else vc(n, c)
         return op("v", lambda q: q.tensor_copy(o, i), r, w, cost, pb)
 
     def ms(o, v, w, n, c=1.0):
         return op("v", lambda q: q.memset(o, v), [], w, vc(n, c))
 
+    def scan(o, d0, d1, ini, o0, o1, r, w, n, pb=()):
+        return op("v", lambda q: q.tensor_tensor_scan(o, d0, d1, ini, o0, o1), r, w, vc(n), pb)
+
     def act(o, i, fn, r, w, n, bias=0.0, scale=1.0, pb=(), ga=False):
-        cost = 80 + n * (GAM if ga else 1.0) * CY
+        cost = 65 + n * GAM * CY if ga else AF + n * CY
         return op("a", lambda q: q.activation(o, i, fn, bias=bias, scale=scale), r, w, cost, pb)
 
     def mm(o, l, rr, st, sp, r, w, m, n, pb, x=1):
-        return op("t", lambda q: q.matmul(o, l, rr, st, sp), r, w, 8 + x * max(min(64, m), n) * PECY, [pb])
+        return op("t", lambda q: q.matmul(o, l, rr, st, sp), r, w, TF + x * max(min(64, m), n) * PECY, [pb])
 
     def iota(o, pat, base, cm, w, n, fl=True):
         if fl:
             return op("g", lambda q: q.iota(o, pat, base, cm, allow_small_or_imprecise_dtypes=True), [], w, 130 + 2 * n * CY)
         return op("g", lambda q: q.iota(o, pat, base, cm), [], w, 130 + 2 * n * CY)
 
-    def dma(eng, o, i, r, w, nbytes):
-        return op(eng, lambda q: q.dma_start(o, i), r, w, 2000 + nbytes / 190.0, kind="d")
+    def sel(o, i, pat, base, r, w, n):
+        return op("g", lambda q: q.affine_select(o, i, pat, A.is_equal, 0.0, base, 0), r, w, 170 + 2 * n * CY)
 
-    dma("s", T.EN[:], T.ent[:], [], ["EN"], 36864)
-    dma("s", T.NB[:, 0:L], T.nb[:], [], ["NBa"], 128 * L * 4)
-    dma("a", T.W[:, 0:L], T.w[:], [], ["Wa"], 128 * L * 6)
-    dma("a", T.X[:, 0:S], T.x[:, 0:S], [], ["X00", "X01", "X02"], 128 * L * 2)
-    dma("s", T.THI[:, 0:1], T.th[:], [], ["THI"], 128 * L * 3)
+    def dma(eng, o, i, r, w, ns):
+        return op(eng, lambda q: q.dma_start(o, i), r, w, ns, kind="d")
+
+    XN_ = [["X%d%d" % (t, c) for c in range(3)] for t in range(NT)]
+    dma("s", T.X[:, 0:S], T.x[:, 0:S], [], XN_[0], 3000)
+    dma("s", T.EN[:], T.ent[:], [], ["EN"], 6000)
+    dma("s", T.NB[:, 0:L], T.nb[:], [], ["NBa"], 9000)
+    dma("a", T.W[:, 0:L], T.w[:], [], ["Wa"], 10000)
+    dma("s", T.THI[:, 0:1], T.th[:], ["Wa"], ["THI"], 2500)
     for t in (1, 2):
-        dma("s", T.X[:, 400 * t:400 * t + S], T.x[:, S * t:S * t + S], ["Wa"], ["X%d0" % t, "X%d1" % t, "X%d2" % t], 128 * S * 2)
-    ms(T.NB[:, L:TW], 65535, ["NBb"], TW - L)
-    ms(T.W[:, L:PU], 0.0, ["Wb"], 288, .5)
-    ms(T.W[:, PU:TW], 8192.0, ["Wc"], TW - PU, .5)
-    ms(T.NF[:, GW:TW], 0.0, ["NF4"], 768)
-    for t in range(NT):
-        ms(T.X[:, 400 * t + S:400 * t + 400], 0.0, ["Xd%d" % t], 16)
+        dma("s", T.X[:, 400 * t:400 * t + S], T.x[:, S * t:S * t + S], ["Wa"], XN_[t], 2500)
     NBR, WR = ["NBa", "NBb"], ["Wa", "Wb", "Wc"]
-    cp(T.LE[:], T.EN[:], ["EN"], ["LE%d%d" % (t, c) for t in range(NT) for c in range(3)], 72)
 
     PC, CP_ = T.PC, ["CI", "PC"]
-    iota(T.CI[:], [[1, 256]], 0, 0, ["CI"], 256)
-    iota(T.PI[:, 0:1], [[0, 1]], 0, 1, ["PI0"], 1, False)
-    iota(T.CM[:], [[0, 8], [1, 16]], 0, 0, ["CM"], 128)
-    iota(T.CD[:], [[1, 8], [0, 16]], 0, 0, ["CD"], 128)
-    iota(T.IOT[:], [[1, GW]], 0, 0, ["IOT"], GW)
-    ms(T.ONE[0:32, :], 1.0, ["ONE"], GW, .5)
-    op("g", lambda q: q.affine_select(T.OH[0:16, :], T.ONE[0:16, :], [[0, GW // 16], [-1, 16]], A.is_equal, 0.0, 0, 1),
-       ["ONE"], ["OH0"], 170 + 2 * GW * CY)
-    for k in range(1, 8):
-        dma("s", T.OH[16 * k:16 * k + 16, :], T.OH[0:16, :], ["OH0"], ["OH%d" % k], 90000)
-    OHR = ["OH%d" % k for k in range(8)]
+    iota(T.PI[:, 0:1], [[0, 1]], 0, 1, ["PI0", "g0"], 1, False)
+    iota(T.CI[:], [[1, 256]], 0, 0, ["CI", "g0"], 256)
+    iota(T.CM[:], [[0, 8], [1, 16]], 0, 0, ["CM", "g0"], 128)
+    iota(T.CD[:], [[1, 8], [0, 16]], 0, 0, ["CD", "g0"], 128)
+    iota(T.MK24[:, 0:192], [[0, 24], [1, 8]], 0, 0, ["MK24", "g0"], 192)
+    for k, (a, b, c) in enumerate(((16, 1, -1), (0, 1, -1), (1, 0, 0))):
+        iota(T.K17[:, 136 * k:136 * k + 136], [[a, 8], [b, 17]], c, 0, ["K17%d" % k, "g0"], 136)
+    iota(T.R32[:], [[1, 8], [0, 3]], 0, 0, ["R32", "g0"], 24)
+    iota(T.NB[:, L:GW], [[0, GW - L]], 65535, 0, ["NBb", "g0"], GW - L, False)
+    iota(T.IOT[:], [[1, GW]], 0, 0, ["IOT", "g0"], GW)
+    ms(T.W[:, L:PU], 0.0, ["Wb"], 288, .5)
+    ms(T.W[:, PU:GW], 8192.0, ["Wc"], 16, .5)
+    iota(T.NB[:, GW:TW], [[0, 768]], 0, 0, ["NBc"], 768, False)
+    iota(T.W[:, GW:TW], [[0, 768]], 0, 0, ["Wd"], 768)
+    iota(T.NF[:, GW:TW], [[0, 768]], 0, 0, ["NF4"], 768)
+    iota(T.CP[:], [[0, 864]], 0, 0, ["CPb"], 864)
+    for t in range(NT):
+        ms(T.X[:, 400 * t + S:400 * t + 400], 0.0, ["Xd%d" % t], 16)
+    ms(T.NEW[:, S:400], 65535.0, ["NEWd"], 16)
+    ms(T.WB[:, S:400], 0.0, ["WBd"], 16)
     ts(T.PI[:, 1:2], T.PI[:, 0:1], 15, None, A.bitwise_and, None, ["PI0"], ["PI1"], 1)
     ts(T.PI[:, 2:3], T.PI[:, 0:1], 4, None, A.arith_shift_right, None, ["PI0"], ["PI2"], 1)
     ts(T.PI[:, 3:4], T.PI[:, 0:1], 4, 1, A.arith_shift_right, A.bitwise_and, ["PI0"], ["PI3"], 1)
@@ -143,44 +161,82 @@ def build(T, topo, rank, core):
     cP, cA, cG, cO, cH = [PC[:, k:k + 1] for k in range(5)]
     ts(T.SMM[:], T.CM[:], cA, None, A.is_equal, None, ["CM", "PC"], ["SMM"], 128)
     ts(T.SGM[:], T.CD[:], cG, None, A.is_equal, None, ["CD", "PC"], ["SGM"], 128)
-    for o, v, nm in ((T.IB[:], 1.0, "IB"), (T.I16[:], 1.0, "I16"), (T.NI[:, 0:128], -1.0, "NI0"), (T.NI[:, 128:256], -1.0 / 64, "NI1"),
+    ts(T.IB[:], T.CI[:, 0:128], cP, None, A.is_equal, None, CP_, ["IB"], 128)
+    for o, v, nm in ((T.I16[:, 0:128], 1.0, "I16"), (T.NI[:, 0:128], -1.0, "NI0"), (T.IF[:], 1.0, "IF"),
+                     (T.I16[:, 128:256], -1.0, "I17"), (T.I16[:, 256:384], 4096.0, "I18"),
                      (T.SI[:, 0:128], .75, "SI0"), (T.SI[:, 128:256], .25, "SI1"), (T.SI[:, 256:384], .875, "SI2"),
-                     (T.SI[:, 384:512], .125, "SI3"), (T.SI[:, 512:640], -65536.0, "SI4"), (T.IF[:], 1.0, "IF"), (T.NF32[:], -1.0, "NF32"),
-                     (T.SJ[:, 0:128], 4096.0, "SJ0"), (T.SJ[:, 128:256], 65536.0, "SJ1"), (T.SJ[:, 256:384], -.375, "SJ2"),
-                     (T.SJ[:, 384:512], -.4375, "SJ3")):
-        ts(o, T.CI[:, 0:128], cP, v, A.is_equal, A.mult, CP_, [nm], 128)
-    for o, v in ((0, 4096.0), (8, 4096.0), (16, -8192.0), (24, -8192.0), (32, 1.0), (64, -4096.0), (72, -4096.0)):
+                     (T.SI[:, 384:512], .125, "SI3"), (T.SI[:, 512:640], -65536.0, "SI4"),
+                     (T.SJ[:, 0:128], 4096.0, "SJ0"), (T.SJ[:, 128:256], MID, "SJ1"), (T.SJ[:, 256:384], -.375, "SJ2"),
+                     (T.SJ[:, 384:512], -2.0 ** 21, "SJ3")):
+        ts(o, T.IB[:], v, None, A.mult, None, ["IB"], [nm], 128, .5)
+    ts(T.SJ[:, 512:640], T.IB[:], 2.0 ** 60, 2.0 ** 61, A.mult, A.mult, ["IB"], ["SJ4"], 128, .5)
+    I16, N16, B16 = T.I16[:, 0:128], T.I16[:, 128:256], T.I16[:, 256:384]
+    for o, v in ((0, 4096.0), (8, 4096.0), (16, -8192.0), (24, -8192.0)):
         ts(T.RC[:, o:o + 8], T.CI[:, 0:8], cG, v, A.is_equal, A.mult, CP_, ["RC%d" % o], 8)
-    ts(T.R32[:], T.CI[:, 0:8], cG, 256.0, A.is_equal, A.mult, CP_, ["R32"], 8)
+    R1, R2, R1N, R2N = T.RC[:, 0:16], T.RC[:, 16:32], ["RC0", "RC8"], ["RC16", "RC24"]
+    ts(T.R32[:], T.R32[:], cG, 256.0, A.is_equal, A.mult, ["R32", "PC"], ["R32"], 24)
     ms(T.RA[:, 8:16], 0.0, ["RA1"], 8)
     ts(T.RA[:, 0:8], T.CI[:, 0:128:16], cP, None, A.is_equal, None, CP_, ["RA0"], 8)
-    ts(T.RC[:, 48:56], T.CI[:, 0:128:16], cP, -1.0, A.is_equal, A.mult, CP_, ["RC48"], 8)
-    ts(T.RC[:, 56:64], T.CI[:, 0:128:16], cP, -1.0 / 64, A.is_equal, A.mult, CP_, ["RC56"], 8)
-    ms(T.D0[:], -128.0, ["D0"], 256)
-    ms(T.D0[:, 0:256:16], 1.0e9, ["D0"], 16)
-    for k in range(8):
-        ts(T.LG[:, 128 * k:128 * k + 128], T.CI[:, 0:128], -16.0 * k, cA, A.add, A.is_equal, CP_, ["LG%d" % k], 128)
+    ts(T.RC[:, 32:40], T.CI[:, 0:128:16], cP, -1.0, A.is_equal, A.mult, CP_, ["RC32"], 8)
+    ts(T.RC[:, 40:48], T.CI[:, 0:128:16], cP, -1.0 / 64, A.is_equal, A.mult, CP_, ["RC40"], 8)
+    ms(T.D0[:], -64.0, ["D0"], 544)
+    ms(T.D0[:, 0:544:17], 1.0e9, ["D0"], 32)
+    ms(T.D0[:, 273:544:17], 1.0e9, ["D0"], 16)
+    for o, v, nm in ((T.NI[:, 128:264], -1.0, "NI1"), (T.NI[:, 264:400], -1.0 / 64, "NI2"), (T.I16[:, 384:520], 1.0, "I19")):
+        ts(o, T.K17[:, 0:136], cP, v, A.is_equal, A.mult, ["K170", "PC"], [nm], 136)
+    ms(T.NI[:, 128:400:17], 0.0, ["NI1", "NI2"], 16)
+    ms(T.I16[:, 384:520:17], 0.0, ["I19"], 8)
+    ts(T.LG[:], T.CI[:, 0:240], -112.0, cA, A.add, A.is_equal, CP_, ["LG"], 240)
+    ts(PC[:, 15:16], cA, 1000.0, cP, A.mult, A.add, ["PC"], ["PC15"], 1)
+    ts(T.SH[:, 0:144], T.CI[:, 0:144], -15.0, PC[:, 15:16], A.add, A.is_equal, ["CI", "PC15"], ["SH"], 144)
+    ts(T.SH[:, 160:304], T.CI[:, 0:144], 1000.0 - 14.0, PC[:, 15:16], A.add, A.is_equal, ["CI", "PC15"], ["SH1"], 144)
+    LG = [T.LG[:, 112 - 16 * k:240 - 16 * k] for k in range(8)]
+    SH = [T.SH[:, 15 - k:143 - k] for k in range(16)]
+    cp(T.SG6[:], T.SGM[:], ["SGM"], ["SG6"], 128)
+    cp(T.SGB[:], T.SGM[:], ["SGM"], ["SGB"], 128)
     for k in range(16):
-        ts(T.DG[:, 128 * k:128 * k + 128], T.I16[:], T.SMM[:, k:k + 1], None, A.mult, None, ["I16", "SMM"], ["DG%d" % k], 128, .5)
-    iota(T.MK24[:], [[0, 24], [1, 8]], 0, 0, ["MK24"], 192)
-    ts(T.MK[:, 0:64], T.MK24[:, 0:64], cG, None, A.is_equal, None, ["MK24", "PC"], ["MK0"], 64)
-    ts(T.MK[:, 64:128], T.MK24[:, 0:64], cG, -64.0, A.is_equal, A.mult, ["MK24", "PC"], ["MK1"], 64)
-    ts(T.MK24[:], T.MK24[:], cG, None, A.is_equal, None, ["MK24", "PC"], ["MK24"], 192)
+        ts(T.SEL[:, 128 * k:128 * k + 128], T.SG6[:], T.SMM[:, k:k + 1], None, A.mult, None, ["SG6", "SMM"], ["SEL%d" % k], 128, .5)
+        sel(T.GS[:, 128 * k:128 * k + 128], T.SGB[:], [[0, 8], [1, 16]], -k, ["SGB"], ["GS%d" % k], 128)
+    RX = {}
+    for k, ne in enumerate(sorted(set(x for row in NE for x in row if x < 16))):
+        RX[ne] = T.RX[:, 272 * k:272 * k + 272]
+        if k == 0:
+            ts(T.K17[:, 272:408], T.K17[:, 272:408], cG, None, A.is_equal, None, ["K172", "PC"], ["K172"], 136)
+        ts(T.IS[:], T.K17[:, 136:272], float(ne), 4096.0, A.is_ge, A.mult, ["K171"], ["IS"], 136)
+        for o in (0, 136):
+            tt(T.RX[:, 272 * k + o:272 * k + o + 136], T.IS[:], T.K17[:, 272:408], A.mult, ["IS", "K172"], ["RX%d_%d" % (ne, o)], 136)
+    cp(T.OH[:, 0:128], T.SMM[:], ["SMM"], ["OH"], 128)
+    for a in (128, 256, 512, 1024, 2048):
+        b = min(a, GW - a)
+        sel(T.OH[:, a:a + b], T.OH[:, 0:b], [[0, b]], 0, ["OH"], ["OH"], b)
+    ts(T.MK24[:, 192:256], T.MK24[:, 0:64], cG, None, A.is_equal, None, ["MK24", "PC"], ["MK0"], 64)
+    ts(T.MK24[:, 256:320], T.MK24[:, 0:64], cG, -64.0, A.is_equal, A.mult, ["MK24", "PC"], ["MK1"], 64)
+    ts(T.MK24[:, 0:192], T.MK24[:, 0:192], cG, None, A.is_equal, None, ["MK24", "PC"], ["MK24"], 192)
     ts(T.CT[:, 0:12], T.CI[:, 0:24:2], cH, None, A.add, None, CP_, ["CT0"], 12)
     cp(T.XL[:, 0:12], T.CT[:, 0:12], ["CT0"], ["XLa"], 12)
-    ts(T.XL[:, 12:20], T.CT[:, 0:8], 2.0, None, A.mult, None, ["CT0"], ["XLb"], 8)
-    ts(T.XL[:, 20:28], T.CT[:, 0:8], 2.0, 1.0, A.mult, A.add, ["CT0"], ["XLc"], 8)
-    ts(T.TRI[:], T.CI[:, 0:128], cP, None, A.is_gt, None, CP_, ["TRI"], 128)
-    ms(T.ON[:], 1.0, ["ON"], 128)
+    cp(T.XL[:, 12:20], T.CI[:, 0:8], ["CI"], ["XLb"], 8)
+    ms(T.ON[:], 1.0, ["ON"], 384, .5)
     ms(T.ZR[:], 0.0, ["ZR"], 128)
     cp(T.I162[:], T.CI[:, 0:HB], ["CI"], ["I162"], HB)
+    ts(T.TRI[:], T.CI[:, 0:128], cP, -1.0, A.is_le, A.mult, CP_, ["TRI"], 128)
+    tt(T.TRI[:], T.TRI[:], T.SGM[:], A.mult, ["TRI", "SGM"], ["TRI"], 128)
+    for k, v in enumerate((-2047.0, 4097.0)):
+        ts(T.IS[:, 0:128], T.IB[:], v, None, A.mult, None, ["IB"], ["IS"], 128)
+        tt(T.TB[:, 128 * k:128 * k + 128], T.IS[:, 0:128], T.TRI[:], A.add, ["IS", "TRI"], ["TB%d" % k], 128)
+    cp(T.TB[:, 256:384], T.TRI[:], ["TRI"], ["TB2"], 128)
     ts(PC[:, 5:6], cA, 12.0, 4096.0, A.is_lt, A.mult, ["PC"], ["PC5"], 1)
-    ts(PC[:, 14:15], PC[:, 5:6], -1.0, 65535.0, A.mult, A.add, ["PC5"], ["PC14"], 1)
     ts(PC[:, 6:7], cA, 12.0, None, A.is_ge, None, ["PC"], ["PC6"], 1)
-    ts(PC[:, 17:18], cA, 2.0, 65535.0 / 4096, A.is_ge, A.mult, ["PC"], ["PC17"], 1)
-    tt(PC[:, 7:8], PC[:, 17:18], PC[:, 5:6], A.mult, ["PC17", "PC5"], ["PC7"], 1)
-    ts(PC[:, 8:9], cA, 0.0, None, A.is_equal, None, ["PC"], ["PC8"], 1)
-    ts(PC[:, 9:10], cA, 1.0, None, A.is_equal, None, ["PC"], ["PC9"], 1)
+    ts(PC[:, 17:18], cA, 2.0, (65535.0 - MID) / 4096, A.is_ge, A.mult, ["PC"], ["PC17"], 1)
+    ts(PC[:, 7:8], PC[:, 17:18], PC[:, 5:6], MID, A.mult, A.add, ["PC17", "PC5"], ["PC7"], 1)
+    ts(PC[:, 14:15], PC[:, 5:6], MID - 129.0 * 4096 - 2.0 ** 21, None, A.add, None, ["PC5"], ["PC14"], 1)
+    ts(PC[:, 16:17], PC[:, 14:15], -1.0, 65535.0, A.mult, A.add, ["PC14"], ["PC16"], 1)
+    ts(T.IS6[:, 0:128], T.IB[:], PC[:, 6:7], None, A.mult, None, ["IB", "PC6"], ["IS6"], 128, .5)
+    for k in range(2):
+        ts(PC[:, 29 + k:30 + k], cA, float(k), None, A.is_equal, None, ["PC"], ["PC%d" % (29 + k)], 1)
+        ts(T.IS6[:, 128 + 128 * k:256 + 128 * k], T.IB[:], PC[:, 29 + k:30 + k], None, A.mult, None, ["IB", "PC%d" % (29 + k)], ["IS6%d" % k], 128, .5)
+    ts(PC[:, 8:9], cP, 0.0, -129.0 * 4096, A.is_equal, A.mult, ["PC"], ["PC8"], 1)
+    ts(PC[:, 13:14], cP, 1.0, MID, A.is_equal, A.mult, ["PC"], ["PC13"], 1)
+    ts(T.CC[:], T.ZR[:], PC[:, 8:9], PC[:, 13:14], A.add, A.add, ["ZR", "PC13", "PC8"], ["CC0"], 128, .5)
     ts(PC[:, 18:19], cA, -LN2, LN2 * (11 - 108 - 1548), A.mult, A.add, ["PC"], ["PC18"], 1)
     ts(PC[:, 10:11], PC[:, 6:7], -400.0, PC[:, 18:19], A.mult, A.add, ["PC6", "PC18"], ["PC10"], 1)
     ts(PC[:, 19:20], cA, -LN2, LN2 * 107, A.mult, A.add, ["PC"], ["PC19"], 1)
@@ -190,87 +246,94 @@ def build(T, topo, rank, core):
         ts(PC[:, 21 + c:22 + c], cP, -lr, 118 * LN2 - lr * 128 * (c % 2), A.mult, A.add, ["PC"], ["PC%d" % (21 + c)], 1)
     act(PC[:, 24:28], PC[:, 20:24], F.Exp, ["PC20", "PC21", "PC22", "PC23"], ["PCe"], 1300)
     cZ, cW = PC[:, 24:25], [PC[:, 25 + c:26 + c] for c in range(3)]
-    ts(PC[:, 12:13], cO, float(HB), None, A.mult, None, ["PC"], ["PC12"], 1)
-    ts(T.CM[:], T.IB[:], 2.0, None, A.mult, None, ["IB", "CM"], ["CM"], 128)
-    tt(T.ZM[:, 0:128], T.CM[:], T.SGM[:], A.subtract, ["CM", "SGM"], ["ZM0"], 128)
-    ts(T.ZM[:, 128:256], T.ZM[:, 0:128], cZ, None, A.mult, None, ["ZM0", "PCe"], ["ZM1"], 128)
-    ms(T.THR[:, 48:64], 0.0, ["THRx"], 16)
-    for c in range(3):
-        ts(T.THR[:, c:48:3], T.ON[:, 0:16], cW[c], 2.5, A.mult, A.mult, ["ON", "PCe"], ["THR%d" % c], 16)
-        ts(T.DS[:, c:24:3], T.ON[:, 0:8], cP, 480.0 + 128 * c, A.mult, A.add, ["ON", "PC"], ["DS%d" % c], 8)
-    ts(T.CT[:, 16:64], T.CI[:, 0:48], 16.0, float(GW), A.mult, A.add, ["CI"], ["CT1"], 48)
-    ts(T.DUM[:], T.CT[:, 16:64], cA, None, A.add, None, ["CT1", "PC"], ["DUM"], 48)
-    ts(T.CT[:, 0:7], T.CI[:, 0:112:16], cA, None, A.add, None, ["CI", "PC", "CT0"], ["CT0"], 7)
-    ts(T.CTI[:, 0:7], T.CT[:, 0:7], 1.0 / 7, -3.0 / 7, A.mult, A.add, ["CT0"], ["CTI"], 7)
-    ts(T.CT[:, 8:15], T.CTI[:, 0:7], -223.0 / 32, None, A.mult, None, ["CTI", "CT0"], ["CT2"], 7)
-    tt(T.CT[:, 8:15], T.CT[:, 8:15], T.CT[:, 0:7], A.add, ["CT2", "CT0"], ["CT2"], 7)
-    ts(T.PL[:, 0:7], T.CT[:, 8:15], 32.0, None, A.mult, None, ["CT2"], ["PLa"], 7)
-    ts(T.PL[:, 7:14], T.CT[:, 8:15], 32.0, 16.0, A.mult, A.add, ["CT2"], ["PLb"], 7)
-    ms(T.CP[:, 208:864], 0.0, ["CPb"], 656)
+    ts(T.IS[:, 0:128], T.IB[:], 2.0, None, A.mult, None, ["IB"], ["IS"], 128)
+    tt(T.ZM[:, 0:128], T.IS[:, 0:128], T.SGM[:], A.subtract, ["IS", "SGM"], ["ZM0"], 128)
+    ts(PC[:, 9:10], cO, float(HB), -0.46875, A.mult, A.add, ["PC"], ["PC9"], 1)
+    ts(PC[:, 11:12], PC[:, 9:10], 252.0, None, A.add, None, ["PC9"], ["PC11"], 1)
     ms(T.TS[:, 324:336], 0.0, ["TSd"], 8)
-    for b, nm, v in ((T.EB, "EB", 65535.0), (T.UV, "UV", 65535.0), (T.WB, "WB", 0.0), (T.XE, "XE", 0.0)):
-        ms(b[:, S:400], v, [nm + "d"], 16)
-        if nm in ("UV", "XE"):
-            ms(b[:, 400 + S:800], v, [nm + "e"], 16)
+    ts(T.ZM[:, 128:256], T.ZM[:, 0:128], cZ, None, A.mult, None, ["ZM0", "PCe"], ["ZM1"], 128)
+    ts(T.CT[:, 16:64], T.CI[:, 0:48], 16.0, cA, A.mult, A.add, CP_, ["CT1"], 48)
+    ts(T.DUM[:], T.CT[:, 16:64], GW - MID, None, A.add, None, ["CT1"], ["DUM"], 48)
+    for t in range(NT):
+        ts(T.DS[:, 24 * t:24 * t + 24], T.CT[:, 16:40], L + CN * t - MID - 768, None, A.add, None, ["CT1"], ["DS%d" % t], 24)
+    ts(T.THR[:, 24:40], T.CT[:, 16:32], -lr, 118 * LN2 + math.log(2.5), A.mult, A.add, ["CT1"], ["THRa"], 16)
+    cp(T.THR[:, 40:48], T.THR[:, 24:32], ["THRa"], ["THRb"], 8)
+    act(T.THR[:, 0:24], T.THR[:, 24:48], F.Exp, ["THRa", "THRb"], ["THR0"], 24)
+    cp(T.THR[:, 24:48], T.THR[:, 0:24], ["THR0"], ["THRa", "THRb"], 24)
+    ts(T.PI[:, 8:15], T.CT[:, 16:23], 1.0 / 7, -3.0 / 7, A.mult, A.add, ["CT1"], ["CTI"], 7)
+    ts(T.CT[:, 8:15], T.PI[:, 8:15], -111.0 / 16, None, A.mult, None, ["CTI", "CT0"], ["CT0"], 7)
+    tt(T.CT[:, 8:15], T.CT[:, 8:15], T.CT[:, 16:23], A.add, ["CT1", "CT0"], ["CT0"], 7)
+    ts(T.PL[:, 0:7], T.CT[:, 8:15], 16.0, None, A.mult, None, ["CT0"], ["PLa"], 7)
+    ts(PC[:, 12:13], cA, 7.0, None, A.mult, None, ["PC"], ["PC12"], 1)
+    ts(T.PL[:, 8:15], T.CI[:, 0:7], PC[:, 12:13], None, A.add, None, ["CI", "PC12"], ["PLb"], 7)
+    ts(PC[:, 31:32], PC[:, 29:30], 256.0 * MID, 2.0 ** 20, A.mult, A.add, ["PC29"], ["PC31"], 1)
+    for k in range(2):
+        ts(T.D16[:, 128 * k:128 * k + 128], T.IS6[:, 128 + 128 * k:256 + 128 * k], 256.0, None, A.mult, None, ["IS6%d" % k], ["D16%d" % k], 128, .5)
+    sel(T.IO6[:], T.IOT[:, 0:S], [[0, S]], 0, ["IOT"], ["IO6"], S)
     cp(PC[:, 28:29], T.THI[:, 0:1], ["THI"], ["PC28"], 1)
-    ts(T.THB[:], T.ON[:], PC[:, 28:29], -3.0, A.mult, A.add, ["ON", "PC28"], ["THB"], 128)
-    mm(P[4][:, 0:8], T.THB[:], T.R32[:], True, True, ["THB", "R32"], ["dl4"], 128, 8, 4, 4)
-    cp(T.TH8[:], P[4][:, 0:8], ["dl4"], ["TH8"], 8, pb=[4])
+    ts(T.THB[:], T.ON[:, 0:128], PC[:, 28:29], -3.09375, A.mult, A.add, ["ON", "PC28"], ["THB"], 128)
+    mm(P[7][:, 0:24], T.THB[:], T.R32[:], True, True, ["THB", "R32"], ["p7"], 128, 24, 7, 4)
+    cp(T.THK[:], P[7][:, 0:24], ["p7"], ["THK"], 24, pb=[7])
+    early = [k for k, o in enumerate(ops) if o["e"] == "v" and not set(o["w"]) & {"PC28", "THB", "THK", "ZM1", "THRa"}]
+    op("v", lambda q: q.tensor_copy(T.LE[:], T.EN[:]), ["EN"], ["LE%d%d" % (t, c) for t in range(NT) for c in range(3)], vc(72), after=early)
+    def spread(t, c, eng):
+        na = max(row[c] for row in NA)
+        lo, hi = 128 * c + 128 - na, 128 * c + 128
+        for i in range(16 if na else 0):
+            o, src = T.XR[:, XW * t + 16 * (lo - XLO) + i:XW * t + 16 * (hi - XLO):16], T.X[:, 400 * t + lo:400 * t + hi]
+            if eng == "v":
+                cp(o, src, [XN_[t][c]], ["XR%d%d_%d" % (t, c, i)], na, .5)
+            else:
+                sel(o, src, [[0, na]], 0, [XN_[t][c]], ["XR%d%d_%d" % (t, c, i)], na)
+    for t in range(NT):
+        for c in range(3 if t == 0 else 2):
+            spread(t, c, "v" if t == 0 else "g")
     for t in (1, 2):
-        o = 224 * (t - 1)
-        act(T.OWN[:, o:o + XN], T.X[:, 400 * t + 272:400 * t + S], ID, ["X%d2" % t], ["OWx%d" % t], XN)
-        act(T.TA[:], T.IOT[:].indirect(T.LE[:, 24 * t + 16:24 * t + 24]), ID, ["IOT", "LE%d2" % t], ["TA0"], 128, ga=True)
-        act(T.OWN[:, o + XN:o + 224], T.TA[:, 16:128], ID, ["TA0"], ["OWe%d" % t], XN)
+        o = XN * (t - 1)
+        act(T.TA[:], T.IOT[:].indirect(T.LE[:, 24 * t + 16:24 * t + 24]), ID, ["IOT", "LE%d2" % t], ["TA0"], 128, scale=256.0, ga=True)
+        tt(T.OWN[:, o:o + XN], T.TA[:, 16:128], T.X[:, 400 * t + 272:400 * t + S], A.add, ["TA0", "X%d2" % t], ["OWN%d" % t], XN)
 
     send = [None, None]
+    turn = [0]
     for t in range(NT):
         last = t == NT - 1
         n0 = L + CN * t
         xo = 400 * t
         if t > 0:
-            o = 224 * (t - 1)
+            o = XN * (t - 1)
             op("x", None, [], ["LND%d" % t], 6000, kind="x%d" % (t - 1), after=[send[t - 1]])
-            tt(T.MX[:], T.LND[:, o:o + 224].indirect(T.PL[:, 0:14]), T.OWN[:, o:o + 224], A.max,
-               ["LND%d" % t, "PLa", "PLb", "OWx%d" % t, "OWe%d" % t], ["MX"], 224, ga=True)
-            ts(T.MY[:], T.MX[:], 4095, None, A.bitwise_and, None, ["MX"], ["MY"], 224)
-            cp(T.X[:, xo + 272:xo + S], T.MY[:, 0:XN], ["MY"], ["X%d2" % t], XN)
-            ts(T.E16[:], T.MY[:, XN:224], -1312.0, None, A.add, None, ["MY"], ["E16"], XN)
+            tt(T.MX[:], T.LND[:, o:o + XN].indirect(T.PL[:, 0:7]), T.OWN[:, o:o + XN], A.max, ["LND%d" % t, "PLa", "OWN%d" % t], ["MX"], XN, ga=True)
+            ts(T.MY[:, XN:224], T.MX[:], 8, 4095, A.arith_shift_right, A.bitwise_and, ["MX"], ["MYe"], XN)
+            ts(T.E16[:], T.MY[:, XN:224], -MID, None, A.add, None, ["MYe"], ["E16"], XN)
+            ts(T.MY[:, 0:XN], T.MX[:], 255, None, A.bitwise_and, None, ["MX"], ["MYx"], XN)
+            cp(T.X[:, xo + 272:xo + S], T.MY[:, 0:XN], ["MYx"], ["X%d2" % t], XN)
             for a in range(16):
-                mm(P[3][:, 288:295], T.DG[:, 128 * a:128 * a + 128], T.E16[:, a:XN:16], a == 0, a == 15, ["DG%d" % a, "E16"], ["k2e"], 128, 7, 3)
-            ts(T.LE[:, 24 * t + 17:24 * t + 24], P[3][:, 288:295], 1312.0, None, A.add, None, ["k2e"], ["LE%d2" % t], 7, pb=[3])
+                mm(P[3][:, 304:311], SH[a], T.E16[:, a:XN:16], a == 0, a == 15, ["SH", "E16"], ["k2e"], 128, 7, 3)
+            ts(T.LE[:, 24 * t + 17:24 * t + 24], P[3][:, 304:311], MID, None, A.add, None, ["k2e"], ["LE%d2" % t], 7, pb=[3])
+            spread(t, 2, "v")
         if last:
             for k in range(4):
-                cp(T.NF[:, 652 * k:652 * k + 652], T.NB[:, 652 * k:652 * k + 652], NBR, ["NF%d" % k], 652)
-        xb = [0, 0, 7]
-        xp = [P[0][:, 0:128], P[0][:, 128:256], P[7][:, 0:128]]
+                sel(T.NF[:, 652 * k:652 * k + 652], T.NB[:, 652 * k:652 * k + 652], [[0, 652]], 0, NBR, ["NF%d" % k], 652)
         for c in range(3):
             C = str(c)
             cs = slice(128 * c, 128 * c + 128)
             K, kb = P[1 + c], 1 + c
-            xc, xn = T.X[:, xo + 128 * c:xo + 128 * c + 128], "X%d%d" % (t, c)
+            xc, xn = T.X[:, xo + 128 * c:xo + 128 * c + 128], XN_[t][c]
             le, ln = T.LE[:, 24 * t + 8 * c:24 * t + 8 * c + 8], "LE%d%d" % (t, c)
             bias[0] = BINIT
-            if c == 0:
-                mm(P[0][:, 0:256], T.IB[:], T.X[:, xo:xo + 256], True, True, ["IB", xn, "X%d1" % t], ["xp0", "xp1"], 128, 256, 0)
-            if c == 2:
-                mm(xp[c], T.IB[:], xc, True, True, ["IB", xn], ["xp2"], 128, 128, xb[c])
-            act(T.ID0[:, cs], T.IOT[:].indirect(le), ID, ["IOT", ln], ["ID0" + C], 128, bias=-1312.0, ga=True)
-            act(T.BH0[:, cs], T.ID0[:, cs], ID, ["ID0" + C], ["BH0" + C], 128, bias=8256.0 + 1312.0)
+            if any(NE[h][c] < 16 and NA[h][c] < 128 for h in range(4)):
+                mm(P[6][:, cs], T.IB[:], xc, True, True, ["IB", xn], ["xp" + C, "p6"], 128, 128, 6)
+            act(T.ID0[:, cs], T.IOT[:].indirect(le), ID, ["IOT", ln], ["ID0" + C], 128, bias=-MID, ga=True)
+            act(T.BH0[:, cs], T.ID0[:, cs], ID, ["ID0" + C], ["BH0" + C], 128, bias=8224.5 + MID)
             act(T.G0[:, cs], T.W[:, 0:GW].indirect(le), ID, WR + [ln], ["G0" + C], 128, ga=True)
-            tt(T.M0[:, cs], T.G0[:, cs], xp[c], A.min, ["G0" + C, "xp" + C], ["M0" + C], 128, pb=[xb[c]])
-            mm(K[:, 280:288], xc, T.RC[:, 0:8], True, True, [xn, "RC0"], ["ks" + C], 128, 8, kb)
-            mm(K[:, 264:280], T.BH0[:, cs], T.RC[:, 48:64], True, False, ["BH0" + C, "RC48", "RC56"], ["ki" + C], 128, 16, kb)
-            mm(K[:, 264:280], T.ID0[:, cs], T.RA[:], False, False, ["ID0" + C, "RA0", "RA1"], ["ki" + C], 128, 16, kb, 4)
-            mm(K[:, 264:280], T.G0[:, cs], T.RC[:, 0:16], False, False, ["G0" + C, "RC0", "RC8"], ["ki" + C], 128, 16, kb)
-            mm(K[:, 264:280], T.M0[:, cs], T.RC[:, 16:32], False, True, ["M0" + C, "RC16", "RC24"], ["ki" + C], 128, 16, kb)
-            k16 = slice(16 * c, 16 * c + 16)
-            cp(T.KM[:, k16], K[:, 264:280], ["ki" + C], ["KM" + C], 16, pb=[kb])
-            tt(T.THK[:, 8 * c:8 * c + 8], T.TH8[:], K[:, 280:288], A.subtract, ["TH8", "ks" + C], ["THK" + C], 8, pb=[kb])
-            ts(T.CUR[:, k16], T.KM[:, k16], -3969, None, A.bitwise_and, None, ["KM" + C], ["CUR" + C], 16)
+            mm(K[:, 384:512], T.IB[:], T.G0[:, cs], True, False, ["IB", "G0" + C], ["kd" + C], 128, 128, kb)
+            mm(K[:, 384:512], T.NI[:, 0:128], xc, False, True, ["NI0", xn], ["kd" + C], 128, 128, kb)
+            act(T.M0[:, cs], K[:, 384:512], F.Abs, ["kd" + C], ["M0" + C], 128, pb=[kb])
             bias[0] = 0.0
-            if not last:
-                act(T.XE[:, cs], xc, ID, [xn], ["XEx" + C], 128, bias=4096.0)
-                act(T.XE[:, 400 + 128 * c:528 + 128 * c], T.ID0[:, cs], ID, ["ID0" + C], ["XEe" + C], 128, bias=4096.0 + 1312.0)
+        for k, (a, b, nm) in enumerate(((T.IB[:], T.X[:, xo:xo + S], ["IB"] + XN_[t]), (T.D16[:, 0:128], T.ID0[:], ["D160", "ID00", "ID01", "ID02"]),
+                                        (T.D16[:, 128:256], T.IO6[:], ["D161", "IO6"]))):
+            mm(P[7][:, 0:S], a, b, k == 0, k == 2, nm, ["p7"], 128, S, 7)
+        act(T.XE[:], P[7][:, 0:S], ID, ["p7", "PC31"], ["XE"], S, bias=PC[:, 31:32], pb=[7])
         for h in range(4):
             for c in range(3):
                 bias[0] = STAG[c]
@@ -278,7 +341,7 @@ def build(T, topo, rank, core):
                 k16 = slice(16 * c, 16 * c + 16)
                 K, kb = P[1 + c], 1 + c
                 C = str(c)
-                xc, xn = T.X[:, xo + 128 * c:xo + 128 * c + 128], "X%d%d" % (t, c)
+                xn = XN_[t][c]
                 if h == 0:
                     li, ln = T.LE[:, 24 * t + 8 * c:24 * t + 8 * c + 8], "LE%d%d" % (t, c)
                 elif h < 3:
@@ -291,203 +354,273 @@ def build(T, topo, rank, core):
                     lo, lon = T.LUV[:, 24 * (h - 2) + 8 * c:24 * (h - 2) + 8 * c + 8], "LU%d%d" % (h - 2, c)
                 ts(T.I32[:, cs], T.NB[:, 0:GW].indirect(li), 4095, None, A.bitwise_and, None, NBR + [ln], ["I32" + C], 128, ga=True)
                 ts(T.O16[:, cs], T.I32[:, cs], float(PU), None, A.min, None, ["I32" + C], ["O16" + C], 128)
+                ts(T.BH[:, cs], T.O16[:, cs], 8224.5, None, A.add, None, ["O16" + C], ["BH" + C], 128, .5)
+                ts(T.A16[:, cs], T.O16[:, cs], -MID, None, A.add, None, ["O16" + C], ["A16" + C], 128, .5)
                 go = 2048 * c
-                act(T.G[:, go:go + 2048], T.W[:, 0:GW].indirect(T.O16[:, cs]), ID, WR + ["O16" + C], ["G" + C], 2048, ga=True)
-                ts(T.BH[:, cs], T.O16[:, cs], 8256.0, None, A.add, None, ["O16" + C], ["BH" + C], 128, .5)
-                ts(T.A16[:, cs], T.O16[:, cs], -1312.0, None, A.add, None, ["O16" + C], ["A16" + C], 128, .5)
-                mm(K[:, 0:256], T.BH[:, cs], T.NI[:], True, False, ["BH" + C, "NI0", "NI1"], ["k" + C], 128, 256, kb)
-                mm(K[:, 0:128], T.A16[:, cs], T.I16[:], False, False, ["A16" + C, "I16"], ["k" + C], 128, 128, kb)
-                nv, db = 16 - NE, 4 + (3 * h + c) % 2
-                for i in range(nv, 16):
-                    o = P[db][:, 128 * (i - nv):128 * (i - nv) + 128]
-                    mm(o, T.IB[:], T.G[:, go + i:go + 2048:16], True, False, ["IB", "G" + C], ["dl%d" % db], 128, 128, db)
-                    mm(o, T.NI[:, 0:128], xc, False, True, ["NI0", xn], ["dl%d" % db], 128, 128, db)
-                    mm(K[:, i:256:16], xc, T.RC[:, 64:80], False, False, [xn, "RC64", "RC72"], ["k" + C], 128, 16, kb)
-                act(T.M[:, go + 128 * nv:go + 2048], P[db][:, 0:128 * NE], F.Abs, ["dl%d" % db], ["M%d_%d" % (c, i) for i in range(nv, 16)], 128 * NE, pb=[db])
-                for i in range(nv):
-                    tt(T.M[:, go + 128 * i:go + 128 * i + 128], T.G[:, go + i:go + 2048:16], xp[c], A.min,
-                       ["G" + C, "xp" + C], ["M%d_%d" % (c, i)], 128, pb=[xb[c]])
-                for i in range(nv):
-                    mm(K[:, i:256:16], T.G[:, go + i:go + 2048:16], T.RC[:, 0:16], False, False, ["G" + C, "RC0", "RC8"], ["k" + C], 128, 16, kb)
-                for i in range(16):
-                    mm(K[:, i:256:16], T.M[:, go + 128 * i:go + 128 * i + 128], T.RC[:, 16:32] if i < nv else T.RC[:, 0:16], False, i == 15,
-                       ["M%d_%d" % (c, i), "RC0", "RC8", "RC16", "RC24"], ["k" + C], 128, 16, kb)
-                sc = T.SC[:, 256 * c:256 * c + 256]
-                op("v", lambda q, sc=sc, K=K: q.tensor_tensor_scan(sc, T.D0[:], K[:, 0:256], 0.0, A.add, A.min),
-                   ["D0", "k" + C], ["SC" + C], vc(256), [kb])
-                ends = T.SC[:, 256 * c + 15:256 * c + 256:16]
-                if h < 3:
-                    tt(T.KM[:, k16], ends, T.CUR[:, k16], A.min, ["SC" + C, "CUR" + C], ["KM" + C], 16)
-                else:
-                    cp(T.KM[:, k16], ends, ["SC" + C], ["KM" + C], 16)
-                FB, fn, uv = (T.FH, "FH" + C, h) if h < 2 else (T.FU, "FU" + C, h - 2)
-                if t == 0 and uv == 0:
-                    ms(FB[:, 32 * c + 1:32 * c + 32:2], 0, [fn + "1"], 16)
-                ts(FB[:, 32 * c + uv:32 * c + 32:2], T.KM[:, k16], 127, None, A.bitwise_and, None, ["KM" + C], [fn + str(uv)], 16)
-                if h < 3:
-                    ts(T.CUR[:, k16], T.KM[:, k16], -3969, None, A.bitwise_and, None, ["KM" + C], ["CUR" + C], 16)
-                tt(T.EX[:, cs], FB[:, 32 * c:32 * c + 32].indirect(T.XL[:, 12 + 8 * uv:20 + 8 * uv]), T.MK[:], A.mult,
-                   [fn + "0", fn + "1", "XLb", "XLc", "MK0", "MK1"], ["EX" + C], 128, ga=True)
+                nb = 128 - NA[h][c]
+                gn = lambda a, b: ["G%d_%d" % (c, k) for k in range(a // 32, (b + 31) // 32)]
+                mall = ["M%d_%d" % (c, k) for k in range(16)]
+                bp = BP_ if nb % BP_ == 0 else nb
+                ne = NE[h][c] if nb else 16
+                rs = 8 if bp <= 64 and ne % 8 == 0 else 4
+                mslot = lambda i: T.M[:, go + rs * nb * (i // rs) + i % rs:go + rs * nb * (i // rs + 1):rs]
+                mname = lambda i: mall[rs * nb * (i // rs) // 128:(rs * nb * (i // rs + 1) + 127) // 128]
+                for a0 in range(0, nb, bp):
+                    a1 = a0 + bp
+                    ns = a1 - a0
+                    act(T.G[:, go + 16 * a0:go + 16 * a1], T.W[:, 0:GW].indirect(T.O16[:, 128 * c + a0:128 * c + a1]), ID,
+                        WR + ["O16" + C], gn(a0, a1), 16 * ns, ga=True)
+                    for q in range(ne // rs):
+                        db = 4 + turn[0] % ND
+                        turn[0] += 1
+                        for r in range(rs):
+                            o = P[db][:, r:rs * ns:rs]
+                            mm(o, T.IB[:], T.G[:, go + 16 * a0 + rs * q + r:go + 16 * a1:16], True, False, ["IB"] + gn(a0, a1), ["p%d" % db], 128, ns, db)
+                            mm(o, T.NI[:, 0:128], T.X[:, xo + 128 * c + a0:xo + 128 * c + a1], False, True, ["NI0", xn], ["p%d" % db], 128, ns, db)
+                        mo = go + rs * nb * q + rs * a0
+                        nm = mall[(mo - go) // 128:(mo - go + rs * ns + 127) // 128]
+                        act(T.M[:, mo:mo + rs * ns], P[db][:, 0:rs * ns], F.Abs, ["p%d" % db], nm, rs * ns, pb=[db])
+                for i in range(ne, 16):
+                    tt(mslot(i), T.G[:, go + i:go + 16 * nb:16], P[6][:, 128 * c:128 * c + nb], A.min, gn(0, nb) + ["xp" + C],
+                       ["m%d%d%d_%d" % (t, h, c, i)], nb, pb=[6])
+                for a0 in range(nb, 128, AP_):
+                    a1 = min(128, a0 + AP_)
+                    r_ = slice(go + 16 * a0, go + 16 * a1)
+                    xr = XW * t + 16 * (128 * c - XLO)
+                    tt(T.G[:, r_], T.W[:, 0:GW].indirect(T.O16[:, 128 * c + a0:128 * c + a1]), T.XR[:, xr + 16 * a0:xr + 16 * a1], A.subtract,
+                       WR + ["O16" + C] + ["XR%d%d_%d" % (t, c, i) for i in range(16)], gn(a0, a1), 16 * (a1 - a0), ga=True)
+                    ts(T.M[:, r_], T.G[:, r_], 0.0, None, A.min, None, gn(a0, a1), mall[a0 // 8:a1 // 8], 16 * (a1 - a0), .5)
+                kn = ["k" + C]
+                cuf = T.FAR[:, 24 + 16 * c:40 + 16 * c]
+                mm(K[:, 0:272], T.BH[:, cs], T.NI[:, 128:400], True, False, ["BH" + C, "NI1", "NI2"], kn, 128, 272, kb)
+                mm(K[:, 0:136], T.A16[:, cs], T.I16[:, 384:520], False, False, ["A16" + C, "I19"], kn, 128, 136, kb)
+                if h == 0:
+                    mm(K[:, 0:272:17], T.BH0[:, cs], T.RC[:, 32:48], False, False, ["BH0" + C, "RC32", "RC40"], kn, 128, 16, kb)
+                    mm(K[:, 0:272:17], T.ID0[:, cs], T.RA[:], False, False, ["ID0" + C, "RA0", "RA1"], kn, 128, 16, kb)
+                    mm(K[:, 0:272:17], T.M0[:, cs], R1, False, False, ["M0" + C] + R1N, kn, 128, 16, kb)
+                elif h < 3:
+                    mm(K[:, 0:272:17], T.IF[:], cuf, False, False, ["IF", "CUF" + C], kn, 128, 16, kb, 4)
+                sums = []
+                if nb < 128:
+                    sums += [(K[nb:128, 1 + i:272:17], T.G[:, go + 16 * nb + i:go + 2048:16], R1, gn(nb, 128) + R1N, 128 - nb, 16) for i in range(16)]
+                    sums += [(K[nb:128, 1 + i:272:17], T.M[:, go + 16 * nb + i:go + 2048:16], R2, mall[nb // 8:16] + R2N, 128 - nb, 16) for i in range(16)]
+                sums += [(K[0:nb, 1 + i:272:17], T.G[:, go + i:go + 16 * nb:16], R1, gn(0, nb) + R1N, nb, 16) for i in range(ne, 16)]
+                if nb > 0:
+                    sums += [(K[0:nb, 1 + i:272:17], mslot(i), R1, mname(i) + R1N, nb, 16) for i in range(ne)]
+                    sums += [(K[0:nb, 1 + i:272:17], mslot(i), R2, ["m%d%d%d_%d" % (t, h, c, i)] + R2N, nb, 16) for i in range(ne, 16)]
+                if ne < 16:
+                    sums.append((K[0:nb, 0:272], T.X[:, xo + 128 * c:xo + 128 * c + nb], RX[ne], [xn, "RX%d_0" % ne, "RX%d_136" % ne], nb, 272))
+                if 0 < nb < 128:
+                    sums.append((K[:, 0:16], T.ZR[:], T.ON[:, 0:16], ["ZR", "ON"], 128, 16))
+                for k, (o, a, b, nm, m_, n_) in enumerate(sums):
+                    mm(o, a, b, False, k == len(sums) - 1, nm, kn, m_, n_, kb)
+                d0 = 272 * (h // 3)
+                scan(T.SC[:, 272 * c:272 * c + 272], T.D0[:, d0:d0 + 272], K[:, 0:272], 0.0, A.add, A.min, ["D0"] + kn, ["SC" + C], 272, [kb])
+                ends = T.SC[:, 272 * c + 16:272 * c + 272:17]
+                ts(T.FH[:, k16], ends, 63, None, A.bitwise_and, None, ["SC" + C], ["FH" + C], 16)
+                if h < 2:
+                    cp(cuf, ends, ["SC" + C], ["CUF" + C], 16)
+                elif h == 2:
+                    cp(T.CUR[:, c:48:3], ends, ["SC" + C], ["CUR" + C], 16)
+                tt(T.EX[:, cs], T.FH[:, k16].indirect(T.XL[:, 0:8]), T.MK24[:, 192:320], A.mult, ["FH" + C, "XLa", "MK0", "MK1"], ["EX" + C], 128, ga=True)
                 for j in range(16):
-                    mm(K[:, 256:264], T.LG[:, 128 * (j % 8):128 * (j % 8) + 128], T.EX[:, 128 * c + 8 * j:128 * c + 8 * j + 8], j == 0, j == 15,
-                       ["LG%d" % (j % 8), "EX" + C], ["kl" + C], 128, 8, kb)
-                ts(lo, K[:, 256:264], 8096.0, None, A.add, None, ["kl" + C], [lon], 8, pb=[kb])
+                    mm(K[:, 280:288], LG[j % 8], T.EX[:, 128 * c + 8 * j:128 * c + 8 * j + 8], j == 0, j == 15, ["LG", "EX" + C], ["kl" + C], 128, 8, kb)
+                ts(lo, K[:, 280:288], 4032.0, None, A.add, None, ["kl" + C], [lon], 8, pb=[kb])
+                if h == 3 and c == 2:
+                    ts(T.LI[:, 40:48], K[:, 280:288], 1.0 / 16, PC[:, 11:12], A.mult, A.add, ["kl" + C, "PC11"], ["LI12"], 8, pb=[kb])
         bias[0] = 0.0
-        for tb, pbk in ((0, 6), (1, 7)):
-            mm(P[pbk][:, 128:452], T.ZR[:], T.SI[:, 0:324], True, False, ["ZR", "SI0", "SI1", "SI2"], ["tb%d" % tb], 128, 324, pbk)
+        LN = [["LU%d%d" % (u, c) for c in range(3)] for u in range(2)]
+        CURN, A16N = ["CUR0", "CUR1", "CUR2"], ["A160", "A161", "A162"]
+        lu = [T.LUV[:, 0:24], T.LUV[:, 24:48]]
+        bs = [slice(0, S), slice(S, 2 * S)]
+        xb = T.X[:, xo:xo + S]
+        CL = T.CL
+        nbad, farl, want, cs1, rest, cs2 = CL[:, 0:48], CL[:, 48:72], CL[:, 72:96], CL[:, 96:120], CL[:, 120:144], CL[:, 144:168]
+        tt(T.FAR[:, 0:24], T.CUR[:, 0:24], T.THK[:], A.is_ge, CURN + ["THK"], ["FAR"], 24)
+        tt(T.EXP[:], T.FAR[:, 0:24].indirect(T.XL[:, 0:12]), T.MK24[:, 0:192], A.mult, ["FAR", "XLa", "MK24"], ["EXP"], 192, ga=True)
+        for gg in range(8):
+            mm(P[7][:, 400:424], LG[gg], T.EXP[:, 24 * gg:24 * gg + 24], gg == 0, gg == 7, ["LG", "EXP"], ["p7f"], 128, 24, 7)
+        cp(farl, P[7][:, 400:424], ["p7f"], ["farl"], 24, pb=[7])
+        off = n0 - MID - 768
+        kfo = T.LSA[:, 168:192]
+        if not last:
+            scan(cs2, T.ON[:, 0:24], farl, 0.0, A.mult, A.add, ["ON", "farl"], ["cs2"], 24)
+            mm(P[7][:, 424:448], T.TB[:, 128:256], farl, True, False, ["TB1", "farl"], ["p7g"], 128, 24, 7)
+            mm(P[7][:, 424:448], T.SG6[:], cs2, False, True, ["SG6", "cs2"], ["p7g"], 128, 24, 7)
+            act(kfo, P[7][:, 424:448], ID, ["p7g"], ["kfo"], 24, bias=S + off - 4097 - 2048, pb=[7])
+
+        def sides(u, pk):
+            U = str(u)
+            late = [LATE[0:1], LATE[1:2], LATE[2:3]] if u else [[], [], []]
+            if EBS:
+                act(T.EB[:, bs[u]], T.NB[:, 0:GW].indirect(lu[u]), ID, NBR + LN[u] + late[0], ["EB" + U], S, ga=True)
+            else:
+                cp(T.EB[:, bs[u]], T.NB[:, 0:GW].indirect(lu[u]), NBR + LN[u], ["EB" + U], S, ga=True)
+            act(T.UV[:, bs[u]], T.IOT[:].indirect(lu[u]), ID, ["IOT"] + LN[u] + late[1], ["UV" + U], S, bias=-MID, ga=True)
+            act(T.WB[:, 400 * u:400 * u + S], T.W[:, 0:GW].indirect(lu[u]), ID, WR + LN[u] + late[2], ["WB" + U], S, ga=True)
+            act(T.AGB[:, bs[u]], T.EB[:, bs[u]], ID, ["EB" + U], ["AG" + U], S, bias=128.7, scale=1.0 / 4096)
+            act(T.WT[:, bs[u]], T.AGB[:, bs[u]], F.Exp, ["AG" + U, "PC10"], ["WT" + U], S, bias=PC[:, 10:11], scale=12 * LN2)
+            o, on = P[pk][:, 0:S], ["p%d" % pk]
+            mm(o, T.SI[:, 256 * u:256 * u + 128], T.WB[:, 400 * u:400 * u + S], True, False, ["SI0", "SI2", "WB" + U], on, 128, S, pk)
+            mm(o, T.SI[:, 256 * u + 128:256 * u + 256], xb, False, True, ["SI1", "SI3"] + XN_[t], on, 128, S, pk)
+            if SI32:
+                act(T.WI[:, bs[u]], o, ID, on, ["WI" + U], S, bias=-.375 - .0625 * u, pb=[pk])
+            else:
+                ts(T.WI[:, bs[u]], o, -.375 - .0625 * u, None, A.add, None, on, ["WI" + U], S, pb=[pk])
+
+        def rows(u, c0, c1, pk, po):
+            d = slice(S * u + 128 * c0, S * u + 128 * c1)
+            nm = ["%d%d" % (u, c) for c in range(c0, c1)]
+            act(T.OT[:, d], T.OH[:].indirect(T.LUV[:, 24 * u + 8 * c0:24 * u + 8 * c1]), ID, ["OH"] + LN[u][c0:c1], ["OT" + x for x in nm], 128 * (c1 - c0), ga=True)
+            if pk is None:
+                return
+            for c in range(c0, c1):
+                mm(P[pk][:, 128 * (c - c0):128 * (c - c0) + 128], T.OT[:, S * u + 128 * c:S * u + 128 * c + 128], T.IB[:], True, True,
+                   ["OT%d%d" % (u, c), "IB"], [po], 128, 128, pk)
+            act(T.AW[:, d], P[pk][:, 0:128 * (c1 - c0)], ID, [po], ["AW" + x for x in nm], 128 * (c1 - c0), pb=[pk])
+
+        def weights(u, c):
+            pk = 7 * (c // 2)
+            for gg in range(8):
+                j = 16 * c + 2 * gg + u
+                hf = T.HF[:, 3 * gg + c:3 * gg + c + 1] if u == 0 else T.HF[:, 24 + 8 * c + gg:25 + 8 * c + gg]
+                ts(T.BB[:, HB * j:HB * j + HB], T.I162[:], hf, cW[c], A.is_equal, A.mult, ["I162", "PCe", "HF0" if u == 0 else "HF1%d" % c], ["BB%d" % j], HB, .5)
+                a, o = 32 * (gg // 2), HB * (gg % 2)
+                ao = S * u + 128 * c + a
+                mm(P[pk][a:a + 32, o:o + HB], T.AW[:, ao:ao + 32], T.BB[:, HB * j:HB * j + HB], False, False,
+                   ["AW%d%d" % (u, c), "BB%d" % j], ["p%d" % pk], 32, HB, pk)
+
+        def places(u, c0, c1):
+            a, b, nm = 24 * u + 8 * c0, 24 * u + 8 * c1, "%d%d" % (u, c0)
+            if c0 < 2:
+                ts(T.LI[:, a:b], T.LUV[:, a:b], 1.0 / 16, PC[:, 9:10], A.mult, A.add, LN[u][c0:c1] + ["PC9"], ["LI" + nm], 16)
+            cp(T.LT[:, a:b], T.LI[:, a:b], ["LI" + nm], ["LT" + nm], 16)
+
+        def reads(u, c0, c1, lt):
+            a, b = 24 * u + 8 * c0, 24 * u + 8 * c1
+            d = slice(S * u + 128 * c0, S * u + 128 * c1)
+            win, wn = (T.TS[:, 0:336], ["TS0", "TSd"]) if c0 == 0 else (T.TS[:, 336:660], ["TS1"])
+            tt(T.RR[:, d], win.indirect(T.LT[:, a:b]), T.OT[:, d], A.mult, wn + [lt] + ["OT%d%d" % (u, c) for c in range(c0, c1)],
+               ["RR%d%d" % (u, c0)], 128 * (c1 - c0), ga=True)
+        ts(T.LF[:, 0:24], lu[0], -MID, None, A.add, None, LN[0], ["LF0"], 24)
+        ts(T.LF[:, 48:72], lu[0], -MID, None, A.add, None, LN[0], ["LF2"], 24)
+        ts(T.HT[:, 0:24], T.CUR[:, 0:24], 63, 4, A.bitwise_and, A.arith_shift_right, CURN, ["HTa"], 24)
+        ts(T.HT[:, 24:48], T.CUR[:, 24:48], 63, None, A.bitwise_and, None, CURN, ["HTb"], 24)
+        ts(T.HT[:, 24:48], T.HT[:, 24:48], -4.0, 252.0, A.mult, A.add, ["HTb"], ["HTb"], 24)
+        tt(T.HF[:, 0:24], T.HT[:, 0:24], T.HT[:, 24:48], A.add, ["HTa", "HTb"], ["HF0"], 24)
+        rows(0, 0, 3, 7, "p7")
+        sides(0, 7)
+        act(T.RB[:], T.AGB[:, 0:S], F.Relu, ["AG0"], ["RB"], S, bias=-136.5 * 65536, scale=65536.0)
+        places(0, 0, 3)
+        for pk in (0, 7):
+            mm(P[pk][:, 0:324], T.ZR[:], T.ON[:, 0:324], True, False, ["ZR", "ON"], ["p%d" % pk], 128, 324, pk)
+        for c in range(3):
+            weights(0, c)
         for c in range(3):
             C = str(c)
-            K, kb = P[1 + c], 1 + c
-            cs = slice(128 * c, 128 * c + 128)
-            xc, xn = T.X[:, xo + 128 * c:xo + 128 * c + 128], "X%d%d" % (t, c)
-            lu = [T.LUV[:, 24 * u + 8 * c:24 * u + 8 * c + 8] for u in range(2)]
-            ln = ["LU0" + C, "LU1" + C]
-            US = ["0" + C, "1" + C]
-            bs = [slice(S * u + 128 * c, S * u + 128 * c + 128) for u in range(2)]
-            es = [slice(400 * u + 128 * c, 400 * u + 128 * c + 128) for u in range(2)]
-            tb, pbk = c // 2, 6 + c // 2
-            tt(T.SMA[:, c:24:3], T.CUR[:, 16 * c:16 * c + 8], T.THK[:, 8 * c:8 * c + 8], A.is_ge, ["CUR" + C, "THK" + C], ["far" + C], 8)
-            for u in range(2):
-                U = US[u]
-                ha, hc = slice(16 * c + u, 16 * c + 16, 2), slice(48 + 16 * c + u, 64 + 16 * c, 2)
-                ts(T.HT[:, ha], T.FU[:, 32 * c + u:32 * c + 16:2], 4, None, A.arith_shift_right, None, ["FU%d%d" % (c, u)], ["HTa" + U], 8)
-                ts(T.HT[:, hc], T.FU[:, 32 * c + 16 + u:32 * c + 32:2], -4.0, 506.0, A.mult, A.add, ["FU%d%d" % (c, u)], ["HTb" + U], 8)
-                tt(T.HF[:, ha], T.HT[:, ha], T.HT[:, hc], A.add, ["HTa" + U, "HTb" + U], ["HF" + U], 8)
-                act(T.OT[:, bs[u]], T.OH[:].indirect(lu[u]), ID, OHR + [ln[u]], ["OT" + U], 128, ga=True)
-                mm(P[4 + u][:, cs], T.OT[:, bs[u]], T.IB[:], True, True, ["OT" + U, "IB"], ["dl%d" % (4 + u)], 128, 128, 4 + u)
-                act(T.AW[:, bs[u]], P[4 + u][:, cs], ID, ["dl%d" % (4 + u), "PCe"], ["AW" + U], 128, scale=cW[c], pb=[4 + u])
-                for gg in range(8):
-                    j = 16 * c + 2 * gg + u
-                    ts(T.BB[:, HB * j:HB * j + HB], T.I162[:], T.HF[:, j:j + 1], None, A.is_equal, None, ["I162", "HF" + U], ["BB%d" % j], HB, .5)
-                    a = 32 * (gg // 2)
-                    o = 128 + HB * (gg % 2)
-                    ao = S * u + 128 * c + a
-                    mm(P[pbk][a:a + 32, o:o + HB], T.AW[:, ao:ao + 32], T.BB[:, HB * j:HB * j + HB], False, False,
-                       ["AW" + U, "BB%d" % j], ["tb%d" % tb], 32, HB, pbk)
+            ha, hc = slice(48 + 16 * c, 56 + 16 * c), slice(56 + 16 * c, 64 + 16 * c)
+            ts(T.HT[:, ha], T.FH[:, 16 * c:16 * c + 8], 4, None, A.arith_shift_right, None, ["FH" + C], ["HTc" + C], 8)
+            ts(T.HT[:, hc], T.FH[:, 16 * c + 8:16 * c + 16], -4.0, 252.0, A.mult, A.add, ["FH" + C], ["HTd" + C], 8)
+            tt(T.HF[:, 24 + 8 * c:32 + 8 * c], T.HT[:, ha], T.HT[:, hc], A.add, ["HTc" + C, "HTd" + C], ["HF1" + C], 8)
+            if c in AWV:
+                rows(1, c, c + 1, None, None)
+                ts(T.FH[:, 48 + 8 * c:56 + 8 * c], T.SC[:, 272 * c + 16:272 * c + 136:17], 15, None, A.bitwise_and, None, ["SC" + C], ["L16" + C], 8)
+                tt(T.AW[:, S + 128 * c:S + 128 * c + 128], T.FH[:, 48 + 8 * c:56 + 8 * c].indirect(T.XL[:, 12:20]), T.CM[:], A.is_equal,
+                   ["L16" + C, "XLb", "CM"], ["AW1" + C], 128, ga=True)
+            else:
+                rows(1, c, c + 1, 1 + c, "k" + C)
+            if c == 2:
+                mm(P[7][:, 0:324], T.SJ[:, 512:640], T.TG[:], False, False, ["SJ4", "TG"], ["p7"], 128, 324, 7)
+            weights(1, c)
             if c > 0:
-                mm(P[pbk][:, 128:452], T.ZR[:], T.SI[:, 0:324], False, True, ["ZR", "SI0", "SI1", "SI2"], ["tb%d" % tb], 128, 324, pbk)
-                act(T.TS[:, 336 * tb:336 * tb + 324], P[pbk][:, 128:452], ID, ["tb%d" % tb], ["TS%d" % tb], 324, pb=[pbk])
-            Z = [K[:, 0:128], K[:, 128:256]]
-            Y = [K[:, 256:384], K[:, 384:512]]
-            kz, ky = ["k" + C], ["kl" + C, "ki" + C, "ks" + C] + (["k2e"] if c == 2 else [])
-            for u in range(2):
-                U = US[u]
-                cp(T.EB[:, es[u]], T.NB[:, 0:GW].indirect(lu[u]), NBR + [ln[u]], ["EB" + U], 128, ga=True)
-                act(T.UV[:, es[u]], T.IOT[:].indirect(lu[u]), ID, ["IOT", ln[u]], ["UV" + U], 128, ga=True)
-                act(T.WB[:, es[u]], T.W[:, 0:GW].indirect(lu[u]), ID, WR + [ln[u]], ["WB" + U], 128, ga=True)
-                act(T.AGB[:, bs[u]], T.EB[:, es[u]], ID, ["EB" + U], ["AG" + U], 128, bias=128.7, scale=1.0 / 4096)
-                act(T.WT[:, bs[u]], T.AGB[:, bs[u]], F.Exp, ["AG" + U, "PC10"], ["WT" + U], 128, bias=PC[:, 10:11], scale=12 * LN2)
-            act(T.RB[:, cs], T.EB[:, es[0]], F.Relu, ["EB0" + C], ["RB" + C], 128, bias=-32767.0 * 65536, scale=65536.0)
-            for u in range(2):
-                U = US[u]
-                mm(Y[u], T.IF[:], T.UV[:, es[1 - u]], True, False, ["IF", "UV" + US[1 - u]], ky, 128, 128, kb, 4)
-                mm(Y[u], T.NF32[:], T.EB[:, es[u]], False, False, ["NF32", "EB" + U], ky, 128, 128, kb, 4)
-                mm(Y[u], T.SJ[:, 0:128], T.AGB[:, bs[u]], False, True, ["SJ0", "AG" + U], ky, 128, 128, kb)
-            mm(Z[0], T.IF[:], T.EB[:, es[0]], True, False, ["IF", "EB0" + C], kz, 128, 128, kb, 4)
-            mm(Z[0], T.IB[:], T.RB[:, cs], False, True, ["IB", "RB" + C], kz, 128, 128, kb)
-            for u in range(2):
-                act(T.DA[:, bs[u]], Y[u], F.Abs, ky, ["DA" + US[u]], 128, bias=-129.0 * 4096, pb=[kb])
-            act(T.TR[:, cs], Z[0], F.Relu, kz + ["PC14"], ["TR" + C], 128, bias=PC[:, 14:15], scale=-1.0, pb=[kb])
-            for u in range(2):
-                act(T.MT[:, bs[u]], T.DA[:, bs[u]], F.Relu, ["DA" + US[u]], ["MT" + US[u]], 128, bias=1.0, scale=-1.0)
-            for u in range(2):
-                U = US[u]
-                mm(Z[u], T.ZM[:, 0:128], T.WT[:, bs[u]], True, False, ["ZM0", "WT" + U], kz, 128, 128, kb)
-                mm(Z[u], T.ZM[:, 128:256], T.MT[:, bs[u]], False, True, ["ZM1", "MT" + U], kz, 128, 128, kb)
-                mm(Y[u], T.SJ[:, 256 + 128 * u:384 + 128 * u], T.ON[:], True, False, ["SJ2", "SJ3", "ON"], ky, 128, 128, kb)
-                mm(Y[u], T.SI[:, 256 * u:256 * u + 128], T.WB[:, es[u]], False, False, ["SI0", "SI2", "WB" + U], ky, 128, 128, kb)
-                mm(Y[u], T.SI[:, 256 * u + 128:256 * u + 256], xc, False, True, ["SI1", "SI3", xn], ky, 128, 128, kb)
-            for u in range(2):
-                U = US[u]
-                act(T.SG[:, bs[u]], Z[u], F.Sign, kz, ["SG" + U], 128, pb=[kb])
-                act(T.DA[:, bs[u]], Y[u], ID, ky, ["DA" + U], 128, bias=RND, pb=[kb])
-            for u in range(2):
-                U = US[u]
-                act(T.WI[:, bs[u]], T.DA[:, bs[u]], ID, ["DA" + U], ["WI" + U], 128, bias=-RND)
-                mm(Z[u], T.SI[:, 512:640], T.SG[:, bs[u]], True, False, ["SI4", "SG" + U], kz, 128, 128, kb)
-                if u == 0:
-                    mm(Z[0], T.NI[:, 0:128], T.ON[:], False, False, ["NI0", "ON"], kz, 128, 128, kb)
-                    mm(Z[0], T.NF32[:], T.TR[:, cs], False, True, ["NF32", "TR" + C], kz, 128, 128, kb, 4)
+                pk = 7 * (c - 1)
+                mm(P[pk][:, 0:16], T.ZR[:], T.ON[:, 0:16], False, True, ["ZR", "ON"], ["p%d" % pk], 128, 16, pk)
+                act(T.TS[:, 336 * (c - 1):336 * (c - 1) + 324], P[pk][:, 0:324], ID, ["p%d" % pk], ["TS%d" % (c - 1)], 324, pb=[pk])
+            if c == 1:
+                act(T.TG[:], P[0][:, 0:324], F.Sign, ["p0"], ["TG"], 324, pb=[0])
+                places(1, 0, 2)
+                reads(0, 0, 2, "LT00")
+                reads(1, 0, 2, "LT10")
+        places(1, 2, 3)
+        reads(0, 2, 3, "LT00")
+        reads(1, 2, 3, "LT12")
+        ts(T.LF[:, 24:48], lu[1], -MID, None, A.add, None, LN[1], ["LF1"], 24)
+        sides(1, 6)
+        for u in range(2):
+            U, pk = str(u), 4 + u
+            o, on = P[pk][:, 0:S], ["p%d" % pk]
+            if u == 0:
+                mm(o, I16, T.UV[:, bs[1]], True, True, ["I16", "UV1"], on, 128, S, pk)
+                tt(T.MT[:, bs[0]], o, T.A16[:], A.is_equal, on + A16N, ["MT0"], S, pb=[pk])
+            else:
+                mm(o, T.CC[0:32, :], T.ON[0:32, :], True, False, ["CC0", "ON"], on, 128, S, pk)
+                mm(o, I16, T.UV[:, bs[0]], False, False, ["I16", "UV0"], on, 128, S, pk)
+                mm(o, T.SJ[:, 0:128], T.AGB[:, bs[1]], False, True, ["SJ0", "AG1"], on, 128, S, pk)
+                tt(T.MT[:, bs[1]], o, T.EB[:, bs[1]], A.is_equal, on + ["EB1"], ["MT1"], S, pb=[pk])
+            mm(o, T.ZM[:, 0:128], T.WT[:, bs[u]], True, False, ["ZM0", "WT" + U], on, 128, S, pk)
+            mm(o, T.ZM[:, 128:256], T.MT[:, bs[u]], False, True, ["ZM1", "MT" + U], on, 128, S, pk)
+            act(T.SG[:, bs[u]], o, F.Sign, on, ["SG" + U], S, pb=[pk])
+            if u == 0:
+                mm(o, T.SJ[:, 384:512], T.SG[:, bs[0]], True, False, ["SJ3", "SG0"], on, 128, S, pk)
+                mm(o, T.IB[:], T.RB[:], False, False, ["IB", "RB"], on, 128, S, pk)
+                mm(o, T.SJ[:, 0:128], T.AGB[:, bs[0]], False, False, ["SJ0", "AG0"], on, 128, S, pk)
+                mm(o, I16, T.A16[:], False, True, ["I16"] + A16N, on, 128, S, pk)
+                if MSS[0]:
+                    act(T.NW[:, bs[0]], o, F.Relu, on + ["PC16"], ["NW0"], S, bias=PC[:, 16:17], scale=-1.0, pb=[pk])
+                    act(T.MS[:, bs[0]], T.NW[:, bs[0]], ID, ["NW0"], ["MS0"], S, bias=65535.0, scale=-1.0)
                 else:
-                    mm(Z[1], T.SI[:, 512:640], T.ON[:], False, False, ["SI4", "ON"], kz, 128, 128, kb)
-                    mm(Z[1], T.IF[:], T.EB[:, es[1]], False, True, ["IF", "EB1" + C], kz, 128, 128, kb, 4)
-            for u in range(2):
-                act(T.MS[:, bs[u]], Z[u], ID, kz, ["MS" + US[u]], 128, pb=[kb])
-        LUR = ["LU%d%d" % (u, c) for u in range(2) for c in range(3)]
-        al = lambda s: [s + "%d%d" % (u, c) for u in range(2) for c in range(3)]
-        cp(T.LF[:, 0:48], T.LUV[:], LUR, ["LF"], 48)
-        ts(T.LF[:, 48:72], T.LUV[:, 24:48], -float(n0), None, A.add, None, LUR, ["LFa"], 24)
-        ts(T.LF[:, 72:96], T.LUV[:, 0:24], -float(n0), None, A.add, None, LUR, ["LFb"], 24)
+                    ts(T.MS[:, bs[0]], o, PC[:, 14:15], 65535.0, A.add, A.min, on + ["PC14"], ["MS0"], S, pb=[pk])
+            elif MSS[1]:
+                mm(o, T.SI[:, 512:640], T.SG[:, bs[1]], True, False, ["SI4", "SG1"], on, 128, S, pk)
+                mm(o, T.IF[:], T.EB[:, bs[1]], False, True, ["IF", "EB1"], on, 128, S, pk, 4)
+                act(T.MS[:, bs[1]], o, ID, on, ["MS1"], S, bias=-65536.0, pb=[pk])
+            else:
+                mm(o, T.SI[:, 512:640], T.SG[:, bs[1]], True, True, ["SI4", "SG1"], on, 128, S, pk)
+                tt(T.MS[:, bs[1]], o, T.EB[:, bs[1]], A.min, on + ["EB1"], ["MS1"], S, pb=[pk])
+        o = P[6][:, 0:S]
+        mm(o, T.IS6[:, 0:128], T.A16[:], True, False, ["IS6"] + A16N, ["p6"], 128, S, 6)
+        for u in range(2):
+            mm(o, T.IS6[:, 128 + 128 * u:256 + 128 * u], T.UV[:, bs[u]], False, u == 1, ["IS6%d" % u, "UV%d" % u], ["p6"], 128, S, 6)
+        act(T.NEW[:, 0:S], o, ID, ["p6", "PC7"], ["NEW"], S, bias=PC[:, 7:8], pb=[6])
         RP = P[0]
-        for c0, c1 in ((0, 2), (2, 3)):
-            for u in range(2):
-                a, b, nm = 24 * u + 8 * c0, 24 * u + 8 * c1, "%d%d" % (u, c0)
-                cp(T.LI[:, a:b], T.LUV[:, a:b], ["LU%d%d" % (u, c) for c in range(c0, c1)], ["LI" + nm], 16)
-                ts(T.LI[:, a:b], T.LI[:, a:b], 4, None, A.arith_shift_right, None, ["LI" + nm], ["LI" + nm], 16)
-                ts(T.LT[:, a:b], T.LI[:, a:b], PC[:, 12:13], None, A.add, None, ["LI" + nm, "PC12"], ["LT" + nm], 16)
-                d = slice(S * u + 128 * c0, S * u + 128 * c1)
-                ot = ["OT%d%d" % (u, c) for c in range(c0, c1)]
-                tt(T.RR[:, d], T.TS[:, 0:336].indirect(T.LT[:, a:b]), T.OT[:, d], A.mult, ["TS0", "TSd", "LT" + nm] + ot, ["RR" + nm], 128 * (c1 - c0), ga=True)
-                if c0 == 2:
-                    tt(T.RR[:, 768 + 128 * u:896 + 128 * u], T.TS[:, 336:660].indirect(T.LT[:, a:b]), T.OT[:, d], A.mult, ["TS1", "LT" + nm] + ot, ["RS%d" % u], 128, ga=True)
-        for u in range(2):
-            for c in range(3):
-                o = RP[:, 256 + 24 * u + c:256 + 24 * u + 24:3] if c < 2 else RP[:, 304 + 8 * u:312 + 8 * u]
-                mm(o, T.RR[:, S * u + 128 * c:S * u + 128 * c + 128], T.RC[:, 32:40], True, True, ["RR%d%d" % (u, c // 2 * 2), "RC32"], ["rp%d%d" % (u, c)], 128, 8, 0)
-        for u in range(2):
-            mm(RP[:, 258 + 24 * u:280 + 24 * u:3], T.RR[:, 768 + 128 * u:896 + 128 * u], T.RC[:, 32:40], True, True, ["RS%d" % u, "RC32"], ["rq%d" % u], 128, 8, 0)
-        m = T.SMA
-        FAR = ["far0", "far1", "far2"]
-        far, ok, cnt, cn, aa, c1, ns, b2, m1 = m[:, 0:24], m[:, 32:96], m[:, 96:120], m[:, 128:152], m[:, 160:184], m[:, 192:216], m[:, 224:248], m[:, 256:280], m[:, 288:312]
-        want, rest = T.SMB[:, 0:24], T.SMB[:, 32:56]
-        tt(ok, RP[:, 256:320], T.THR[:], A.is_le, al("rp") + ["rq0", "rq1", "THR0", "THR1", "THR2", "THRx"], ["ok"], 64, pb=[0])
-        tt(m[:, 34:80:3], m[:, 34:80:3], m[:, 80:96], A.mult, ["ok"], ["ok"], 16)
-        tt(cnt, m[:, 32:56], m[:, 56:80], A.mult, ["ok"], ["cnt"], 24)
-        tt(want, cnt, far, A.mult, ["cnt"] + FAR, ["want"], 24)
-
-        def prefix(o, src, nm, on):
-            mm(RP[:, o:o + 24], T.TRI[:], T.SMB[:, src:src + 24], True, False, ["TRI", nm], [on], 128, 24, 0)
-            for x, y in ((0, 1), (0, 2), (1, 2)):
-                mm(RP[:, o + y:o + 24:3], T.ON[:], T.SMB[:, src + x:src + 24:3], False, x == 1, ["ON", nm], [on], 128, 8, 0)
-        prefix(320, 0, "want", "kp")
-        ts(aa, want, -2048.0, 2048.0, A.mult, A.add, ["want"], ["aa"], 24)
-        ts(cn, cnt, 1024.0, None, A.mult, None, ["cnt"], ["cn"], 24)
-        tt(c1, aa, RP[:, 320:344], A.add, ["aa", "kp"], ["c1"], 24, pb=[0])
-        if not last:
-            ts(ns, c1, 96.0, None, A.is_ge, None, ["c1"], ["ns"], 24)
-            tt(rest, ns, far, A.mult, ["ns"] + FAR, ["rest"], 24)
-            prefix(352, 32, "rest", "kq")
-        ts(aa, c1, 96.0, 2048.0, A.is_ge, A.mult, ["c1"], ["aa"], 24)
-        tt(c1, c1, aa, A.add, ["c1", "aa"], ["c1"], 24)
-        tt(m1, c1, T.DS[:], A.min, ["c1", "DS0", "DS1", "DS2"], ["m1"], 24)
-        if not last:
-            ts(b2, rest, -2048.0, 2144.0, A.mult, A.add, ["rest"], ["b2"], 24)
-            tt(b2, b2, RP[:, 352:376], A.add, ["b2", "kq"], ["b2"], 24, pb=[0])
-            tt(m1, m1, b2, A.min, ["m1", "b2"], ["m1"], 24)
-        tt(T.PK[:], m1, cn, A.add, ["m1", "cn"], ["PK"], 24)
-        tt(T.EXP[:], T.PK[:].indirect(T.XL[:, 0:12]), T.MK24[:], A.mult, ["PK", "XLa", "MK24"], ["EXP"], 192, ga=True)
-        for r_ in range(2):
-            for gg in range(8):
-                mm(RP[:, 384 + 24 * r_:408 + 24 * r_], T.LG[:, 128 * gg:128 * gg + 128], T.EXP[:, 24 * gg:24 * gg + 24], gg == 0, gg == 7,
-                   ["LG%d" % gg, "EXP"], ["pp%d" % r_], 128, 24, 0)
+        for b in range(16):
+            mm(RP[:, 0:48], T.GS[:, 128 * b:128 * b + 128], T.RR[:, b:768:16], b == 0, b == 15, ["GS%d" % b, "RR00", "RR10", "RR02", "RR12"], ["p0"], 128, 48, 0)
+        tt(nbad, RP[:, 0:48], T.THR[:], A.is_gt, ["p0", "THR0", "THRa", "THRb"], ["nbad"], 48, pb=[0])
+        mm(RP[:, 96:120], I16, farl, True, False, ["I16", "farl"], ["p0"], 128, 24, 0)
+        mm(RP[:, 96:120], N16, CL[:, 0:24], False, False, ["I17", "nbad"], ["p0"], 128, 24, 0)
+        mm(RP[:, 96:120], N16, CL[:, 24:48], False, True, ["I17", "nbad"], ["p0"], 128, 24, 0)
+        LQ = P[3]
+        mm(LQ[:, 400:448], I16, T.LF[:, 0:48], True, False, ["I16", "LF0", "LF1"], ["lq"], 128, 48, 3)
+        mm(LQ[:, 400:448], B16, nbad, False, False, ["I18", "nbad"], ["lq"], 128, 48, 3)
+        mm(LQ[:, 400:424], B16, CL[:, 24:48], False, False, ["I18", "nbad"], ["lq"], 128, 24, 3)
+        mm(LQ[:, 424:448], B16, CL[:, 0:24], False, True, ["I18", "nbad"], ["lq"], 128, 24, 3)
         l = T.LSA
-        P2, lm, pos, l1, l2 = RP[:, 384:432], l[:, 0:48], l[:, 48:96], l[:, 96:144], l[:, 144:192]
-        PP = ["pp0", "pp1"]
-        ts(lm, P2, 1024.0, -1024.0, A.is_ge, A.mult, PP, ["lm"], 48, pb=[0])
-        ts(l1, P2, 1024.0, 4096.0, A.is_lt, A.mult, PP, ["l1"], 48, pb=[0])
-        tt(pos, lm, P2, A.add, PP + ["lm"], ["pos"], 48, pb=[0])
-        cp(T.LP[:], l[:, 48:72], ["pos"], ["LP"], 24)
-        ms(T.CP[:, 0:208], float(S), ["CPa"], 208)
-        cp(T.CP[:].indirect(T.LP[:]), T.IOT[:, 0:S], ["IOT", "LP"], ["CPa", "CPb"], S, sc=True)
-        cp(T.C16[:], T.CP[:, 0:208], ["CPa"], ["C16"], 208)
+        l1, z, z2, m = l[:, 0:48], l[:, 48:96], l[:, 96:144], l[:, 144:168]
+        ts(want, RP[:, 96:120], 1.0, None, A.is_ge, None, ["p0"], ["want"], 24, pb=[0])
+        tt(l1, LQ[:, 400:448], T.DUM[:], A.min, ["lq", "DUM"], ["l1"], 48, pb=[3])
+        ts(T.LD[:], l1, MID, None, A.add, None, ["l1"], ["LD"], 48)
+        scan(cs1, T.ON[:, 0:24], want, -128.0, A.mult, A.add, ["ON", "want"], ["cs1"], 24)
+        for o, k in ((128, 0), (152, 0), (176, 2))[0:2 if last else 3]:
+            mm(RP[:, o:o + 24], T.TB[:, 128 * k:128 * k + 128], want, True, False, ["TB%d" % k, "want"], ["p0"], 128, 24, 0)
+            mm(RP[:, o:o + 24], T.SG6[:], cs1, False, True, ["SG6", "cs1"], ["p0"], 128, 24, 0)
+        ts(z, RP[:, 128:176], CN - 4095.0, n0 - MID + 4095.0, A.is_lt, A.mult, ["p0"], ["z"], 48, pb=[0])
+        tt(z2, z, RP[:, 128:176], A.add, ["z", "p0"], ["z2"], 48, pb=[0])
+        tt(T.TGT[:], z2, T.LF[:, 24:72], A.max, ["z2", "LF1", "LF2"], ["TGT"], 48)
         if not last:
-            for a in range(16):
-                mm(P[6][:, 0:7], T.DG[:, 128 * a:128 * a + 128], T.C16[:, CN + 7 * a:CN + 7 * a + 7], a == 0, a == 15, ["DG%d" % a, "C16"], ["ps"], 128, 7, 6)
-            ts(T.LSN[:, 0:14:2], P[6][:, 0:7], 0.0, None, A.add, None, ["ps"], ["LSa"], 7, pb=[6])
-            ts(T.LSN[:, 1:14:2], P[6][:, 0:7], 400.0, None, A.add, None, ["ps"], ["LSb"], 7, pb=[6])
-            so = 224 * t
-            act(T.SND[:, so:so + 224], T.XE[:].indirect(T.LSN[:, 0:14]), ID,
-                ["LSa", "LSb", "XEd", "XEe"] + ["XEx%d" % c for c in range(3)] + ["XEe%d" % c for c in range(3)], ["SND%d" % t], 224, ga=True)
+            ka, kc = l[:, 192:216], l[:, 216:240]
+            ts(ka, RP[:, 176:200], CN - 2048.0, -1.0, A.min, A.mult, ["p0"], ["ka"], 24, pb=[0])
+            tt(ka, ka, kfo, A.add, ["ka", "kfo"], ["ka"], 24)
+            tt(kc, ka, T.DS[:, 24 * t:24 * t + 24], A.max, ["ka", "DS%d" % t], ["kc"], 24)
+            tt(m, kc, l[:, 96:120], A.max, ["kc", "z2"], ["m"], 24)
+            iota(T.CP[:, S:S + XN], [[0, XN]], 0, 0, ["CPb"], XN)
+        else:
+            tt(m, T.DS[:, 24 * t:24 * t + 24], l[:, 96:120], A.max, ["DS%d" % t, "z2"], ["m"], 24)
+        ts(T.LP[:], m, -off, None, A.add, None, ["m"], ["LP"], 24)
+        iota(T.CP[:, 768:864], [[0, CN]], 2 ** 20 + 256 * S, 0, ["CPb"], CN)
+        cp(T.CP[:].indirect(T.LP[:]), T.XE[:], ["XE", "LP"], ["CPb"], S, sc=True)
+        if not last:
+            so = XN * t
+            act(T.SND[:, so:so + XN], T.CP[:, S:S + XN].indirect(T.PL[:, 8:15]), ID, ["CPb", "PLb"], ["SND%d" % t], XN, ga=True)
 
             def fire(q, t=t, so=so):
                 tr = []
@@ -496,55 +629,45 @@ def build(T, topo, rank, core):
                     rid, pid = topo.addr(dst)[0:2]
                     en = topo.engines(core, dst)
                     tr.append(RemoteDMATransfer(dst_ids=[DstId(rid=rid, pnc=pid)], dma_engine_mask=1 << en[k % len(en)],
-                                                remote_sem=T.sem["arr%d" % t], src=T.SND[:, so + 32 * k:so + 32 * k + 32],
-                                                dst=T.LND[:, so + 32 * k:so + 32 * k + 32]))
+                                                remote_sem=T.sem["arr%d" % t], src=T.SND[:, so + 16 * k:so + 16 * k + 16],
+                                                dst=T.LND[:, so + 16 * k:so + 16 * k + 16]))
                 return q.remote_dma_fused(tr, local_sem=T.sem["loc%d" % t])
             send[t] = op("g", fire, ["SND%d" % t], [], 1000, kind="r")
+        ts(T.C16[:], T.CP[:, 768:864], 1.0 / 256, 1024 - 4096 - .498, A.mult, A.add, ["CPb"], ["C16"], CN)
         for a in range(16):
-            mm(P[7][:, 460:466], T.DG[:, 128 * a:128 * a + 128], T.C16[:, a:CN:16], a == 0, a == 15, ["DG%d" % a, "C16"], ["pt"], 128, 6, 7)
-        ts(T.LSP[:, 0:6], P[7][:, 460:466], 0.0, None, A.add, None, ["pt"], ["LPa"], 6, pb=[7])
-        ts(T.LSP[:, 6:12], P[7][:, 460:466], 400.0, None, A.add, None, ["pt"], ["LPb"], 6, pb=[7])
-        tt(l1, l1, T.LF[:, 0:48], A.add, ["l1", "LF"], ["l1"], 48)
-        tt(l1, l1, T.DUM[:], A.min, ["l1", "DUM"], ["l1"], 48)
-        cp(T.LD[:], l1, ["l1"], ["LD"], 48)
-        ts(l2, pos, 96.0, -8192.0, A.is_ge, A.mult, ["pos"], ["l2"], 48)
-        tt(l2, l2, pos, A.add, ["l2", "pos"], ["l2"], 48)
-        tt(l2, l2, T.LF[:, 48:96], A.max, ["l2", "LFa", "LFb"], ["l2"], 48)
-        ts(T.LTG[:], l2, float(n0), None, A.add, None, ["l2"], ["LTG"], 48)
-        TB, TBN = (T.NF, ["NF%d" % k for k in range(5)] + ["NFn"]) if last else (T.NB, NBR)
-        EBR = ["EB0%d" % c for c in range(3)] + ["EBd"]
-        UVR = al("UV") + ["UVd", "UVe"]
-        nu = T.NU
-        act(nu[:, 0:96], T.EB[:, 0:400].indirect(T.LSP[:, 0:6]), ID, EBR + ["LPa", "PC6", "PC7"], ["nu0"], 96, bias=PC[:, 7:8], scale=PC[:, 6:7], ga=True)
-        act(nu[:, 96:192], T.UV[:].indirect(T.LSP[:, 0:6]), ID, UVR + ["LPa", "PC8"], ["nu1"], 96, scale=PC[:, 8:9], ga=True)
-        act(nu[:, 192:288], T.UV[:].indirect(T.LSP[:, 6:12]), ID, UVR + ["LPb", "PC9"], ["nu2"], 96, scale=PC[:, 9:10], ga=True)
-        for k in range(3):
-            mm(P[6][:, 16:112], T.IF[:], nu[:, 96 * k:96 * k + 96], k == 0, k == 2, ["IF", "nu%d" % k], ["pn"], 128, 96, 6, 4)
-        act(T.XS[:], T.X[:, xo:xo + 400].indirect(T.LSP[:, 0:6]), ID, ["X%d%d" % (t, c) for c in range(3)] + ["Xd%d" % t, "LPa"], ["XS"], 96, ga=True)
-        act(T.WS[:], T.WB[:, 0:400].indirect(T.LSP[:, 0:6]), ID, ["WB0%d" % c for c in range(3)] + ["WBd", "LPa"], ["WS"], 96, ga=True)
-        for k, (a, b, nm) in enumerate(((T.SJ[:, 256:384], T.ON[:, 0:96], ["SJ2", "ON"]), (T.IB[:], T.XS[:], ["IB", "XS"]), (T.IB[:], T.WS[:], ["IB", "WS"]))):
-            mm(P[7][:, 128:224], a, b, k == 0, k == 2, nm, ["tb1"], 128, 96, 7)
-        act(nu[:, 288:384], P[7][:, 128:224], ID, ["tb1"], ["nu3"], 96, bias=RND, scale=.5, pb=[7])
+            mm(P[2][:, 300:306], T.SH[:, 160 + 15 - a:160 + 143 - a], T.C16[:, a:CN:16], a == 0, a == 15, ["SH1", "C16"], ["pt"], 128, 6, 2)
+        ts(T.LSP[:, 0:6], P[2][:, 300:306], -1024.0, None, A.add, None, ["pt"], ["LSP"], 6, pb=[2])
+        TB, TBN = (T.NF, ["NF%d" % k for k in range(5)]) if last else (T.NB, NBR + ["NBc"])
         for u in range(2):
-            b = slice(S * u, S * u + S)
-            qn = ["dl%d" % (4 + u)]
-            act(T.Q[:, b], T.IOT[:].indirect(T.LTG[:, 24 * u:24 * u + 24]), ID, ["IOT", "LTG"], ["Q%d" % u], S, bias=-65536.0, ga=True)
-            mm(P[4 + u][:, 0:S], T.SJ[:, 128:256], T.SG[:, b], True, False, ["SJ1"] + ["SG%d%d" % (u, c) for c in range(3)], qn, 128, S, 4 + u)
-            mm(P[4 + u][:, 0:S], T.IF[:], T.Q[:, b], False, True, ["IF", "Q%d" % u], qn, 128, S, 4 + u, 4)
-            tt(T.NW[:, b], T.MS[:, b], P[4 + u][:, 0:S], A.max, qn + ["MS%d%d" % (u, c) for c in range(3)], ["NW%d" % u], S, pb=[4 + u])
-            cp(TB[:].indirect(T.LD[:, 24 * u:24 * u + 24]), T.NW[:, b], ["NW%d" % u, "LD"], TBN, S, sc=True)
-        for u in range(2):
-            cp(T.W[:].indirect(T.LD[:, 24 * u:24 * u + 24]), T.WI[:, S * u:S * u + S], ["LD"] + ["WI%d%d" % (u, c) for c in range(3)], WR + ["Wn"], S, sc=True)
+            cp(T.W[:].indirect(T.LD[:, 24 * u:24 * u + 24]), T.WI[:, bs[u]], ["LD", "WI%d" % u] + ([] if last else ["C16"]), WR + ["Wd"], S, sc=True)
         if last:
-            dma("a", T.yw[:, 0:n0], T.W[:, 0:n0], WR, ["yw"], 128 * PU * 6)
-            dma("s", T.yn[:, 0:n0], T.NF[:, 0:n0], TBN[0:5], ["yn"], 128 * PU * 4)
-            act(T.NF[:, n0:PU], P[6][:, 16:112], ID, ["pn"], ["NFn"], 96, pb=[6])
-            act(T.W[:, n0:PU], nu[:, 288:384], ID, ["nu3"], ["Wn"], 96, bias=-RND)
-            dma("s", T.yn[:, n0:PU], T.NF[:, n0:PU], ["NFn"], ["yn2"], 50000)
-            dma("s", T.yw[:, n0:PU], T.W[:, n0:PU], ["Wn"], ["yw2"], 25000)
+            dma("a", T.yw[:, 0:n0], T.W[:, 0:n0], WR, ["yw"], 5000)
+        for u in range(2):
+            U, pk = str(u), 4 + u
+            o, on = P[pk][:, 0:S], ["p%d" % pk]
+            mm(o, T.SJ[:, 128:256], T.SG[:, bs[u]], True, False, ["SJ1", "SG" + U], on, 128, S, pk)
+            for b in range(16):
+                mm(P[pk][:, b:S:16], T.SEL[:, 128 * b:128 * b + 128], T.TGT[:, 24 * u:24 * u + 24], False, b == 15, ["SEL%d" % b, "TGT"], on, 128, 24, pk)
+            tt(T.NW[:, bs[u]], T.MS[:, bs[u]], o, A.max, on + ["MS" + U], ["NW" + U], S, pb=[pk])
+            cp(TB[:].indirect(T.LD[:, 24 * u:24 * u + 24]), T.NW[:, bs[u]], ["NW" + U, "LD"], TBN, S, sc=True)
+        lsp = T.LSP[:, 0:6]
+        act(T.XS[:], T.X[:, xo:xo + 400].indirect(lsp), ID, XN_[t] + ["Xd%d" % t, "LSP"], ["XS"], CN, ga=True)
+        act(T.WS[:], T.WB[:, 0:400].indirect(lsp), ID, ["WB0", "WBd", "LSP"], ["WS"], CN, ga=True)
+        for k, (a, b, nm) in enumerate(((T.SJ[:, 256:384], T.ON[:, 0:CN], ["SJ2", "ON"]), (T.IB[:], T.XS[:], ["IB", "XS"]), (T.IB[:], T.WS[:], ["IB", "WS"]))):
+            mm(P[7][:, 128:224], a, b, k == 0, k == 2, nm, ["p7"], 128, CN, 7)
+        act(T.NU[:], P[7][:, 128:224], ID, ["p7"], ["NU"], CN, bias=RND, scale=.5, pb=[7])
+        if last:
+            dma("s", T.yn[:, 0:n0], T.NF[:, 0:n0], TBN, ["yn"], 8000)
+            act(T.NFN[:], T.NEW[:].indirect(lsp), ID, ["NEW", "NEWd", "LSP"], ["NFN"], CN, ga=True)
+            act(T.WN[:], T.NU[:], ID, ["NU"], ["WN"], CN, bias=-RND)
+            dma("a", T.yn[:, n0:PU], T.NFN[:], ["NFN"], ["yn2"], 2500)
+            dma("a", T.yw[:, n0:PU], T.WN[:], ["WN"], ["yw2"], 2500)
         else:
-            cp(T.NB[:, n0:n0 + CN], P[6][:, 16:112], ["pn"], NBR, 96, pb=[6])
-            act(T.W[:, n0:n0 + CN], nu[:, 288:384], ID, ["nu3"], WR, 96, bias=-RND)
+            if SI32:
+                act(T.NB[:, n0:n0 + CN], T.NEW[:].indirect(lsp), ID, ["NEW", "NEWd", "LSP"], NBR, CN, ga=True)
+            else:
+                cp(T.NB[:, n0:n0 + CN], T.NEW[:].indirect(lsp), ["NEW", "NEWd", "LSP"], NBR, CN, ga=True)
+            act(T.W[:, n0:n0 + CN], T.NU[:], ID, ["NU"], WR, CN, bias=-RND)
     return ops
 
 
@@ -554,7 +677,7 @@ def plan(ops):
     succ = [[] for _ in range(n)]
     for i, o in enumerate(ops):
         for d in o["d"]:
-            w = (70 if o["d"][d] or o["e"] != "t" else 0) if ops[d]["e"] == o["e"] and ops[d]["k"] == "c" else 120
+            w = (WSAME if o["d"][d] or o["e"] != "t" else 0) if ops[d]["e"] == o["e"] and ops[d]["k"] == "c" else WOTHER
             pred[i].append((d, w))
             succ[d].append((i, w))
     eng = [o["e"] for o in ops]
@@ -600,8 +723,17 @@ def plan(ops):
         for _ in range(ROUNDS):
             order, fin = run(prio, pred, succ)
             if best is None or max(fin) < best[0]:
-                best = (max(fin), order)
+                best = (max(fin), order, fin)
             prio = run(fin, succ, pred)[1]
+    for k in range(SHAKES):
+        amp = (300.0, 800.0, 2000.0)[k % 3]
+        prio = [f + amp * ((i // 8 * 2654435761 + k * 40503 * (i // 8 + 1)) % 1009) / 1009.0 for i, f in enumerate(best[2])]
+        for _ in range(2):
+            order, fin = run(run(prio, succ, pred)[1], pred, succ)
+            if max(fin) < best[0]:
+                best = (max(fin), order, fin)
+            prio = fin
+    CACHE["span"] = best[0]
     return best[1]
 
 

@@ -10,17 +10,15 @@ HB = 162
 MID = 1344.0
 LN2 = math.log(2.0)
 RND = 12582912.0
-XLO, XHI = 64, 384
-XW = 16 * (XHI - XLO)
 bf, f32, i32, u16, f16 = "bfloat16", "float32", "int32", "uint16", "float16"
 SCRATCH = {}
 for _d, _s in (
-        (bf, "W:3376 OH:2608 X:1200 XR:15360 BH:384 G:6144 M:6144 G0:384 M0:384 BH0:384 BB:7776 OT:768 AW:768 TS:672 TG:324 RR:768 RX:1088 "
+        (bf, "W:3376 OH:2608 X:1200 XR:18432 BH:384 G:6144 M:6144 G0:384 M0:384 BH0:384 BB:7776 OT:768 AW:768 TS:672 TG:324 RR:768 RX:272 "
              "WB:800 AGB:768 WT:768 MT:768 SG:768 RB:384 WS:96 XS:96 WN:96 IB:128 NI:400 RC:48 ON:384 ZR:128 ZM:256 SI:640 "
              "SJ:640 I162:162 GS:2048 SGB:128 CC:128"),
         (f32, "NF:3376 IOT:2608 THB:128 THK:24 XE:384 HF:48 FAR:72 LSA:240 CP:864 EB:768 MS:768 NEW:400 NFN:96 "
               "NW:768 TA:128 NU:96 SND:224 LND:224 OWN:224 CI:256 CM:128 CD:128 PC:32 R32:24 SMM:128 "
-              "SGM:128 IS:136 IF:128 D0:544 MK24:320 THR:48 DUM:48 DS:72 CT:64 TRI:128 K17:408"),
+              "SGM:128 IS:136 IF:128 D0:544 MK24:320 THR:48 DUM:48 DS:72 CT:64 TRI:128 K17:272"),
         (i32, "NB:3376 EN:72 THI:8 I32:384 SC:816 CUR:48 FH:72 HT:96 LI:48 MX:112 MY:224 PI:16 WI:768"),
         (u16, "LE:72 O16:384 LH:48 LUV:48 LT:48 LD:48 LP:24 LSP:8 XL:32 PL:16"),
         (f16, "A16:384 EX:384 EXP:192 C16:96 E16:112 I16:520 LG:240 SH:304 ID0:384 RA:16 D16:256 IO6:384 SEL:2048 SG6:128 TB:384 LF:72 TGT:48 CL:192 IS6:384 UV:768")):
@@ -31,15 +29,19 @@ for _k in range(8):
 SEMAPHORES = ["sv", "sa", "sp", "st", "arr0", "arr1", "loc0", "loc1"] + ["d%d" % _k for _k in range(20)]
 
 GAM, SIG, CY, PECY, VF, AF, TF = 1.56, 3.8, 0.83, 0.44, 5.0, 30.0, 5.0
-NA = [[0, 0, 0]] * 4
-NE = [[0, 0, 0]] * 4
-AP_, BP_ = 32, 64
-ND, EBS = 2, True
+RG = [(64, 96)] * 3
+CUT = [(0, 32, 64)] * 3
+AP_, EBS = 32, True
 LATE = ["OT12", "TS1", "TS1"]
 AWV = (2,)
 SI32, MSS = True, (False, True)
+WP, CUS = (3, 1), True
+LHS, MTS = False, (False, False)
+SPR = "vaav"
+NOV = ()
 STAG = [0.0, 0.0, 0.0]
-BINIT, LOOK, ROUNDS, TRIES, SHAKES = 5000.0, 60.0, 3, 8, 150
+BINIT, LOOK, ROUNDS, TRIES, SHAKES = 5000.0, 60.0, 3, 8, 300
+PEN, FIT = 0.0, 20.0
 WSAME, WOTHER = 200.0, 200.0
 CACHE = {}
 ID = F.Identity
@@ -111,13 +113,15 @@ def build(T, topo, rank, core):
     def mm(o, l, rr, st, sp, r, w, m, n, pb, x=1):
         return op("t", lambda q: q.matmul(o, l, rr, st, sp), r, w, TF + x * max(min(64, m), n) * PECY, [pb])
 
+    first = []
+
     def iota(o, pat, base, cm, w, n, fl=True):
         if fl:
-            return op("g", lambda q: q.iota(o, pat, base, cm, allow_small_or_imprecise_dtypes=True), [], w, 130 + 2 * n * CY)
-        return op("g", lambda q: q.iota(o, pat, base, cm), [], w, 130 + 2 * n * CY)
+            return op("g", lambda q: q.iota(o, pat, base, cm, allow_small_or_imprecise_dtypes=True), [], w, 130 + 2 * n * CY, after=first)
+        return op("g", lambda q: q.iota(o, pat, base, cm), [], w, 130 + 2 * n * CY, after=first)
 
     def sel(o, i, pat, base, r, w, n):
-        return op("g", lambda q: q.affine_select(o, i, pat, A.is_equal, 0.0, base, 0), r, w, 170 + 2 * n * CY)
+        return op("g", lambda q: q.affine_select(o, i, pat, A.is_equal, 0.0, base, 0), r, w, 170 + 2 * n * CY, after=first)
 
     def dma(eng, o, i, r, w, ns):
         return op(eng, lambda q: q.dma_start(o, i), r, w, ns, kind="d")
@@ -138,11 +142,11 @@ def build(T, topo, rank, core):
     iota(T.CM[:], [[0, 8], [1, 16]], 0, 0, ["CM", "g0"], 128)
     iota(T.CD[:], [[1, 8], [0, 16]], 0, 0, ["CD", "g0"], 128)
     iota(T.MK24[:, 0:192], [[0, 24], [1, 8]], 0, 0, ["MK24", "g0"], 192)
-    for k, (a, b, c) in enumerate(((16, 1, -1), (0, 1, -1), (1, 0, 0))):
+    for k, (a, b, c) in enumerate(((16, 1, -1), (1, 0, 0))):
         iota(T.K17[:, 136 * k:136 * k + 136], [[a, 8], [b, 17]], c, 0, ["K17%d" % k, "g0"], 136)
     iota(T.R32[:], [[1, 8], [0, 3]], 0, 0, ["R32", "g0"], 24)
     iota(T.NB[:, L:GW], [[0, GW - L]], 65535, 0, ["NBb", "g0"], GW - L, False)
-    iota(T.IOT[:], [[1, GW]], 0, 0, ["IOT", "g0"], GW)
+    first.append(iota(T.IOT[:], [[1, GW]], 0, 0, ["IOT", "g0"], GW))
     ms(T.W[:, L:PU], 0.0, ["Wb"], 288, .5)
     ms(T.W[:, PU:GW], 8192.0, ["Wc"], 16, .5)
     iota(T.NB[:, GW:TW], [[0, 768]], 0, 0, ["NBc"], 768, False)
@@ -168,7 +172,7 @@ def build(T, topo, rank, core):
                      (T.SI[:, 384:512], .125, "SI3"), (T.SI[:, 512:640], -65536.0, "SI4"),
                      (T.SJ[:, 0:128], 4096.0, "SJ0"), (T.SJ[:, 128:256], MID, "SJ1"), (T.SJ[:, 256:384], -.375, "SJ2"),
                      (T.SJ[:, 384:512], -2.0 ** 21, "SJ3")):
-        ts(o, T.IB[:], v, None, A.mult, None, ["IB"], [nm], 128, .5)
+        act(o, T.IB[:], ID, ["IB"], [nm], 128, scale=v)
     ts(T.SJ[:, 512:640], T.IB[:], 2.0 ** 60, 2.0 ** 61, A.mult, A.mult, ["IB"], ["SJ4"], 128, .5)
     I16, N16, B16 = T.I16[:, 0:128], T.I16[:, 128:256], T.I16[:, 256:384]
     for o, v in ((0, 4096.0), (8, 4096.0), (16, -8192.0), (24, -8192.0)):
@@ -192,19 +196,28 @@ def build(T, topo, rank, core):
     ts(T.SH[:, 160:304], T.CI[:, 0:144], 1000.0 - 14.0, PC[:, 15:16], A.add, A.is_equal, ["CI", "PC15"], ["SH1"], 144)
     LG = [T.LG[:, 112 - 16 * k:240 - 16 * k] for k in range(8)]
     SH = [T.SH[:, 15 - k:143 - k] for k in range(16)]
-    cp(T.SG6[:], T.SGM[:], ["SGM"], ["SG6"], 128)
-    cp(T.SGB[:], T.SGM[:], ["SGM"], ["SGB"], 128)
+    act(T.SG6[:], T.SGM[:], ID, ["SGM"], ["SG6"], 128)
+    act(T.SGB[:], T.SGM[:], ID, ["SGM"], ["SGB"], 128)
     for k in range(16):
-        ts(T.SEL[:, 128 * k:128 * k + 128], T.SG6[:], T.SMM[:, k:k + 1], None, A.mult, None, ["SG6", "SMM"], ["SEL%d" % k], 128, .5)
+        act(T.SEL[:, 128 * k:128 * k + 128], T.SGM[:], ID, ["SGM", "SMM"], ["SEL%d" % k], 128, scale=T.SMM[:, k:k + 1])
         sel(T.GS[:, 128 * k:128 * k + 128], T.SGB[:], [[0, 8], [1, 16]], -k, ["SGB"], ["GS%d" % k], 128)
-    RX = {}
-    for k, ne in enumerate(sorted(set(x for row in NE for x in row if x < 16))):
-        RX[ne] = T.RX[:, 272 * k:272 * k + 272]
-        if k == 0:
-            ts(T.K17[:, 272:408], T.K17[:, 272:408], cG, None, A.is_equal, None, ["K172", "PC"], ["K172"], 136)
-        ts(T.IS[:], T.K17[:, 136:272], float(ne), 4096.0, A.is_ge, A.mult, ["K171"], ["IS"], 136)
-        for o in (0, 136):
-            tt(T.RX[:, 272 * k + o:272 * k + o + 136], T.IS[:], T.K17[:, 272:408], A.mult, ["IS", "K172"], ["RX%d_%d" % (ne, o)], 136)
+    for o in (0, 136):
+        ts(T.RX[:, o:o + 136], T.K17[:, 136:272], cG, 4096.0, A.is_equal, A.mult, ["K171", "PC"], ["RX%d" % o], 136)
+    ms(T.RX[:, 0:272:17], 0.0, ["RX0", "RX136"], 16)
+    XO, XB, XC = [0], [], []
+    for c in range(3):
+        n1, n2 = RG[c]
+        XO.append(XO[-1] + 16 * (128 - n1))
+        if c and XC[-1] + 4 * RG[c - 1][0] + 4 * n1 <= 512:
+            XB.append(XB[-1])
+            XC.append(XC[-1] + 4 * RG[c - 1][0])
+        else:
+            XB.append(XB[-1] + 1 if c else 4)
+            XC.append(0)
+        if n2 > n1:
+            ms(T.M[:, 2048 * c + 16 * n1:2048 * c + 16 * n2], 0.0, ["Mz%d" % c], 16 * (n2 - n1), .5)
+    XW = XO[3]
+    DB = list(range(XB[2] + 1 if any(a for a, b in RG) else 4, 7))
     cp(T.OH[:, 0:128], T.SMM[:], ["SMM"], ["OH"], 128)
     for a in (128, 256, 512, 1024, 2048):
         b = min(a, GW - a)
@@ -234,9 +247,12 @@ def build(T, topo, rank, core):
     for k in range(2):
         ts(PC[:, 29 + k:30 + k], cA, float(k), None, A.is_equal, None, ["PC"], ["PC%d" % (29 + k)], 1)
         ts(T.IS6[:, 128 + 128 * k:256 + 128 * k], T.IB[:], PC[:, 29 + k:30 + k], None, A.mult, None, ["IB", "PC%d" % (29 + k)], ["IS6%d" % k], 128, .5)
-    ts(PC[:, 8:9], cP, 0.0, -129.0 * 4096, A.is_equal, A.mult, ["PC"], ["PC8"], 1)
-    ts(PC[:, 13:14], cP, 1.0, MID, A.is_equal, A.mult, ["PC"], ["PC13"], 1)
-    ts(T.CC[:], T.ZR[:], PC[:, 8:9], PC[:, 13:14], A.add, A.add, ["ZR", "PC13", "PC8"], ["CC0"], 128, .5)
+    if MTS[1]:
+        act(T.CC[:], T.IB[:], ID, ["IB"], ["CC1"], 128, scale=-4096.0)
+    else:
+        ts(PC[:, 8:9], cP, 0.0, -129.0 * 4096, A.is_equal, A.mult, ["PC"], ["PC8"], 1)
+        ts(PC[:, 13:14], cP, 1.0, MID, A.is_equal, A.mult, ["PC"], ["PC13"], 1)
+        ts(T.CC[:], T.ZR[:], PC[:, 8:9], PC[:, 13:14], A.add, A.add, ["ZR", "PC13", "PC8"], ["CC0"], 128, .5)
     ts(PC[:, 18:19], cA, -LN2, LN2 * (11 - 108 - 1548), A.mult, A.add, ["PC"], ["PC18"], 1)
     ts(PC[:, 10:11], PC[:, 6:7], -400.0, PC[:, 18:19], A.mult, A.add, ["PC6", "PC18"], ["PC10"], 1)
     ts(PC[:, 19:20], cA, -LN2, LN2 * 107, A.mult, A.add, ["PC"], ["PC19"], 1)
@@ -275,19 +291,22 @@ def build(T, topo, rank, core):
     mm(P[7][:, 0:24], T.THB[:], T.R32[:], True, True, ["THB", "R32"], ["p7"], 128, 24, 7, 4)
     cp(T.THK[:], P[7][:, 0:24], ["p7"], ["THK"], 24, pb=[7])
     early = [k for k, o in enumerate(ops) if o["e"] == "v" and not set(o["w"]) & {"PC28", "THB", "THK", "ZM1", "THRa"}]
+    early += [k for k, o in enumerate(ops) if o["e"] == "a" and o["k"] == "c" and not set(o["w"]) & {"THR0"}]
     op("v", lambda q: q.tensor_copy(T.LE[:], T.EN[:]), ["EN"], ["LE%d%d" % (t, c) for t in range(NT) for c in range(3)], vc(72), after=early)
     def spread(t, c, eng):
-        na = max(row[c] for row in NA)
+        na = 128 - RG[c][0]
         lo, hi = 128 * c + 128 - na, 128 * c + 128
         for i in range(16 if na else 0):
-            o, src = T.XR[:, XW * t + 16 * (lo - XLO) + i:XW * t + 16 * (hi - XLO):16], T.X[:, 400 * t + lo:400 * t + hi]
+            o, src = T.XR[:, XW * t + XO[c] + i:XW * t + XO[c] + 16 * na:16], T.X[:, 400 * t + lo:400 * t + hi]
             if eng == "v":
                 cp(o, src, [XN_[t][c]], ["XR%d%d_%d" % (t, c, i)], na, .5)
+            elif eng == "a":
+                act(o, src, ID, [XN_[t][c]], ["XR%d%d_%d" % (t, c, i)], na)
             else:
                 sel(o, src, [[0, na]], 0, [XN_[t][c]], ["XR%d%d_%d" % (t, c, i)], na)
     for t in range(NT):
         for c in range(3 if t == 0 else 2):
-            spread(t, c, "v" if t == 0 else "g")
+            spread(t, c, SPR[c] if t == 0 else "g")
     for t in (1, 2):
         o = XN * (t - 1)
         act(T.TA[:], T.IOT[:].indirect(T.LE[:, 24 * t + 16:24 * t + 24]), ID, ["IOT", "LE%d2" % t], ["TA0"], 128, scale=256.0, ga=True)
@@ -310,7 +329,7 @@ def build(T, topo, rank, core):
             for a in range(16):
                 mm(P[3][:, 304:311], SH[a], T.E16[:, a:XN:16], a == 0, a == 15, ["SH", "E16"], ["k2e"], 128, 7, 3)
             ts(T.LE[:, 24 * t + 17:24 * t + 24], P[3][:, 304:311], MID, None, A.add, None, ["k2e"], ["LE%d2" % t], 7, pb=[3])
-            spread(t, 2, "v")
+            spread(t, 2, SPR[3])
         if last:
             for k in range(4):
                 sel(T.NF[:, 652 * k:652 * k + 652], T.NB[:, 652 * k:652 * k + 652], [[0, 652]], 0, NBR, ["NF%d" % k], 652)
@@ -321,8 +340,9 @@ def build(T, topo, rank, core):
             xc, xn = T.X[:, xo + 128 * c:xo + 128 * c + 128], XN_[t][c]
             le, ln = T.LE[:, 24 * t + 8 * c:24 * t + 8 * c + 8], "LE%d%d" % (t, c)
             bias[0] = BINIT
-            if any(NE[h][c] < 16 and NA[h][c] < 128 for h in range(4)):
-                mm(P[6][:, cs], T.IB[:], xc, True, True, ["IB", xn], ["xp" + C, "p6"], 128, 128, 6)
+            n1 = RG[c][0]
+            for j in range(4 if n1 else 0):
+                mm(P[XB[c]][:, XC[c] + j:XC[c] + 4 * n1:4], T.IB[:], T.X[:, xo + 128 * c:xo + 128 * c + n1], True, True, ["IB", xn], ["xp" + C, "p%d" % XB[c]], 128, n1, XB[c])
             act(T.ID0[:, cs], T.IOT[:].indirect(le), ID, ["IOT", ln], ["ID0" + C], 128, bias=-MID, ga=True)
             act(T.BH0[:, cs], T.ID0[:, cs], ID, ["ID0" + C], ["BH0" + C], 128, bias=8224.5 + MID)
             act(T.G0[:, cs], T.W[:, 0:GW].indirect(le), ID, WR + [ln], ["G0" + C], 128, ga=True)
@@ -357,39 +377,39 @@ def build(T, topo, rank, core):
                 ts(T.BH[:, cs], T.O16[:, cs], 8224.5, None, A.add, None, ["O16" + C], ["BH" + C], 128, .5)
                 ts(T.A16[:, cs], T.O16[:, cs], -MID, None, A.add, None, ["O16" + C], ["A16" + C], 128, .5)
                 go = 2048 * c
-                nb = 128 - NA[h][c]
-                gn = lambda a, b: ["G%d_%d" % (c, k) for k in range(a // 32, (b + 31) // 32)]
-                mall = ["M%d_%d" % (c, k) for k in range(16)]
-                bp = BP_ if nb % BP_ == 0 else nb
-                ne = NE[h][c] if nb else 16
-                rs = 8 if bp <= 64 and ne % 8 == 0 else 4
-                mslot = lambda i: T.M[:, go + rs * nb * (i // rs) + i % rs:go + rs * nb * (i // rs + 1):rs]
-                mname = lambda i: mall[rs * nb * (i // rs) // 128:(rs * nb * (i // rs + 1) + 127) // 128]
-                for a0 in range(0, nb, bp):
-                    a1 = a0 + bp
-                    ns = a1 - a0
+                n1, n2 = RG[c]
+                if (h, c) in NOV:
+                    n2 = 128
+                u_ = "%d%d%d" % (t, h, c)
+                gn = lambda a, b: ["G%s_%d" % (u_, k) for k in range(a // 16, b // 16)]
+                mn = [["Mz" + C] if n2 > n1 else [] for q in range(4)]
+                xr, xrn = XW * t + XO[c] - 16 * n1, ["XR%d%d_%d" % (t, c, i) for i in range(16)]
+                cuts = [a for a in CUT[c] if a < n2] + [n2]
+                for a0, a1 in zip(cuts, cuts[1:]):
                     act(T.G[:, go + 16 * a0:go + 16 * a1], T.W[:, 0:GW].indirect(T.O16[:, 128 * c + a0:128 * c + a1]), ID,
-                        WR + ["O16" + C], gn(a0, a1), 16 * ns, ga=True)
-                    for q in range(ne // rs):
-                        db = 4 + turn[0] % ND
-                        turn[0] += 1
-                        for r in range(rs):
-                            o = P[db][:, r:rs * ns:rs]
-                            mm(o, T.IB[:], T.G[:, go + 16 * a0 + rs * q + r:go + 16 * a1:16], True, False, ["IB"] + gn(a0, a1), ["p%d" % db], 128, ns, db)
-                            mm(o, T.NI[:, 0:128], T.X[:, xo + 128 * c + a0:xo + 128 * c + a1], False, True, ["NI0", xn], ["p%d" % db], 128, ns, db)
-                        mo = go + rs * nb * q + rs * a0
-                        nm = mall[(mo - go) // 128:(mo - go + rs * ns + 127) // 128]
-                        act(T.M[:, mo:mo + rs * ns], P[db][:, 0:rs * ns], F.Abs, ["p%d" % db], nm, rs * ns, pb=[db])
-                for i in range(ne, 16):
-                    tt(mslot(i), T.G[:, go + i:go + 16 * nb:16], P[6][:, 128 * c:128 * c + nb], A.min, gn(0, nb) + ["xp" + C],
-                       ["m%d%d%d_%d" % (t, h, c, i)], nb, pb=[6])
-                for a0 in range(nb, 128, AP_):
+                        WR + ["O16" + C], gn(a0, a1), 16 * (a1 - a0), ga=True)
+                    if a0 < n1:
+                        b1 = min(a1, n1)
+                        for q in range(4):
+                            r_ = slice(go + 16 * a0 + q, go + 16 * b1, 4)
+                            mn[q].append("m%s_%d_%d" % (u_, q, a0))
+                            tt(T.M[:, r_], T.G[:, r_], P[XB[c]][:, XC[c] + 4 * a0:XC[c] + 4 * b1], A.min, gn(a0, b1) + ["xp" + C], mn[q][-1:], 4 * (b1 - a0), pb=[XB[c]])
+                for a0 in range(n1, n2, 32):
+                    a1 = min(n2, a0 + 32)
+                    db = DB[turn[0] % len(DB)]
+                    turn[0] += 1
+                    r_, o = slice(go + 16 * a0, go + 16 * a1), P[db][:, 0:16 * (a1 - a0)]
+                    mm(o, T.NI[:, 0:128], T.XR[:, xr + 16 * a0:xr + 16 * a1], True, False, ["NI0"] + xrn, ["p%d" % db], 128, 16 * (a1 - a0), db)
+                    mm(o, T.IB[:], T.G[:, r_], False, True, ["IB"] + gn(a0, a1), ["p%d" % db], 128, 16 * (a1 - a0), db)
+                    act(T.G[:, r_], o, F.Abs, ["p%d" % db], gn(a0, a1), 16 * (a1 - a0), pb=[db])
+                for a0 in range(n2, 128, AP_):
                     a1 = min(128, a0 + AP_)
                     r_ = slice(go + 16 * a0, go + 16 * a1)
-                    xr = XW * t + 16 * (128 * c - XLO)
                     tt(T.G[:, r_], T.W[:, 0:GW].indirect(T.O16[:, 128 * c + a0:128 * c + a1]), T.XR[:, xr + 16 * a0:xr + 16 * a1], A.subtract,
-                       WR + ["O16" + C] + ["XR%d%d_%d" % (t, c, i) for i in range(16)], gn(a0, a1), 16 * (a1 - a0), ga=True)
-                    ts(T.M[:, r_], T.G[:, r_], 0.0, None, A.min, None, gn(a0, a1), mall[a0 // 8:a1 // 8], 16 * (a1 - a0), .5)
+                       WR + ["O16" + C] + xrn, gn(a0, a1), 16 * (a1 - a0), ga=True)
+                    ts(T.M[:, r_], T.G[:, r_], 0.0, None, A.min, None, gn(a0, a1), ["m%s_%d" % (u_, a0)], 16 * (a1 - a0), .5)
+                    for q in range(4):
+                        mn[q].append("m%s_%d" % (u_, a0))
                 kn = ["k" + C]
                 cuf = T.FAR[:, 24 + 16 * c:40 + 16 * c]
                 mm(K[:, 0:272], T.BH[:, cs], T.NI[:, 128:400], True, False, ["BH" + C, "NI1", "NI2"], kn, 128, 272, kb)
@@ -400,17 +420,13 @@ def build(T, topo, rank, core):
                     mm(K[:, 0:272:17], T.M0[:, cs], R1, False, False, ["M0" + C] + R1N, kn, 128, 16, kb)
                 elif h < 3:
                     mm(K[:, 0:272:17], T.IF[:], cuf, False, False, ["IF", "CUF" + C], kn, 128, 16, kb, 4)
-                sums = []
-                if nb < 128:
-                    sums += [(K[nb:128, 1 + i:272:17], T.G[:, go + 16 * nb + i:go + 2048:16], R1, gn(nb, 128) + R1N, 128 - nb, 16) for i in range(16)]
-                    sums += [(K[nb:128, 1 + i:272:17], T.M[:, go + 16 * nb + i:go + 2048:16], R2, mall[nb // 8:16] + R2N, 128 - nb, 16) for i in range(16)]
-                sums += [(K[0:nb, 1 + i:272:17], T.G[:, go + i:go + 16 * nb:16], R1, gn(0, nb) + R1N, nb, 16) for i in range(ne, 16)]
-                if nb > 0:
-                    sums += [(K[0:nb, 1 + i:272:17], mslot(i), R1, mname(i) + R1N, nb, 16) for i in range(ne)]
-                    sums += [(K[0:nb, 1 + i:272:17], mslot(i), R2, ["m%d%d%d_%d" % (t, h, c, i)] + R2N, nb, 16) for i in range(ne, 16)]
-                if ne < 16:
-                    sums.append((K[0:nb, 0:272], T.X[:, xo + 128 * c:xo + 128 * c + nb], RX[ne], [xn, "RX%d_0" % ne, "RX%d_136" % ne], nb, 272))
-                if 0 < nb < 128:
+                sums = [(K[:, 1 + i:272:17], T.G[:, go + i:go + 2048:16], R1, gn(0, 128) + R1N, 128, 16) for i in range(16)]
+                nm_ = n1 if n2 == 128 else 128
+                if nm_:
+                    sums += [(K[0:nm_, 1 + i:272:17], T.M[:, go + i:go + 16 * nm_:16], R2, mn[q] + R2N, nm_, 16) for q in range(4) for i in range(q, 16, 4)]
+                if n1:
+                    sums.append((K[0:n1, 0:272], T.X[:, xo + 128 * c:xo + 128 * c + n1], T.RX[:], [xn, "RX0", "RX136"], n1, 272))
+                if 0 < n1 < 128:
                     sums.append((K[:, 0:16], T.ZR[:], T.ON[:, 0:16], ["ZR", "ON"], 128, 16))
                 for k, (o, a, b, nm, m_, n_) in enumerate(sums):
                     mm(o, a, b, False, k == len(sums) - 1, nm, kn, m_, n_, kb)
@@ -418,14 +434,19 @@ def build(T, topo, rank, core):
                 scan(T.SC[:, 272 * c:272 * c + 272], T.D0[:, d0:d0 + 272], K[:, 0:272], 0.0, A.add, A.min, ["D0"] + kn, ["SC" + C], 272, [kb])
                 ends = T.SC[:, 272 * c + 16:272 * c + 272:17]
                 ts(T.FH[:, k16], ends, 63, None, A.bitwise_and, None, ["SC" + C], ["FH" + C], 16)
-                if h < 2:
+                if h < 2 and CUS:
+                    act(cuf, ends, ID, ["SC" + C], ["CUF" + C], 16)
+                elif h < 2:
                     cp(cuf, ends, ["SC" + C], ["CUF" + C], 16)
                 elif h == 2:
                     cp(T.CUR[:, c:48:3], ends, ["SC" + C], ["CUR" + C], 16)
                 tt(T.EX[:, cs], T.FH[:, k16].indirect(T.XL[:, 0:8]), T.MK24[:, 192:320], A.mult, ["FH" + C, "XLa", "MK0", "MK1"], ["EX" + C], 128, ga=True)
                 for j in range(16):
                     mm(K[:, 280:288], LG[j % 8], T.EX[:, 128 * c + 8 * j:128 * c + 8 * j + 8], j == 0, j == 15, ["LG", "EX" + C], ["kl" + C], 128, 8, kb)
-                ts(lo, K[:, 280:288], 4032.0, None, A.add, None, ["kl" + C], [lon], 8, pb=[kb])
+                if LHS:
+                    act(lo, K[:, 280:288], ID, ["kl" + C], [lon], 8, bias=4032.0, pb=[kb])
+                else:
+                    ts(lo, K[:, 280:288], 4032.0, None, A.add, None, ["kl" + C], [lon], 8, pb=[kb])
                 if h == 3 and c == 2:
                     ts(T.LI[:, 40:48], K[:, 280:288], 1.0 / 16, PC[:, 11:12], A.mult, A.add, ["kl" + C, "PC11"], ["LI12"], 8, pb=[kb])
         bias[0] = 0.0
@@ -484,11 +505,12 @@ def build(T, topo, rank, core):
             for gg in range(8):
                 j = 16 * c + 2 * gg + u
                 hf = T.HF[:, 3 * gg + c:3 * gg + c + 1] if u == 0 else T.HF[:, 24 + 8 * c + gg:25 + 8 * c + gg]
-                ts(T.BB[:, HB * j:HB * j + HB], T.I162[:], hf, cW[c], A.is_equal, A.mult, ["I162", "PCe", "HF0" if u == 0 else "HF1%d" % c], ["BB%d" % j], HB, .5)
+                hb = n0 // 16
+                ts(T.BB[:, HB * j:HB * j + hb], T.I162[:, 0:hb], hf, cW[c], A.is_equal, A.mult, ["I162", "PCe", "HF0" if u == 0 else "HF1%d" % c], ["BB%d" % j], hb, .5)
                 a, o = 32 * (gg // 2), HB * (gg % 2)
                 ao = S * u + 128 * c + a
-                mm(P[pk][a:a + 32, o:o + HB], T.AW[:, ao:ao + 32], T.BB[:, HB * j:HB * j + HB], False, False,
-                   ["AW%d%d" % (u, c), "BB%d" % j], ["p%d" % pk], 32, HB, pk)
+                mm(P[pk][a:a + 32, o:o + hb], T.AW[:, ao:ao + 32], T.BB[:, HB * j:HB * j + hb], False, False,
+                   ["AW%d%d" % (u, c), "BB%d" % j], ["p%d" % pk], 32, hb, pk)
 
         def places(u, c0, c1):
             a, b, nm = 24 * u + 8 * c0, 24 * u + 8 * c1, "%d%d" % (u, c0)
@@ -550,8 +572,19 @@ def build(T, topo, rank, core):
             U, pk = str(u), 4 + u
             o, on = P[pk][:, 0:S], ["p%d" % pk]
             if u == 0:
-                mm(o, I16, T.UV[:, bs[1]], True, True, ["I16", "UV1"], on, 128, S, pk)
-                tt(T.MT[:, bs[0]], o, T.A16[:], A.is_equal, on + A16N, ["MT0"], S, pb=[pk])
+                mm(o, I16, T.UV[:, bs[1]], True, not MTS[0], ["I16", "UV1"], on, 128, S, pk)
+                if MTS[0]:
+                    mm(o, N16, T.A16[:], False, True, ["I17"] + A16N, on, 128, S, pk)
+                    act(T.NW[:, bs[0]], o, F.Abs, on, ["NW0"], S, pb=[pk])
+                    act(T.MT[:, bs[0]], T.NW[:, bs[0]], F.Relu, ["NW0"], ["MT0"], S, bias=1.0, scale=-1.0)
+                else:
+                    tt(T.MT[:, bs[0]], o, T.A16[:], A.is_equal, on + A16N, ["MT0"], S, pb=[pk])
+            elif MTS[1]:
+                mm(o, T.IF[:], T.EB[:, bs[1]], True, False, ["IF", "EB1"], on, 128, S, pk, 4)
+                mm(o, N16, T.UV[:, bs[0]], False, False, ["I17", "UV0"], on, 128, S, pk)
+                mm(o, T.CC[:], T.AGB[:, bs[1]], False, True, ["CC1", "AG1"], on, 128, S, pk)
+                act(T.NW[:, bs[1]], o, F.Abs, on, ["NW1"], S, bias=129.0 * 4096 - MID, pb=[pk])
+                act(T.MT[:, bs[1]], T.NW[:, bs[1]], F.Relu, ["NW1"], ["MT1"], S, bias=1.0, scale=-1.0)
             else:
                 mm(o, T.CC[0:32, :], T.ON[0:32, :], True, False, ["CC0", "ON"], on, 128, S, pk)
                 mm(o, I16, T.UV[:, bs[0]], False, False, ["I16", "UV0"], on, 128, S, pk)
@@ -638,19 +671,28 @@ def build(T, topo, rank, core):
             mm(P[2][:, 300:306], T.SH[:, 160 + 15 - a:160 + 143 - a], T.C16[:, a:CN:16], a == 0, a == 15, ["SH1", "C16"], ["pt"], 128, 6, 2)
         ts(T.LSP[:, 0:6], P[2][:, 300:306], -1024.0, None, A.add, None, ["pt"], ["LSP"], 6, pb=[2])
         TB, TBN = (T.NF, ["NF%d" % k for k in range(5)]) if last else (T.NB, NBR + ["NBc"])
+        lsp = T.LSP[:, 0:6]
         for u in range(2):
-            cp(T.W[:].indirect(T.LD[:, 24 * u:24 * u + 24]), T.WI[:, bs[u]], ["LD", "WI%d" % u] + ([] if last else ["C16"]), WR + ["Wd"], S, sc=True)
+            for k in range(WP[u]):
+                a, b = 24 * u + 24 * k // WP[u], 24 * u + 24 * (k + 1) // WP[u]
+                cp(T.W[:].indirect(T.LD[:, a:b]), T.WI[:, 16 * a:16 * b], ["LD", "WI%d" % u] + (["C16"] if u and not last else []), WR + ["Wd"], 16 * (b - a), sc=True)
         if last:
-            dma("a", T.yw[:, 0:n0], T.W[:, 0:n0], WR, ["yw"], 5000)
+            dma("s", T.yw[:, 0:n0], T.W[:, 0:n0], WR, ["yw"], 5000)
+        else:
+            act(T.NB[:, n0:n0 + CN], T.NEW[:].indirect(lsp), ID, ["NEW", "NEWd", "LSP"], NBR, CN, ga=True)
         for u in range(2):
             U, pk = str(u), 4 + u
             o, on = P[pk][:, 0:S], ["p%d" % pk]
             mm(o, T.SJ[:, 128:256], T.SG[:, bs[u]], True, False, ["SJ1", "SG" + U], on, 128, S, pk)
             for b in range(16):
                 mm(P[pk][:, b:S:16], T.SEL[:, 128 * b:128 * b + 128], T.TGT[:, 24 * u:24 * u + 24], False, b == 15, ["SEL%d" % b, "TGT"], on, 128, 24, pk)
-            tt(T.NW[:, bs[u]], T.MS[:, bs[u]], o, A.max, on + ["MS" + U], ["NW" + U], S, pb=[pk])
-            cp(TB[:].indirect(T.LD[:, 24 * u:24 * u + 24]), T.NW[:, bs[u]], ["NW" + U, "LD"], TBN, S, sc=True)
-        lsp = T.LSP[:, 0:6]
+            if last:
+                act(T.NW[:, bs[u]], o, ID, on, ["NW" + U], S, pb=[pk])
+                op("v", lambda q, u=u: q.tensor_tensor(T.NF[:].indirect(T.LD[:, 24 * u:24 * u + 24]), T.MS[:, bs[u]], T.NW[:, bs[u]], A.max),
+                   ["MS" + U, "NW" + U, "LD"], TBN, 50 + S * SIG * CY)
+            else:
+                tt(T.NW[:, bs[u]], T.MS[:, bs[u]], o, A.max, on + ["MS" + U], ["NW" + U], S, pb=[pk])
+                cp(TB[:].indirect(T.LD[:, 24 * u:24 * u + 24]), T.NW[:, bs[u]], ["NW" + U, "LD"], TBN, S, sc=True)
         act(T.XS[:], T.X[:, xo:xo + 400].indirect(lsp), ID, XN_[t] + ["Xd%d" % t, "LSP"], ["XS"], CN, ga=True)
         act(T.WS[:], T.WB[:, 0:400].indirect(lsp), ID, ["WB0", "WBd", "LSP"], ["WS"], CN, ga=True)
         for k, (a, b, nm) in enumerate(((T.SJ[:, 256:384], T.ON[:, 0:CN], ["SJ2", "ON"]), (T.IB[:], T.XS[:], ["IB", "XS"]), (T.IB[:], T.WS[:], ["IB", "WS"]))):
@@ -663,10 +705,6 @@ def build(T, topo, rank, core):
             dma("a", T.yn[:, n0:PU], T.NFN[:], ["NFN"], ["yn2"], 2500)
             dma("a", T.yw[:, n0:PU], T.WN[:], ["WN"], ["yw2"], 2500)
         else:
-            if SI32:
-                act(T.NB[:, n0:n0 + CN], T.NEW[:].indirect(lsp), ID, ["NEW", "NEWd", "LSP"], NBR, CN, ga=True)
-            else:
-                cp(T.NB[:, n0:n0 + CN], T.NEW[:].indirect(lsp), ["NEW", "NEWd", "LSP"], NBR, CN, ga=True)
             act(T.W[:, n0:n0 + CN], T.NU[:], ID, ["NU"], WR, CN, bias=-RND)
     return ops
 
@@ -682,7 +720,7 @@ def plan(ops):
             succ[d].append((i, w))
     eng = [o["e"] for o in ops]
     cost = [o["c"] for o in ops]
-    busy = [o["c"] if o["k"] == "c" else 60.0 for o in ops]
+    busy = [o["c"] if o["k"] == "c" else o["c"] - 2000.0 if o["w"] in (["yw"], ["yn"]) else 60.0 for o in ops]
 
     def run(prio, before, behind):
         left = [len(x) for x in before]
@@ -701,7 +739,11 @@ def plan(ops):
                     if best is None or t0 < best[0]:
                         best = (t0, e)
             t0, e = best
-            i = max([j for j in ready[e] if rdy[j] <= t0 + LOOK], key=lambda j: prio[j])
+            i = max([j for j in ready[e] if rdy[j] <= t0 + LOOK], key=lambda j: prio[j] - PEN * max(0.0, rdy[j] - t0))
+            if rdy[i] > t0:
+                fit = [j for j in ready[e] if max(t0, rdy[j]) + busy[j] <= rdy[i] + FIT]
+                if fit:
+                    i = max(fit, key=lambda j: prio[j])
             t0 = max(t0, rdy[i])
             ready[e].remove(i)
             order.append(i)

import math
from concourse.bass import DstId, RemoteDMATransfer
from concourse.mybir import AluOpType as A, ActivationFunctionType as F

L, S, NT, CN, XN, N = 2304, 384, 3, 96, 112, 8
PU = L + NT * CN
GW = 2608
TW = GW + 2 * S
HB = 162
MID = 1344.0
LN2 = math.log(2.0)
RND = 12582912.0
bf, f32, i32, u16, f16 = "bfloat16", "float32", "int32", "uint16", "float16"
SCRATCH = {}
for _d, _s in (
        (bf, "W:3376 OH:2608 X:1200 XR:18432 BH:384 G:6144 M:6144 G0:384 M0:384 BH0:384 BB:7776 OT:768 AW:768 TS:672 TG:324 RR:768 RX:272 "
             "WB:800 AGB:768 WT:768 MT:768 SG:768 RB:384 WS:96 XS:96 WN:96 IB:128 NI:400 RC:48 ON:384 ZR:128 ZM:256 SI:640 "
             "SJ:640 I162:162 GS:2048 SGB:128 CC:128"),
        (f32, "NF:3376 IOT:2608 THB:128 THK:24 XE:384 HF:48 FAR:72 LSA:240 CP:864 EB:768 MS:768 NEW:400 NFN:96 "
              "NW:768 TA:128 NU:96 SND:224 LND:224 OWN:224 CI:256 CM:128 CD:128 PC:32 R32:24 SMM:128 "
              "SGM:128 IS:136 IF:128 D0:544 MK24:320 THR:48 DUM:48 DS:72 CT:64 TRI:128 K17:272"),
        (i32, "NB:3376 EN:72 THI:8 I32:384 SC:816 CUR:48 FH:72 HT:96 LI:48 MX:112 MY:224 PI:16 WI:768"),
        (u16, "LE:72 O16:384 LH:48 LUV:48 LT:48 LD:48 LP:24 LSP:8 XL:32 PL:16"),
        (f16, "A16:384 EX:384 EXP:192 C16:96 E16:112 I16:520 LG:240 SH:304 ID0:384 RA:16 D16:256 IO6:384 SEL:2048 SG6:128 TB:384 LF:72 TGT:48 CL:192 IS6:384 UV:768")):
    for _x in _s.split():
        SCRATCH[_x.split(":")[0]] = ("sbuf", [128, int(_x.split(":")[1])], _d)
for _k in range(8):
    SCRATCH["P%d" % _k] = ("psum", [128, 512], f32)
SEMAPHORES = ["sv", "sa", "sp", "st", "arr0", "arr1", "loc0", "loc1"] + ["d%d" % _k for _k in range(20)]

GAM, SIG, CY, PECY, VF, AF, TF = 1.56, 3.8, 0.83, 0.44, 5.0, 30.0, 5.0
RG = [(64, 96)] * 3
CUT = [(0, 32, 64)] * 3
AP_, EBS = 32, True
LATE = ["OT12", "TS1", "TS1"]
AWV = (2,)
SI32, MSS = True, (False, True)
WP, CUS = (3, 1), True
LHS, MTS = False, (False, False)
SPR = "vaav"
NOV = ()
STAG = [0.0, 0.0, 0.0]
BINIT, LOOK, ROUNDS, TRIES, SHAKES = 5000.0, 60.0, 3, 8, 300
PEN, FIT = 0.0, 20.0
WSAME, WOTHER = 200.0, 200.0
CACHE = {}
ID = F.Identity


def build(T, topo, rank, core):
    ops = []
    bias = [0.0]
    last_w, readers, bank = {}, {}, {}
    P = [T["P%d" % k] for k in range(8)]

    def op(eng, fn, r, w, cost, pb=(), kind="c", after=()):
        n = len(ops)
        deps = {}
        for x in r:
            deps[last_w[x]] = True
        for x in w:
            if x in last_w:
                deps.setdefault(last_w[x], False)
            for y in readers.get(x, ()):
                deps.setdefault(y, False)
        for b in pb:
            st = bank.setdefault(b, [None, [], []])
            if st[0] != eng:
                st[0], st[2], st[1] = eng, st[1], []
            for y in st[2]:
                deps.setdefault(y, False)
            if eng == "t" and st[1]:
                deps.setdefault(st[1][-1], False)
            st[1].append(n)
        for y in after:
            deps.setdefault(y, False)
        for x in r:
            readers.setdefault(x, []).append(n)
        for x in w:
            last_w[x] = n
            readers[x] = []
        deps.pop(n, None)
        ops.append({"w": w, "b": bias[0], "e": eng, "f": fn, "d": deps, "c": cost, "k": kind})
        return n

    def vc(n, c=1.0):
        return VF + max(64, n * c) * CY

    def ts(o, i, s1, s2, o0, o1, r, w, n, c=1.0, pb=(), ga=False):
        cost = 50 + n * GAM * CY if ga else vc(n, c)
        if o1 is None:
            return op("v", lambda q: q.tensor_scalar(o, i, s1, None, o0), r, w, cost, pb)
        return op("v", lambda q: q.tensor_scalar(o, i, s1, s2, o0, o1), r, w, cost, pb)

    def tt(o, a, b, o0, r, w, n, pb=(), ga=False):
        cost = 50 + n * GAM * CY if ga else vc(n, 1.0 if pb else 2.0)
        return op("v", lambda q: q.tensor_tensor(o, a, b, o0), r, w, cost, pb)

    def cp(o, i, r, w, n, c=1.0, pb=(), ga=False, sc=False):
        cost = 50 + n * (SIG if sc else GAM) * CY if (ga or sc) else vc(n, c)
        return op("v", lambda q: q.tensor_copy(o, i), r, w, cost, pb)

    def ms(o, v, w, n, c=1.0):
        return op("v", lambda q: q.memset(o, v), [], w, vc(n, c))

    def scan(o, d0, d1, ini, o0, o1, r, w, n, pb=()):
        return op("v", lambda q: q.tensor_tensor_scan(o, d0, d1, ini, o0, o1), r, w, vc(n), pb)

    def act(o, i, fn, r, w, n, bias=0.0, scale=1.0, pb=(), ga=False):
        cost = 65 + n * GAM * CY if ga else AF + n * CY
        return op("a", lambda q: q.activation(o, i, fn, bias=bias, scale=scale), r, w, cost, pb)

    def mm(o, l, rr, st, sp, r, w, m, n, pb, x=1):
        return op("t", lambda q: q.matmul(o, l, rr, st, sp), r, w, TF + x * max(min(64, m), n) * PECY, [pb])

    first = []

    def iota(o, pat, base, cm, w, n, fl=True):
        if fl:
            return op("g", lambda q: q.iota(o, pat, base, cm, allow_small_or_imprecise_dtypes=True), [], w, 130 + 2 * n * CY, after=first)
        return op("g", lambda q: q.iota(o, pat, base, cm), [], w, 130 + 2 * n * CY, after=first)

    def sel(o, i, pat, base, r, w, n):
        return op("g", lambda q: q.affine_select(o, i, pat, A.is_equal, 0.0, base, 0), r, w, 170 + 2 * n * CY, after=first)

    def dma(eng, o, i, r, w, ns):
        return op(eng, lambda q: q.dma_start(o, i), r, w, ns, kind="d")

    XN_ = [["X%d%d" % (t, c) for c in range(3)] for t in range(NT)]
    dma("s", T.X[:, 0:S], T.x[:, 0:S], [], XN_[0], 3000)
    dma("s", T.EN[:], T.ent[:], [], ["EN"], 6000)
    dma("s", T.NB[:, 0:L], T.nb[:], [], ["NBa"], 9000)
    dma("a", T.W[:, 0:L], T.w[:], [], ["Wa"], 10000)
    dma("s", T.THI[:, 0:1], T.th[:], ["Wa"], ["THI"], 2500)
    for t in (1, 2):
        dma("s", T.X[:, 400 * t:400 * t + S], T.x[:, S * t:S * t + S], ["Wa"], XN_[t], 2500)
    NBR, WR = ["NBa", "NBb"], ["Wa", "Wb", "Wc"]

    PC, CP_ = T.PC, ["CI", "PC"]
    iota(T.PI[:, 0:1], [[0, 1]], 0, 1, ["PI0", "g0"], 1, False)
    iota(T.CI[:], [[1, 256]], 0, 0, ["CI", "g0"], 256)
    iota(T.CM[:], [[0, 8], [1, 16]], 0, 0, ["CM", "g0"], 128)
    iota(T.CD[:], [[1, 8], [0, 16]], 0, 0, ["CD", "g0"], 128)
    iota(T.MK24[:, 0:192], [[0, 24], [1, 8]], 0, 0, ["MK24", "g0"], 192)
    for k, (a, b, c) in enumerate(((16, 1, -1), (1, 0, 0))):
        iota(T.K17[:, 136 * k:136 * k + 136], [[a, 8], [b, 17]], c, 0, ["K17%d" % k, "g0"], 136)
    iota(T.R32[:], [[1, 8], [0, 3]], 0, 0, ["R32", "g0"], 24)
    iota(T.NB[:, L:GW], [[0, GW - L]], 65535, 0, ["NBb", "g0"], GW - L, False)
    first.append(iota(T.IOT[:], [[1, GW]], 0, 0, ["IOT", "g0"], GW))
    ms(T.W[:, L:PU], 0.0, ["Wb"], 288, .5)
    ms(T.W[:, PU:GW], 8192.0, ["Wc"], 16, .5)
    iota(T.NB[:, GW:TW], [[0, 768]], 0, 0, ["NBc"], 768, False)
    iota(T.W[:, GW:TW], [[0, 768]], 0, 0, ["Wd"], 768)
    iota(T.NF[:, GW:TW], [[0, 768]], 0, 0, ["NF4"], 768)
    iota(T.CP[:], [[0, 864]], 0, 0, ["CPb"], 864)
    for t in range(NT):
        ms(T.X[:, 400 * t + S:400 * t + 400], 0.0, ["Xd%d" % t], 16)
    ms(T.NEW[:, S:400], 65535.0, ["NEWd"], 16)
    ms(T.WB[:, S:400], 0.0, ["WBd"], 16)
    ts(T.PI[:, 1:2], T.PI[:, 0:1], 15, None, A.bitwise_and, None, ["PI0"], ["PI1"], 1)
    ts(T.PI[:, 2:3], T.PI[:, 0:1], 4, None, A.arith_shift_right, None, ["PI0"], ["PI2"], 1)
    ts(T.PI[:, 3:4], T.PI[:, 0:1], 4, 1, A.arith_shift_right, A.bitwise_and, ["PI0"], ["PI3"], 1)
    ts(T.PI[:, 4:5], T.PI[:, 0:1], 3, 1, A.arith_shift_right, A.bitwise_and, ["PI0"], ["PI4"], 1)
    cp(PC[:, 0:5], T.PI[:, 0:5], ["PI0", "PI1", "PI2", "PI3", "PI4"], ["PC"], 5)
    cP, cA, cG, cO, cH = [PC[:, k:k + 1] for k in range(5)]
    ts(T.SMM[:], T.CM[:], cA, None, A.is_equal, None, ["CM", "PC"], ["SMM"], 128)
    ts(T.SGM[:], T.CD[:], cG, None, A.is_equal, None, ["CD", "PC"], ["SGM"], 128)
    ts(T.IB[:], T.CI[:, 0:128], cP, None, A.is_equal, None, CP_, ["IB"], 128)
    for o, v, nm in ((T.I16[:, 0:128], 1.0, "I16"), (T.NI[:, 0:128], -1.0, "NI0"), (T.IF[:], 1.0, "IF"),
                     (T.I16[:, 128:256], -1.0, "I17"), (T.I16[:, 256:384], 4096.0, "I18"),
                     (T.SI[:, 0:128], .75, "SI0"), (T.SI[:, 128:256], .25, "SI1"), (T.SI[:, 256:384], .875, "SI2"),
                     (T.SI[:, 384:512], .125, "SI3"), (T.SI[:, 512:640], -65536.0, "SI4"),
                     (T.SJ[:, 0:128], 4096.0, "SJ0"), (T.SJ[:, 128:256], MID, "SJ1"), (T.SJ[:, 256:384], -.375, "SJ2"),
                     (T.SJ[:, 384:512], -2.0 ** 21, "SJ3")):
        act(o, T.IB[:], ID, ["IB"], [nm], 128, scale=v)
    ts(T.SJ[:, 512:640], T.IB[:], 2.0 ** 60, 2.0 ** 61, A.mult, A.mult, ["IB"], ["SJ4"], 128, .5)
    I16, N16, B16 = T.I16[:, 0:128], T.I16[:, 128:256], T.I16[:, 256:384]
    for o, v in ((0, 4096.0), (8, 4096.0), (16, -8192.0), (24, -8192.0)):
        ts(T.RC[:, o:o + 8], T.CI[:, 0:8], cG, v, A.is_equal, A.mult, CP_, ["RC%d" % o], 8)
    R1, R2, R1N, R2N = T.RC[:, 0:16], T.RC[:, 16:32], ["RC0", "RC8"], ["RC16", "RC24"]
    ts(T.R32[:], T.R32[:], cG, 256.0, A.is_equal, A.mult, ["R32", "PC"], ["R32"], 24)
    ms(T.RA[:, 8:16], 0.0, ["RA1"], 8)
    ts(T.RA[:, 0:8], T.CI[:, 0:128:16], cP, None, A.is_equal, None, CP_, ["RA0"], 8)
    ts(T.RC[:, 32:40], T.CI[:, 0:128:16], cP, -1.0, A.is_equal, A.mult, CP_, ["RC32"], 8)
    ts(T.RC[:, 40:48], T.CI[:, 0:128:16], cP, -1.0 / 64, A.is_equal, A.mult, CP_, ["RC40"], 8)
    ms(T.D0[:], -64.0, ["D0"], 544)
    ms(T.D0[:, 0:544:17], 1.0e9, ["D0"], 32)
    ms(T.D0[:, 273:544:17], 1.0e9, ["D0"], 16)
    for o, v, nm in ((T.NI[:, 128:264], -1.0, "NI1"), (T.NI[:, 264:400], -1.0 / 64, "NI2"), (T.I16[:, 384:520], 1.0, "I19")):
        ts(o, T.K17[:, 0:136], cP, v, A.is_equal, A.mult, ["K170", "PC"], [nm], 136)
    ms(T.NI[:, 128:400:17], 0.0, ["NI1", "NI2"], 16)
    ms(T.I16[:, 384:520:17], 0.0, ["I19"], 8)
    ts(T.LG[:], T.CI[:, 0:240], -112.0, cA, A.add, A.is_equal, CP_, ["LG"], 240)
    ts(PC[:, 15:16], cA, 1000.0, cP, A.mult, A.add, ["PC"], ["PC15"], 1)
    ts(T.SH[:, 0:144], T.CI[:, 0:144], -15.0, PC[:, 15:16], A.add, A.is_equal, ["CI", "PC15"], ["SH"], 144)
    ts(T.SH[:, 160:304], T.CI[:, 0:144], 1000.0 - 14.0, PC[:, 15:16], A.add, A.is_equal, ["CI", "PC15"], ["SH1"], 144)
    LG = [T.LG[:, 112 - 16 * k:240 - 16 * k] for k in range(8)]
    SH = [T.SH[:, 15 - k:143 - k] for k in range(16)]
    act(T.SG6[:], T.SGM[:], ID, ["SGM"], ["SG6"], 128)
    act(T.SGB[:], T.SGM[:], ID, ["SGM"], ["SGB"], 128)
    for k in range(16):
        act(T.SEL[:, 128 * k:128 * k + 128], T.SGM[:], ID, ["SGM", "SMM"], ["SEL%d" % k], 128, scale=T.SMM[:, k:k + 1])
        sel(T.GS[:, 128 * k:128 * k + 128], T.SGB[:], [[0, 8], [1, 16]], -k, ["SGB"], ["GS%d" % k], 128)
    for o in (0, 136):
        ts(T.RX[:, o:o + 136], T.K17[:, 136:272], cG, 4096.0, A.is_equal, A.mult, ["K171", "PC"], ["RX%d" % o], 136)
    ms(T.RX[:, 0:272:17], 0.0, ["RX0", "RX136"], 16)
    XO, XB, XC = [0], [], []
    for c in range(3):
        n1, n2 = RG[c]
        XO.append(XO[-1] + 16 * (128 - n1))
        if c and XC[-1] + 4 * RG[c - 1][0] + 4 * n1 <= 512:
            XB.append(XB[-1])
            XC.append(XC[-1] + 4 * RG[c - 1][0])
        else:
            XB.append(XB[-1] + 1 if c else 4)
            XC.append(0)
        if n2 > n1:
            ms(T.M[:, 2048 * c + 16 * n1:2048 * c + 16 * n2], 0.0, ["Mz%d" % c], 16 * (n2 - n1), .5)
    XW = XO[3]
    DB = list(range(XB[2] + 1 if any(a for a, b in RG) else 4, 7))
    cp(T.OH[:, 0:128], T.SMM[:], ["SMM"], ["OH"], 128)
    for a in (128, 256, 512, 1024, 2048):
        b = min(a, GW - a)
        sel(T.OH[:, a:a + b], T.OH[:, 0:b], [[0, b]], 0, ["OH"], ["OH"], b)
    ts(T.MK24[:, 192:256], T.MK24[:, 0:64], cG, None, A.is_equal, None, ["MK24", "PC"], ["MK0"], 64)
    ts(T.MK24[:, 256:320], T.MK24[:, 0:64], cG, -64.0, A.is_equal, A.mult, ["MK24", "PC"], ["MK1"], 64)
    ts(T.MK24[:, 0:192], T.MK24[:, 0:192], cG, None, A.is_equal, None, ["MK24", "PC"], ["MK24"], 192)
    ts(T.CT[:, 0:12], T.CI[:, 0:24:2], cH, None, A.add, None, CP_, ["CT0"], 12)
    cp(T.XL[:, 0:12], T.CT[:, 0:12], ["CT0"], ["XLa"], 12)
    cp(T.XL[:, 12:20], T.CI[:, 0:8], ["CI"], ["XLb"], 8)
    ms(T.ON[:], 1.0, ["ON"], 384, .5)
    ms(T.ZR[:], 0.0, ["ZR"], 128)
    cp(T.I162[:], T.CI[:, 0:HB], ["CI"], ["I162"], HB)
    ts(T.TRI[:], T.CI[:, 0:128], cP, -1.0, A.is_le, A.mult, CP_, ["TRI"], 128)
    tt(T.TRI[:], T.TRI[:], T.SGM[:], A.mult, ["TRI", "SGM"], ["TRI"], 128)
    for k, v in enumerate((-2047.0, 4097.0)):
        ts(T.IS[:, 0:128], T.IB[:], v, None, A.mult, None, ["IB"], ["IS"], 128)
        tt(T.TB[:, 128 * k:128 * k + 128], T.IS[:, 0:128], T.TRI[:], A.add, ["IS", "TRI"], ["TB%d" % k], 128)
    cp(T.TB[:, 256:384], T.TRI[:], ["TRI"], ["TB2"], 128)
    ts(PC[:, 5:6], cA, 12.0, 4096.0, A.is_lt, A.mult, ["PC"], ["PC5"], 1)
    ts(PC[:, 6:7], cA, 12.0, None, A.is_ge, None, ["PC"], ["PC6"], 1)
    ts(PC[:, 17:18], cA, 2.0, (65535.0 - MID) / 4096, A.is_ge, A.mult, ["PC"], ["PC17"], 1)
    ts(PC[:, 7:8], PC[:, 17:18], PC[:, 5:6], MID, A.mult, A.add, ["PC17", "PC5"], ["PC7"], 1)
    ts(PC[:, 14:15], PC[:, 5:6], MID - 129.0 * 4096 - 2.0 ** 21, None, A.add, None, ["PC5"], ["PC14"], 1)
    ts(PC[:, 16:17], PC[:, 14:15], -1.0, 65535.0, A.mult, A.add, ["PC14"], ["PC16"], 1)
    ts(T.IS6[:, 0:128], T.IB[:], PC[:, 6:7], None, A.mult, None, ["IB", "PC6"], ["IS6"], 128, .5)
    for k in range(2):
        ts(PC[:, 29 + k:30 + k], cA, float(k), None, A.is_equal, None, ["PC"], ["PC%d" % (29 + k)], 1)
        ts(T.IS6[:, 128 + 128 * k:256 + 128 * k], T.IB[:], PC[:, 29 + k:30 + k], None, A.mult, None, ["IB", "PC%d" % (29 + k)], ["IS6%d" % k], 128, .5)
    if MTS[1]:
        act(T.CC[:], T.IB[:], ID, ["IB"], ["CC1"], 128, scale=-4096.0)
    else:
        ts(PC[:, 8:9], cP, 0.0, -129.0 * 4096, A.is_equal, A.mult, ["PC"], ["PC8"], 1)
        ts(PC[:, 13:14], cP, 1.0, MID, A.is_equal, A.mult, ["PC"], ["PC13"], 1)
        ts(T.CC[:], T.ZR[:], PC[:, 8:9], PC[:, 13:14], A.add, A.add, ["ZR", "PC13", "PC8"], ["CC0"], 128, .5)
    ts(PC[:, 18:19], cA, -LN2, LN2 * (11 - 108 - 1548), A.mult, A.add, ["PC"], ["PC18"], 1)
    ts(PC[:, 10:11], PC[:, 6:7], -400.0, PC[:, 18:19], A.mult, A.add, ["PC6", "PC18"], ["PC10"], 1)
    ts(PC[:, 19:20], cA, -LN2, LN2 * 107, A.mult, A.add, ["PC"], ["PC19"], 1)
    ts(PC[:, 20:21], PC[:, 6:7], -400.0, PC[:, 19:20], A.mult, A.add, ["PC6", "PC19"], ["PC20"], 1)
    lr = math.log(1.9)
    for c in range(3):
        ts(PC[:, 21 + c:22 + c], cP, -lr, 118 * LN2 - lr * 128 * (c % 2), A.mult, A.add, ["PC"], ["PC%d" % (21 + c)], 1)
    act(PC[:, 24:28], PC[:, 20:24], F.Exp, ["PC20", "PC21", "PC22", "PC23"], ["PCe"], 1300)
    cZ, cW = PC[:, 24:25], [PC[:, 25 + c:26 + c] for c in range(3)]
    ts(T.IS[:, 0:128], T.IB[:], 2.0, None, A.mult, None, ["IB"], ["IS"], 128)
    tt(T.ZM[:, 0:128], T.IS[:, 0:128], T.SGM[:], A.subtract, ["IS", "SGM"], ["ZM0"], 128)
    ts(PC[:, 9:10], cO, float(HB), -0.46875, A.mult, A.add, ["PC"], ["PC9"], 1)
    ts(PC[:, 11:12], PC[:, 9:10], 252.0, None, A.add, None, ["PC9"], ["PC11"], 1)
    ms(T.TS[:, 324:336], 0.0, ["TSd"], 8)
    ts(T.ZM[:, 128:256], T.ZM[:, 0:128], cZ, None, A.mult, None, ["ZM0", "PCe"], ["ZM1"], 128)
    ts(T.CT[:, 16:64], T.CI[:, 0:48], 16.0, cA, A.mult, A.add, CP_, ["CT1"], 48)
    ts(T.DUM[:], T.CT[:, 16:64], GW - MID, None, A.add, None, ["CT1"], ["DUM"], 48)
    for t in range(NT):
        ts(T.DS[:, 24 * t:24 * t + 24], T.CT[:, 16:40], L + CN * t - MID - 768, None, A.add, None, ["CT1"], ["DS%d" % t], 24)
    ts(T.THR[:, 24:40], T.CT[:, 16:32], -lr, 118 * LN2 + math.log(2.5), A.mult, A.add, ["CT1"], ["THRa"], 16)
    cp(T.THR[:, 40:48], T.THR[:, 24:32], ["THRa"], ["THRb"], 8)
    act(T.THR[:, 0:24], T.THR[:, 24:48], F.Exp, ["THRa", "THRb"], ["THR0"], 24)
    cp(T.THR[:, 24:48], T.THR[:, 0:24], ["THR0"], ["THRa", "THRb"], 24)
    ts(T.PI[:, 8:15], T.CT[:, 16:23], 1.0 / 7, -3.0 / 7, A.mult, A.add, ["CT1"], ["CTI"], 7)
    ts(T.CT[:, 8:15], T.PI[:, 8:15], -111.0 / 16, None, A.mult, None, ["CTI", "CT0"], ["CT0"], 7)
    tt(T.CT[:, 8:15], T.CT[:, 8:15], T.CT[:, 16:23], A.add, ["CT1", "CT0"], ["CT0"], 7)
    ts(T.PL[:, 0:7], T.CT[:, 8:15], 16.0, None, A.mult, None, ["CT0"], ["PLa"], 7)
    ts(PC[:, 12:13], cA, 7.0, None, A.mult, None, ["PC"], ["PC12"], 1)
    ts(T.PL[:, 8:15], T.CI[:, 0:7], PC[:, 12:13], None, A.add, None, ["CI", "PC12"], ["PLb"], 7)
    ts(PC[:, 31:32], PC[:, 29:30], 256.0 * MID, 2.0 ** 20, A.mult, A.add, ["PC29"], ["PC31"], 1)
    for k in range(2):
        ts(T.D16[:, 128 * k:128 * k + 128], T.IS6[:, 128 + 128 * k:256 + 128 * k], 256.0, None, A.mult, None, ["IS6%d" % k], ["D16%d" % k], 128, .5)
    sel(T.IO6[:], T.IOT[:, 0:S], [[0, S]], 0, ["IOT"], ["IO6"], S)
    cp(PC[:, 28:29], T.THI[:, 0:1], ["THI"], ["PC28"], 1)
    ts(T.THB[:], T.ON[:, 0:128], PC[:, 28:29], -3.09375, A.mult, A.add, ["ON", "PC28"], ["THB"], 128)
    mm(P[7][:, 0:24], T.THB[:], T.R32[:], True, True, ["THB", "R32"], ["p7"], 128, 24, 7, 4)
    cp(T.THK[:], P[7][:, 0:24], ["p7"], ["THK"], 24, pb=[7])
    early = [k for k, o in enumerate(ops) if o["e"] == "v" and not set(o["w"]) & {"PC28", "THB", "THK", "ZM1", "THRa"}]
    early += [k for k, o in enumerate(ops) if o["e"] == "a" and o["k"] == "c" and not set(o["w"]) & {"THR0"}]
    op("v", lambda q: q.tensor_copy(T.LE[:], T.EN[:]), ["EN"], ["LE%d%d" % (t, c) for t in range(NT) for c in range(3)], vc(72), after=early)
    def spread(t, c, eng):
        na = 128 - RG[c][0]
        lo, hi = 128 * c + 128 - na, 128 * c + 128
        for i in range(16 if na else 0):
            o, src = T.XR[:, XW * t + XO[c] + i:XW * t + XO[c] + 16 * na:16], T.X[:, 400 * t + lo:400 * t + hi]
            if eng == "v":
                cp(o, src, [XN_[t][c]], ["XR%d%d_%d" % (t, c, i)], na, .5)
            elif eng == "a":
                act(o, src, ID, [XN_[t][c]], ["XR%d%d_%d" % (t, c, i)], na)
            else:
                sel(o, src, [[0, na]], 0, [XN_[t][c]], ["XR%d%d_%d" % (t, c, i)], na)
    for t in range(NT):
        for c in range(3 if t == 0 else 2):
            spread(t, c, SPR[c] if t == 0 else "g")
    for t in (1, 2):
        o = XN * (t - 1)
        act(T.TA[:], T.IOT[:].indirect(T.LE[:, 24 * t + 16:24 * t + 24]), ID, ["IOT", "LE%d2" % t], ["TA0"], 128, scale=256.0, ga=True)
        tt(T.OWN[:, o:o + XN], T.TA[:, 16:128], T.X[:, 400 * t + 272:400 * t + S], A.add, ["TA0", "X%d2" % t], ["OWN%d" % t], XN)

    send = [None, None]
    turn = [0]
    for t in range(NT):
        last = t == NT - 1
        n0 = L + CN * t
        xo = 400 * t
        if t > 0:
            o = XN * (t - 1)
            op("x", None, [], ["LND%d" % t], 6000, kind="x%d" % (t - 1), after=[send[t - 1]])
            tt(T.MX[:], T.LND[:, o:o + XN].indirect(T.PL[:, 0:7]), T.OWN[:, o:o + XN], A.max, ["LND%d" % t, "PLa", "OWN%d" % t], ["MX"], XN, ga=True)
            ts(T.MY[:, XN:224], T.MX[:], 8, 4095, A.arith_shift_right, A.bitwise_and, ["MX"], ["MYe"], XN)
            ts(T.E16[:], T.MY[:, XN:224], -MID, None, A.add, None, ["MYe"], ["E16"], XN)
            ts(T.MY[:, 0:XN], T.MX[:], 255, None, A.bitwise_and, None, ["MX"], ["MYx"], XN)
            cp(T.X[:, xo + 272:xo + S], T.MY[:, 0:XN], ["MYx"], ["X%d2" % t], XN)
            for a in range(16):
                mm(P[3][:, 304:311], SH[a], T.E16[:, a:XN:16], a == 0, a == 15, ["SH", "E16"], ["k2e"], 128, 7, 3)
            ts(T.LE[:, 24 * t + 17:24 * t + 24], P[3][:, 304:311], MID, None, A.add, None, ["k2e"], ["LE%d2" % t], 7, pb=[3])
            spread(t, 2, SPR[3])
        if last:
            for k in range(4):
                sel(T.NF[:, 652 * k:652 * k + 652], T.NB[:, 652 * k:652 * k + 652], [[0, 652]], 0, NBR, ["NF%d" % k], 652)
        for c in range(3):
            C = str(c)
            cs = slice(128 * c, 128 * c + 128)
            K, kb = P[1 + c], 1 + c
            xc, xn = T.X[:, xo + 128 * c:xo + 128 * c + 128], XN_[t][c]
            le, ln = T.LE[:, 24 * t + 8 * c:24 * t + 8 * c + 8], "LE%d%d" % (t, c)
            bias[0] = BINIT
            n1 = RG[c][0]
            for j in range(4 if n1 else 0):
                mm(P[XB[c]][:, XC[c] + j:XC[c] + 4 * n1:4], T.IB[:], T.X[:, xo + 128 * c:xo + 128 * c + n1], True, True, ["IB", xn], ["xp" + C, "p%d" % XB[c]], 128, n1, XB[c])
            act(T.ID0[:, cs], T.IOT[:].indirect(le), ID, ["IOT", ln], ["ID0" + C], 128, bias=-MID, ga=True)
            act(T.BH0[:, cs], T.ID0[:, cs], ID, ["ID0" + C], ["BH0" + C], 128, bias=8224.5 + MID)
            act(T.G0[:, cs], T.W[:, 0:GW].indirect(le), ID, WR + [ln], ["G0" + C], 128, ga=True)
            mm(K[:, 384:512], T.IB[:], T.G0[:, cs], True, False, ["IB", "G0" + C], ["kd" + C], 128, 128, kb)
            mm(K[:, 384:512], T.NI[:, 0:128], xc, False, True, ["NI0", xn], ["kd" + C], 128, 128, kb)
            act(T.M0[:, cs], K[:, 384:512], F.Abs, ["kd" + C], ["M0" + C], 128, pb=[kb])
            bias[0] = 0.0
        for k, (a, b, nm) in enumerate(((T.IB[:], T.X[:, xo:xo + S], ["IB"] + XN_[t]), (T.D16[:, 0:128], T.ID0[:], ["D160", "ID00", "ID01", "ID02"]),
                                        (T.D16[:, 128:256], T.IO6[:], ["D161", "IO6"]))):
            mm(P[7][:, 0:S], a, b, k == 0, k == 2, nm, ["p7"], 128, S, 7)
        act(T.XE[:], P[7][:, 0:S], ID, ["p7", "PC31"], ["XE"], S, bias=PC[:, 31:32], pb=[7])
        for h in range(4):
            for c in range(3):
                bias[0] = STAG[c]
                cs = slice(128 * c, 128 * c + 128)
                k16 = slice(16 * c, 16 * c + 16)
                K, kb = P[1 + c], 1 + c
                C = str(c)
                xn = XN_[t][c]
                if h == 0:
                    li, ln = T.LE[:, 24 * t + 8 * c:24 * t + 8 * c + 8], "LE%d%d" % (t, c)
                elif h < 3:
                    li, ln = T.LH[:, 24 * (h - 1) + 8 * c:24 * (h - 1) + 8 * c + 8], "LH%d%d" % (h, c)
                else:
                    li, ln = T.LUV[:, 8 * c:8 * c + 8], "LU0" + C
                if h < 2:
                    lo, lon = T.LH[:, 24 * h + 8 * c:24 * h + 8 * c + 8], "LH%d%d" % (h + 1, c)
                else:
                    lo, lon = T.LUV[:, 24 * (h - 2) + 8 * c:24 * (h - 2) + 8 * c + 8], "LU%d%d" % (h - 2, c)
                ts(T.I32[:, cs], T.NB[:, 0:GW].indirect(li), 4095, None, A.bitwise_and, None, NBR + [ln], ["I32" + C], 128, ga=True)
                ts(T.O16[:, cs], T.I32[:, cs], float(PU), None, A.min, None, ["I32" + C], ["O16" + C], 128)
                ts(T.BH[:, cs], T.O16[:, cs], 8224.5, None, A.add, None, ["O16" + C], ["BH" + C], 128, .5)
                ts(T.A16[:, cs], T.O16[:, cs], -MID, None, A.add, None, ["O16" + C], ["A16" + C], 128, .5)
                go = 2048 * c
                n1, n2 = RG[c]
                if (h, c) in NOV:
                    n2 = 128
                u_ = "%d%d%d" % (t, h, c)
                gn = lambda a, b: ["G%s_%d" % (u_, k) for k in range(a // 16, b // 16)]
                mn = [["Mz" + C] if n2 > n1 else [] for q in range(4)]
                xr, xrn = XW * t + XO[c] - 16 * n1, ["XR%d%d_%d" % (t, c, i) for i in range(16)]
                cuts = [a for a in CUT[c] if a < n2] + [n2]
                for a0, a1 in zip(cuts, cuts[1:]):
                    act(T.G[:, go + 16 * a0:go + 16 * a1], T.W[:, 0:GW].indirect(T.O16[:, 128 * c + a0:128 * c + a1]), ID,
                        WR + ["O16" + C], gn(a0, a1), 16 * (a1 - a0), ga=True)
                    if a0 < n1:
                        b1 = min(a1, n1)
                        for q in range(4):
                            r_ = slice(go + 16 * a0 + q, go + 16 * b1, 4)
                            mn[q].append("m%s_%d_%d" % (u_, q, a0))
                            tt(T.M[:, r_], T.G[:, r_], P[XB[c]][:, XC[c] + 4 * a0:XC[c] + 4 * b1], A.min, gn(a0, b1) + ["xp" + C], mn[q][-1:], 4 * (b1 - a0), pb=[XB[c]])
                for a0 in range(n1, n2, 32):
                    a1 = min(n2, a0 + 32)
                    db = DB[turn[0] % len(DB)]
                    turn[0] += 1
                    r_, o = slice(go + 16 * a0, go + 16 * a1), P[db][:, 0:16 * (a1 - a0)]
                    mm(o, T.NI[:, 0:128], T.XR[:, xr + 16 * a0:xr + 16 * a1], True, False, ["NI0"] + xrn, ["p%d" % db], 128, 16 * (a1 - a0), db)
                    mm(o, T.IB[:], T.G[:, r_], False, True, ["IB"] + gn(a0, a1), ["p%d" % db], 128, 16 * (a1 - a0), db)
                    act(T.G[:, r_], o, F.Abs, ["p%d" % db], gn(a0, a1), 16 * (a1 - a0), pb=[db])
                for a0 in range(n2, 128, AP_):
                    a1 = min(128, a0 + AP_)
                    r_ = slice(go + 16 * a0, go + 16 * a1)
                    tt(T.G[:, r_], T.W[:, 0:GW].indirect(T.O16[:, 128 * c + a0:128 * c + a1]), T.XR[:, xr + 16 * a0:xr + 16 * a1], A.subtract,
                       WR + ["O16" + C] + xrn, gn(a0, a1), 16 * (a1 - a0), ga=True)
                    ts(T.M[:, r_], T.G[:, r_], 0.0, None, A.min, None, gn(a0, a1), ["m%s_%d" % (u_, a0)], 16 * (a1 - a0), .5)
                    for q in range(4):
                        mn[q].append("m%s_%d" % (u_, a0))
                kn = ["k" + C]
                cuf = T.FAR[:, 24 + 16 * c:40 + 16 * c]
                mm(K[:, 0:272], T.BH[:, cs], T.NI[:, 128:400], True, False, ["BH" + C, "NI1", "NI2"], kn, 128, 272, kb)
                mm(K[:, 0:136], T.A16[:, cs], T.I16[:, 384:520], False, False, ["A16" + C, "I19"], kn, 128, 136, kb)
                if h == 0:
                    mm(K[:, 0:272:17], T.BH0[:, cs], T.RC[:, 32:48], False, False, ["BH0" + C, "RC32", "RC40"], kn, 128, 16, kb)
                    mm(K[:, 0:272:17], T.ID0[:, cs], T.RA[:], False, False, ["ID0" + C, "RA0", "RA1"], kn, 128, 16, kb)
                    mm(K[:, 0:272:17], T.M0[:, cs], R1, False, False, ["M0" + C] + R1N, kn, 128, 16, kb)
                elif h < 3:
                    mm(K[:, 0:272:17], T.IF[:], cuf, False, False, ["IF", "CUF" + C], kn, 128, 16, kb, 4)
                sums = [(K[:, 1 + i:272:17], T.G[:, go + i:go + 2048:16], R1, gn(0, 128) + R1N, 128, 16) for i in range(16)]
                nm_ = n1 if n2 == 128 else 128
                if nm_:
                    sums += [(K[0:nm_, 1 + i:272:17], T.M[:, go + i:go + 16 * nm_:16], R2, mn[q] + R2N, nm_, 16) for q in range(4) for i in range(q, 16, 4)]
                if n1:
                    sums.append((K[0:n1, 0:272], T.X[:, xo + 128 * c:xo + 128 * c + n1], T.RX[:], [xn, "RX0", "RX136"], n1, 272))
                if 0 < n1 < 128:
                    sums.append((K[:, 0:16], T.ZR[:], T.ON[:, 0:16], ["ZR", "ON"], 128, 16))
                for k, (o, a, b, nm, m_, n_) in enumerate(sums):
                    mm(o, a, b, False, k == len(sums) - 1, nm, kn, m_, n_, kb)
                d0 = 272 * (h // 3)
                scan(T.SC[:, 272 * c:272 * c + 272], T.D0[:, d0:d0 + 272], K[:, 0:272], 0.0, A.add, A.min, ["D0"] + kn, ["SC" + C], 272, [kb])
                ends = T.SC[:, 272 * c + 16:272 * c + 272:17]
                ts(T.FH[:, k16], ends, 63, None, A.bitwise_and, None, ["SC" + C], ["FH" + C], 16)
                if h < 2 and CUS:
                    act(cuf, ends, ID, ["SC" + C], ["CUF" + C], 16)
                elif h < 2:
                    cp(cuf, ends, ["SC" + C], ["CUF" + C], 16)
                elif h == 2:
                    cp(T.CUR[:, c:48:3], ends, ["SC" + C], ["CUR" + C], 16)
                tt(T.EX[:, cs], T.FH[:, k16].indirect(T.XL[:, 0:8]), T.MK24[:, 192:320], A.mult, ["FH" + C, "XLa", "MK0", "MK1"], ["EX" + C], 128, ga=True)
                for j in range(16):
                    mm(K[:, 280:288], LG[j % 8], T.EX[:, 128 * c + 8 * j:128 * c + 8 * j + 8], j == 0, j == 15, ["LG", "EX" + C], ["kl" + C], 128, 8, kb)
                if LHS:
                    act(lo, K[:, 280:288], ID, ["kl" + C], [lon], 8, bias=4032.0, pb=[kb])
                else:
                    ts(lo, K[:, 280:288], 4032.0, None, A.add, None, ["kl" + C], [lon], 8, pb=[kb])
                if h == 3 and c == 2:
                    ts(T.LI[:, 40:48], K[:, 280:288], 1.0 / 16, PC[:, 11:12], A.mult, A.add, ["kl" + C, "PC11"], ["LI12"], 8, pb=[kb])
        bias[0] = 0.0
        LN = [["LU%d%d" % (u, c) for c in range(3)] for u in range(2)]
        CURN, A16N = ["CUR0", "CUR1", "CUR2"], ["A160", "A161", "A162"]
        lu = [T.LUV[:, 0:24], T.LUV[:, 24:48]]
        bs = [slice(0, S), slice(S, 2 * S)]
        xb = T.X[:, xo:xo + S]
        CL = T.CL
        nbad, farl, want, cs1, rest, cs2 = CL[:, 0:48], CL[:, 48:72], CL[:, 72:96], CL[:, 96:120], CL[:, 120:144], CL[:, 144:168]
        tt(T.FAR[:, 0:24], T.CUR[:, 0:24], T.THK[:], A.is_ge, CURN + ["THK"], ["FAR"], 24)
        tt(T.EXP[:], T.FAR[:, 0:24].indirect(T.XL[:, 0:12]), T.MK24[:, 0:192], A.mult, ["FAR", "XLa", "MK24"], ["EXP"], 192, ga=True)
        for gg in range(8):
            mm(P[7][:, 400:424], LG[gg], T.EXP[:, 24 * gg:24 * gg + 24], gg == 0, gg == 7, ["LG", "EXP"], ["p7f"], 128, 24, 7)
        cp(farl, P[7][:, 400:424], ["p7f"], ["farl"], 24, pb=[7])
        off = n0 - MID - 768
        kfo = T.LSA[:, 168:192]
        if not last:
            scan(cs2, T.ON[:, 0:24], farl, 0.0, A.mult, A.add, ["ON", "farl"], ["cs2"], 24)
            mm(P[7][:, 424:448], T.TB[:, 128:256], farl, True, False, ["TB1", "farl"], ["p7g"], 128, 24, 7)
            mm(P[7][:, 424:448], T.SG6[:], cs2, False, True, ["SG6", "cs2"], ["p7g"], 128, 24, 7)
            act(kfo, P[7][:, 424:448], ID, ["p7g"], ["kfo"], 24, bias=S + off - 4097 - 2048, pb=[7])

        def sides(u, pk):
            U = str(u)
            late = [LATE[0:1], LATE[1:2], LATE[2:3]] if u else [[], [], []]
            if EBS:
                act(T.EB[:, bs[u]], T.NB[:, 0:GW].indirect(lu[u]), ID, NBR + LN[u] + late[0], ["EB" + U], S, ga=True)
            else:
                cp(T.EB[:, bs[u]], T.NB[:, 0:GW].indirect(lu[u]), NBR + LN[u], ["EB" + U], S, ga=True)
            act(T.UV[:, bs[u]], T.IOT[:].indirect(lu[u]), ID, ["IOT"] + LN[u] + late[1], ["UV" + U], S, bias=-MID, ga=True)
            act(T.WB[:, 400 * u:400 * u + S], T.W[:, 0:GW].indirect(lu[u]), ID, WR + LN[u] + late[2], ["WB" + U], S, ga=True)
            act(T.AGB[:, bs[u]], T.EB[:, bs[u]], ID, ["EB" + U], ["AG" + U], S, bias=128.7, scale=1.0 / 4096)
            act(T.WT[:, bs[u]], T.AGB[:, bs[u]], F.Exp, ["AG" + U, "PC10"], ["WT" + U], S, bias=PC[:, 10:11], scale=12 * LN2)
            o, on = P[pk][:, 0:S], ["p%d" % pk]
            mm(o, T.SI[:, 256 * u:256 * u + 128], T.WB[:, 400 * u:400 * u + S], True, False, ["SI0", "SI2", "WB" + U], on, 128, S, pk)
            mm(o, T.SI[:, 256 * u + 128:256 * u + 256], xb, False, True, ["SI1", "SI3"] + XN_[t], on, 128, S, pk)
            if SI32:
                act(T.WI[:, bs[u]], o, ID, on, ["WI" + U], S, bias=-.375 - .0625 * u, pb=[pk])
            else:
                ts(T.WI[:, bs[u]], o, -.375 - .0625 * u, None, A.add, None, on, ["WI" + U], S, pb=[pk])

        def rows(u, c0, c1, pk, po):
            d = slice(S * u + 128 * c0, S * u + 128 * c1)
            nm = ["%d%d" % (u, c) for c in range(c0, c1)]
            act(T.OT[:, d], T.OH[:].indirect(T.LUV[:, 24 * u + 8 * c0:24 * u + 8 * c1]), ID, ["OH"] + LN[u][c0:c1], ["OT" + x for x in nm], 128 * (c1 - c0), ga=True)
            if pk is None:
                return
            for c in range(c0, c1):
                mm(P[pk][:, 128 * (c - c0):128 * (c - c0) + 128], T.OT[:, S * u + 128 * c:S * u + 128 * c + 128], T.IB[:], True, True,
                   ["OT%d%d" % (u, c), "IB"], [po], 128, 128, pk)
            act(T.AW[:, d], P[pk][:, 0:128 * (c1 - c0)], ID, [po], ["AW" + x for x in nm], 128 * (c1 - c0), pb=[pk])

        def weights(u, c):
            pk = 7 * (c // 2)
            for gg in range(8):
                j = 16 * c + 2 * gg + u
                hf = T.HF[:, 3 * gg + c:3 * gg + c + 1] if u == 0 else T.HF[:, 24 + 8 * c + gg:25 + 8 * c + gg]
                hb = n0 // 16
                ts(T.BB[:, HB * j:HB * j + hb], T.I162[:, 0:hb], hf, cW[c], A.is_equal, A.mult, ["I162", "PCe", "HF0" if u == 0 else "HF1%d" % c], ["BB%d" % j], hb, .5)
                a, o = 32 * (gg // 2), HB * (gg % 2)
                ao = S * u + 128 * c + a
                mm(P[pk][a:a + 32, o:o + hb], T.AW[:, ao:ao + 32], T.BB[:, HB * j:HB * j + hb], False, False,
                   ["AW%d%d" % (u, c), "BB%d" % j], ["p%d" % pk], 32, hb, pk)

        def places(u, c0, c1):
            a, b, nm = 24 * u + 8 * c0, 24 * u + 8 * c1, "%d%d" % (u, c0)
            if c0 < 2:
                ts(T.LI[:, a:b], T.LUV[:, a:b], 1.0 / 16, PC[:, 9:10], A.mult, A.add, LN[u][c0:c1] + ["PC9"], ["LI" + nm], 16)
            cp(T.LT[:, a:b], T.LI[:, a:b], ["LI" + nm], ["LT" + nm], 16)

        def reads(u, c0, c1, lt):
            a, b = 24 * u + 8 * c0, 24 * u + 8 * c1
            d = slice(S * u + 128 * c0, S * u + 128 * c1)
            win, wn = (T.TS[:, 0:336], ["TS0", "TSd"]) if c0 == 0 else (T.TS[:, 336:660], ["TS1"])
            tt(T.RR[:, d], win.indirect(T.LT[:, a:b]), T.OT[:, d], A.mult, wn + [lt] + ["OT%d%d" % (u, c) for c in range(c0, c1)],
               ["RR%d%d" % (u, c0)], 128 * (c1 - c0), ga=True)
        ts(T.LF[:, 0:24], lu[0], -MID, None, A.add, None, LN[0], ["LF0"], 24)
        ts(T.LF[:, 48:72], lu[0], -MID, None, A.add, None, LN[0], ["LF2"], 24)
        ts(T.HT[:, 0:24], T.CUR[:, 0:24], 63, 4, A.bitwise_and, A.arith_shift_right, CURN, ["HTa"], 24)
        ts(T.HT[:, 24:48], T.CUR[:, 24:48], 63, None, A.bitwise_and, None, CURN, ["HTb"], 24)
        ts(T.HT[:, 24:48], T.HT[:, 24:48], -4.0, 252.0, A.mult, A.add, ["HTb"], ["HTb"], 24)
        tt(T.HF[:, 0:24], T.HT[:, 0:24], T.HT[:, 24:48], A.add, ["HTa", "HTb"], ["HF0"], 24)
        rows(0, 0, 3, 7, "p7")
        sides(0, 7)
        act(T.RB[:], T.AGB[:, 0:S], F.Relu, ["AG0"], ["RB"], S, bias=-136.5 * 65536, scale=65536.0)
        places(0, 0, 3)
        for pk in (0, 7):
            mm(P[pk][:, 0:324], T.ZR[:], T.ON[:, 0:324], True, False, ["ZR", "ON"], ["p%d" % pk], 128, 324, pk)
        for c in range(3):
            weights(0, c)
        for c in range(3):
            C = str(c)
            ha, hc = slice(48 + 16 * c, 56 + 16 * c), slice(56 + 16 * c, 64 + 16 * c)
            ts(T.HT[:, ha], T.FH[:, 16 * c:16 * c + 8], 4, None, A.arith_shift_right, None, ["FH" + C], ["HTc" + C], 8)
            ts(T.HT[:, hc], T.FH[:, 16 * c + 8:16 * c + 16], -4.0, 252.0, A.mult, A.add, ["FH" + C], ["HTd" + C], 8)
            tt(T.HF[:, 24 + 8 * c:32 + 8 * c], T.HT[:, ha], T.HT[:, hc], A.add, ["HTc" + C, "HTd" + C], ["HF1" + C], 8)
            if c in AWV:
                rows(1, c, c + 1, None, None)
                ts(T.FH[:, 48 + 8 * c:56 + 8 * c], T.SC[:, 272 * c + 16:272 * c + 136:17], 15, None, A.bitwise_and, None, ["SC" + C], ["L16" + C], 8)
                tt(T.AW[:, S + 128 * c:S + 128 * c + 128], T.FH[:, 48 + 8 * c:56 + 8 * c].indirect(T.XL[:, 12:20]), T.CM[:], A.is_equal,
                   ["L16" + C, "XLb", "CM"], ["AW1" + C], 128, ga=True)
            else:
                rows(1, c, c + 1, 1 + c, "k" + C)
            if c == 2:
                mm(P[7][:, 0:324], T.SJ[:, 512:640], T.TG[:], False, False, ["SJ4", "TG"], ["p7"], 128, 324, 7)
            weights(1, c)
            if c > 0:
                pk = 7 * (c - 1)
                mm(P[pk][:, 0:16], T.ZR[:], T.ON[:, 0:16], False, True, ["ZR", "ON"], ["p%d" % pk], 128, 16, pk)
                act(T.TS[:, 336 * (c - 1):336 * (c - 1) + 324], P[pk][:, 0:324], ID, ["p%d" % pk], ["TS%d" % (c - 1)], 324, pb=[pk])
            if c == 1:
                act(T.TG[:], P[0][:, 0:324], F.Sign, ["p0"], ["TG"], 324, pb=[0])
                places(1, 0, 2)
                reads(0, 0, 2, "LT00")
                reads(1, 0, 2, "LT10")
        places(1, 2, 3)
        reads(0, 2, 3, "LT00")
        reads(1, 2, 3, "LT12")
        ts(T.LF[:, 24:48], lu[1], -MID, None, A.add, None, LN[1], ["LF1"], 24)
        sides(1, 6)
        for u in range(2):
            U, pk = str(u), 4 + u
            o, on = P[pk][:, 0:S], ["p%d" % pk]
            if u == 0:
                mm(o, I16, T.UV[:, bs[1]], True, not MTS[0], ["I16", "UV1"], on, 128, S, pk)
                if MTS[0]:
                    mm(o, N16, T.A16[:], False, True, ["I17"] + A16N, on, 128, S, pk)
                    act(T.NW[:, bs[0]], o, F.Abs, on, ["NW0"], S, pb=[pk])
                    act(T.MT[:, bs[0]], T.NW[:, bs[0]], F.Relu, ["NW0"], ["MT0"], S, bias=1.0, scale=-1.0)
                else:
                    tt(T.MT[:, bs[0]], o, T.A16[:], A.is_equal, on + A16N, ["MT0"], S, pb=[pk])
            elif MTS[1]:
                mm(o, T.IF[:], T.EB[:, bs[1]], True, False, ["IF", "EB1"], on, 128, S, pk, 4)
                mm(o, N16, T.UV[:, bs[0]], False, False, ["I17", "UV0"], on, 128, S, pk)
                mm(o, T.CC[:], T.AGB[:, bs[1]], False, True, ["CC1", "AG1"], on, 128, S, pk)
                act(T.NW[:, bs[1]], o, F.Abs, on, ["NW1"], S, bias=129.0 * 4096 - MID, pb=[pk])
                act(T.MT[:, bs[1]], T.NW[:, bs[1]], F.Relu, ["NW1"], ["MT1"], S, bias=1.0, scale=-1.0)
            else:
                mm(o, T.CC[0:32, :], T.ON[0:32, :], True, False, ["CC0", "ON"], on, 128, S, pk)
                mm(o, I16, T.UV[:, bs[0]], False, False, ["I16", "UV0"], on, 128, S, pk)
                mm(o, T.SJ[:, 0:128], T.AGB[:, bs[1]], False, True, ["SJ0", "AG1"], on, 128, S, pk)
                tt(T.MT[:, bs[1]], o, T.EB[:, bs[1]], A.is_equal, on + ["EB1"], ["MT1"], S, pb=[pk])
            mm(o, T.ZM[:, 0:128], T.WT[:, bs[u]], True, False, ["ZM0", "WT" + U], on, 128, S, pk)
            mm(o, T.ZM[:, 128:256], T.MT[:, bs[u]], False, True, ["ZM1", "MT" + U], on, 128, S, pk)
            act(T.SG[:, bs[u]], o, F.Sign, on, ["SG" + U], S, pb=[pk])
            if u == 0:
                mm(o, T.SJ[:, 384:512], T.SG[:, bs[0]], True, False, ["SJ3", "SG0"], on, 128, S, pk)
                mm(o, T.IB[:], T.RB[:], False, False, ["IB", "RB"], on, 128, S, pk)
                mm(o, T.SJ[:, 0:128], T.AGB[:, bs[0]], False, False, ["SJ0", "AG0"], on, 128, S, pk)
                mm(o, I16, T.A16[:], False, True, ["I16"] + A16N, on, 128, S, pk)
                if MSS[0]:
                    act(T.NW[:, bs[0]], o, F.Relu, on + ["PC16"], ["NW0"], S, bias=PC[:, 16:17], scale=-1.0, pb=[pk])
                    act(T.MS[:, bs[0]], T.NW[:, bs[0]], ID, ["NW0"], ["MS0"], S, bias=65535.0, scale=-1.0)
                else:
                    ts(T.MS[:, bs[0]], o, PC[:, 14:15], 65535.0, A.add, A.min, on + ["PC14"], ["MS0"], S, pb=[pk])
            elif MSS[1]:
                mm(o, T.SI[:, 512:640], T.SG[:, bs[1]], True, False, ["SI4", "SG1"], on, 128, S, pk)
                mm(o, T.IF[:], T.EB[:, bs[1]], False, True, ["IF", "EB1"], on, 128, S, pk, 4)
                act(T.MS[:, bs[1]], o, ID, on, ["MS1"], S, bias=-65536.0, pb=[pk])
            else:
                mm(o, T.SI[:, 512:640], T.SG[:, bs[1]], True, True, ["SI4", "SG1"], on, 128, S, pk)
                tt(T.MS[:, bs[1]], o, T.EB[:, bs[1]], A.min, on + ["EB1"], ["MS1"], S, pb=[pk])
        o = P[6][:, 0:S]
        mm(o, T.IS6[:, 0:128], T.A16[:], True, False, ["IS6"] + A16N, ["p6"], 128, S, 6)
        for u in range(2):
            mm(o, T.IS6[:, 128 + 128 * u:256 + 128 * u], T.UV[:, bs[u]], False, u == 1, ["IS6%d" % u, "UV%d" % u], ["p6"], 128, S, 6)
        act(T.NEW[:, 0:S], o, ID, ["p6", "PC7"], ["NEW"], S, bias=PC[:, 7:8], pb=[6])
        RP = P[0]
        for b in range(16):
            mm(RP[:, 0:48], T.GS[:, 128 * b:128 * b + 128], T.RR[:, b:768:16], b == 0, b == 15, ["GS%d" % b, "RR00", "RR10", "RR02", "RR12"], ["p0"], 128, 48, 0)
        tt(nbad, RP[:, 0:48], T.THR[:], A.is_gt, ["p0", "THR0", "THRa", "THRb"], ["nbad"], 48, pb=[0])
        mm(RP[:, 96:120], I16, farl, True, False, ["I16", "farl"], ["p0"], 128, 24, 0)
        mm(RP[:, 96:120], N16, CL[:, 0:24], False, False, ["I17", "nbad"], ["p0"], 128, 24, 0)
        mm(RP[:, 96:120], N16, CL[:, 24:48], False, True, ["I17", "nbad"], ["p0"], 128, 24, 0)
        LQ = P[3]
        mm(LQ[:, 400:448], I16, T.LF[:, 0:48], True, False, ["I16", "LF0", "LF1"], ["lq"], 128, 48, 3)
        mm(LQ[:, 400:448], B16, nbad, False, False, ["I18", "nbad"], ["lq"], 128, 48, 3)
        mm(LQ[:, 400:424], B16, CL[:, 24:48], False, False, ["I18", "nbad"], ["lq"], 128, 24, 3)
        mm(LQ[:, 424:448], B16, CL[:, 0:24], False, True, ["I18", "nbad"], ["lq"], 128, 24, 3)
        l = T.LSA
        l1, z, z2, m = l[:, 0:48], l[:, 48:96], l[:, 96:144], l[:, 144:168]
        ts(want, RP[:, 96:120], 1.0, None, A.is_ge, None, ["p0"], ["want"], 24, pb=[0])
        tt(l1, LQ[:, 400:448], T.DUM[:], A.min, ["lq", "DUM"], ["l1"], 48, pb=[3])
        ts(T.LD[:], l1, MID, None, A.add, None, ["l1"], ["LD"], 48)
        scan(cs1, T.ON[:, 0:24], want, -128.0, A.mult, A.add, ["ON", "want"], ["cs1"], 24)
        for o, k in ((128, 0), (152, 0), (176, 2))[0:2 if last else 3]:
            mm(RP[:, o:o + 24], T.TB[:, 128 * k:128 * k + 128], want, True, False, ["TB%d" % k, "want"], ["p0"], 128, 24, 0)
            mm(RP[:, o:o + 24], T.SG6[:], cs1, False, True, ["SG6", "cs1"], ["p0"], 128, 24, 0)
        ts(z, RP[:, 128:176], CN - 4095.0, n0 - MID + 4095.0, A.is_lt, A.mult, ["p0"], ["z"], 48, pb=[0])
        tt(z2, z, RP[:, 128:176], A.add, ["z", "p0"], ["z2"], 48, pb=[0])
        tt(T.TGT[:], z2, T.LF[:, 24:72], A.max, ["z2", "LF1", "LF2"], ["TGT"], 48)
        if not last:
            ka, kc = l[:, 192:216], l[:, 216:240]
            ts(ka, RP[:, 176:200], CN - 2048.0, -1.0, A.min, A.mult, ["p0"], ["ka"], 24, pb=[0])
            tt(ka, ka, kfo, A.add, ["ka", "kfo"], ["ka"], 24)
            tt(kc, ka, T.DS[:, 24 * t:24 * t + 24], A.max, ["ka", "DS%d" % t], ["kc"], 24)
            tt(m, kc, l[:, 96:120], A.max, ["kc", "z2"], ["m"], 24)
            iota(T.CP[:, S:S + XN], [[0, XN]], 0, 0, ["CPb"], XN)
        else:
            tt(m, T.DS[:, 24 * t:24 * t + 24], l[:, 96:120], A.max, ["DS%d" % t, "z2"], ["m"], 24)
        ts(T.LP[:], m, -off, None, A.add, None, ["m"], ["LP"], 24)
        iota(T.CP[:, 768:864], [[0, CN]], 2 ** 20 + 256 * S, 0, ["CPb"], CN)
        cp(T.CP[:].indirect(T.LP[:]), T.XE[:], ["XE", "LP"], ["CPb"], S, sc=True)
        if not last:
            so = XN * t
            act(T.SND[:, so:so + XN], T.CP[:, S:S + XN].indirect(T.PL[:, 8:15]), ID, ["CPb", "PLb"], ["SND%d" % t], XN, ga=True)

            def fire(q, t=t, so=so):
                tr = []
                for k in range(N - 1):
                    dst = T.cores[(rank + 1 + k) % N]
                    rid, pid = topo.addr(dst)[0:2]
                    en = topo.engines(core, dst)
                    tr.append(RemoteDMATransfer(dst_ids=[DstId(rid=rid, pnc=pid)], dma_engine_mask=1 << en[k % len(en)],
                                                remote_sem=T.sem["arr%d" % t], src=T.SND[:, so + 16 * k:so + 16 * k + 16],
                                                dst=T.LND[:, so + 16 * k:so + 16 * k + 16]))
                return q.remote_dma_fused(tr, local_sem=T.sem["loc%d" % t])
            send[t] = op("g", fire, ["SND%d" % t], [], 1000, kind="r")
        ts(T.C16[:], T.CP[:, 768:864], 1.0 / 256, 1024 - 4096 - .498, A.mult, A.add, ["CPb"], ["C16"], CN)
        for a in range(16):
            mm(P[2][:, 300:306], T.SH[:, 160 + 15 - a:160 + 143 - a], T.C16[:, a:CN:16], a == 0, a == 15, ["SH1", "C16"], ["pt"], 128, 6, 2)
        ts(T.LSP[:, 0:6], P[2][:, 300:306], -1024.0, None, A.add, None, ["pt"], ["LSP"], 6, pb=[2])
        TB, TBN = (T.NF, ["NF%d" % k for k in range(5)]) if last else (T.NB, NBR + ["NBc"])
        lsp = T.LSP[:, 0:6]
        for u in range(2):
            for k in range(WP[u]):
                a, b = 24 * u + 24 * k // WP[u], 24 * u + 24 * (k + 1) // WP[u]
                cp(T.W[:].indirect(T.LD[:, a:b]), T.WI[:, 16 * a:16 * b], ["LD", "WI%d" % u] + (["C16"] if u and not last else []), WR + ["Wd"], 16 * (b - a), sc=True)
        if last:
            dma("s", T.yw[:, 0:n0], T.W[:, 0:n0], WR, ["yw"], 5000)
        else:
            act(T.NB[:, n0:n0 + CN], T.NEW[:].indirect(lsp), ID, ["NEW", "NEWd", "LSP"], NBR, CN, ga=True)
        for u in range(2):
            U, pk = str(u), 4 + u
            o, on = P[pk][:, 0:S], ["p%d" % pk]
            mm(o, T.SJ[:, 128:256], T.SG[:, bs[u]], True, False, ["SJ1", "SG" + U], on, 128, S, pk)
            for b in range(16):
                mm(P[pk][:, b:S:16], T.SEL[:, 128 * b:128 * b + 128], T.TGT[:, 24 * u:24 * u + 24], False, b == 15, ["SEL%d" % b, "TGT"], on, 128, 24, pk)
            if last:
                act(T.NW[:, bs[u]], o, ID, on, ["NW" + U], S, pb=[pk])
                op("v", lambda q, u=u: q.tensor_tensor(T.NF[:].indirect(T.LD[:, 24 * u:24 * u + 24]), T.MS[:, bs[u]], T.NW[:, bs[u]], A.max),
                   ["MS" + U, "NW" + U, "LD"], TBN, 50 + S * SIG * CY)
            else:
                tt(T.NW[:, bs[u]], T.MS[:, bs[u]], o, A.max, on + ["MS" + U], ["NW" + U], S, pb=[pk])
                cp(TB[:].indirect(T.LD[:, 24 * u:24 * u + 24]), T.NW[:, bs[u]], ["NW" + U, "LD"], TBN, S, sc=True)
        act(T.XS[:], T.X[:, xo:xo + 400].indirect(lsp), ID, XN_[t] + ["Xd%d" % t, "LSP"], ["XS"], CN, ga=True)
        act(T.WS[:], T.WB[:, 0:400].indirect(lsp), ID, ["WB0", "WBd", "LSP"], ["WS"], CN, ga=True)
        for k, (a, b, nm) in enumerate(((T.SJ[:, 256:384], T.ON[:, 0:CN], ["SJ2", "ON"]), (T.IB[:], T.XS[:], ["IB", "XS"]), (T.IB[:], T.WS[:], ["IB", "WS"]))):
            mm(P[7][:, 128:224], a, b, k == 0, k == 2, nm, ["p7"], 128, CN, 7)
        act(T.NU[:], P[7][:, 128:224], ID, ["p7"], ["NU"], CN, bias=RND, scale=.5, pb=[7])
        if last:
            dma("s", T.yn[:, 0:n0], T.NF[:, 0:n0], TBN, ["yn"], 8000)
            act(T.NFN[:], T.NEW[:].indirect(lsp), ID, ["NEW", "NEWd", "LSP"], ["NFN"], CN, ga=True)
            act(T.WN[:], T.NU[:], ID, ["NU"], ["WN"], CN, bias=-RND)
            dma("a", T.yn[:, n0:PU], T.NFN[:], ["NFN"], ["yn2"], 2500)
            dma("a", T.yw[:, n0:PU], T.WN[:], ["WN"], ["yw2"], 2500)
        else:
            act(T.W[:, n0:n0 + CN], T.NU[:], ID, ["NU"], WR, CN, bias=-RND)
    return ops


def plan(ops):
    n = len(ops)
    pred = [[] for _ in range(n)]
    succ = [[] for _ in range(n)]
    for i, o in enumerate(ops):
        for d in o["d"]:
            w = (WSAME if o["d"][d] or o["e"] != "t" else 0) if ops[d]["e"] == o["e"] and ops[d]["k"] == "c" else WOTHER
            pred[i].append((d, w))
            succ[d].append((i, w))
    eng = [o["e"] for o in ops]
    cost = [o["c"] for o in ops]
    busy = [o["c"] if o["k"] == "c" else o["c"] - 2000.0 if o["w"] in (["yw"], ["yn"]) else 60.0 for o in ops]

    def run(prio, before, behind):
        left = [len(x) for x in before]
        rdy, fin = [0.0] * n, [0.0] * n
        free = {e: 0.0 for e in "vatgsx"}
        ready = {e: [] for e in "vatgsx"}
        for i in range(n):
            if not left[i]:
                ready[eng[i]].append(i)
        order = []
        while len(order) < n:
            best = None
            for e, lst in ready.items():
                if lst:
                    t0 = max(free[e], min([rdy[i] for i in lst]))
                    if best is None or t0 < best[0]:
                        best = (t0, e)
            t0, e = best
            i = max([j for j in ready[e] if rdy[j] <= t0 + LOOK], key=lambda j: prio[j] - PEN * max(0.0, rdy[j] - t0))
            if rdy[i] > t0:
                fit = [j for j in ready[e] if max(t0, rdy[j]) + busy[j] <= rdy[i] + FIT]
                if fit:
                    i = max(fit, key=lambda j: prio[j])
            t0 = max(t0, rdy[i])
            ready[e].remove(i)
            order.append(i)
            fin[i] = t0 + cost[i]
            free[e] = t0 + busy[i]
            for j, w in behind[i]:
                if fin[i] + w > rdy[j]:
                    rdy[j] = fin[i] + w
                left[j] -= 1
                if not left[j]:
                    ready[eng[j]].append(j)
        return order, fin
    base = [0.0] * n
    for i in range(n - 1, -1, -1):
        base[i] = cost[i] + max([base[j] + w for j, w in succ[i]] + [0.0])
    best = None
    for k in range(TRIES):
        prio = [base[i] + ops[i]["b"] * (k % 4 + 1) / 2.0 + (i * 2654435761 * (k // 4) % 1000) * 0.3 for i in range(n)]
        for _ in range(ROUNDS):
            order, fin = run(prio, pred, succ)
            if best is None or max(fin) < best[0]:
                best = (max(fin), order, fin)
            prio = run(fin, succ, pred)[1]
    for k in range(SHAKES):
        amp = (300.0, 800.0, 2000.0)[k % 3]
        prio = [f + amp * ((i // 8 * 2654435761 + k * 40503 * (i // 8 + 1)) % 1009) / 1009.0 for i, f in enumerate(best[2])]
        for _ in range(2):
            order, fin = run(run(prio, succ, pred)[1], pred, succ)
            if max(fin) < best[0]:
                best = (max(fin), order, fin)
            prio = fin
    CACHE["span"] = best[0]
    return best[1]


def rank_program(g, core, T, topo):
    rank = T.rank_of(core)
    if rank is None:
        return
    ops = build(T, topo, rank, core)
    if "order" not in CACHE:
        CACHE["order"] = plan(ops)
    order = CACHE["order"]
    q = {"v": g.vector, "a": g.scalar, "t": g.tensor, "g": g, "s": g.sync}
    esem = {"v": "sv", "a": "sa", "t": "st", "g": "sp"}
    at = {i: k for k, i in enumerate(order)}

    def needs(i, d):
        a, b = ops[d], ops[i]
        if a["k"] == "r" or b["k"][0] == "x":
            return False
        if a["e"] == b["e"] == "t":
            return b["d"][d]
        return True
    waits = []
    marked = set()
    for i in range(len(ops)):
        w = {}
        for d in ops[i]["d"]:
            if needs(i, d):
                key = ops[d]["e"] if ops[d]["k"] == "c" else d
                if key not in w or at[d] > at[w[key]]:
                    w[key] = d
        waits.append(list(w.values()))
    seen = {}
    for i in order:
        keep = []
        for d in waits[i]:
            key = (ops[i]["e"], ops[d]["e"] if ops[d]["k"] == "c" else d)
            if seen.get(key, -1) < at[d]:
                seen[key] = at[d]
                keep.append(d)
                marked.add(d)
        waits[i] = keep
    count = {e: 0 for e in esem}
    token = {}
    nd = 0
    for i in order:
        o = ops[i]
        if o["k"][0] == "x":
            token[i] = ("arr" + o["k"][1], N - 1)
            continue
        for d in waits[i]:
            q[o["e"]].wait_ge(T.sem[token[d][0]], token[d][1])
        ins = o["f"](q[o["e"]])
        if o["k"] == "d":
            token[i] = ("d%d" % nd, 16)
            ins.then_inc(T.sem["d%d" % nd], 16)
            nd += 1
        elif o["k"] == "c" and i in marked:
            count[o["e"]] += 1
            token[i] = (esem[o["e"]], count[o["e"]])
            ins.then_inc(T.sem[esem[o["e"]]], 1)
    for e in esem:
        if count[e]:
            g.wait_ge(T.sem[esem[e]], count[e])
    for k in range(nd):
        g.wait_ge(T.sem["d%d" % k], 16)
    for t in range(NT - 1):
        g.wait_ge(T.sem["loc%d" % t], N - 1)
        g.wait_ge(T.sem["arr%d" % t], N - 1)
